import numpy as np
import ml_dtypes


def mxq(x, axis, fmt="e4m3"):
    dtype, down = {"e4m3": (ml_dtypes.float8_e4m3fn, 7), "e5m2": (ml_dtypes.float8_e5m2, 14)}[fmt]
    v = np.moveaxis(np.asarray(x, np.float32).astype(ml_dtypes.bfloat16).astype(np.float64), axis, -1)
    blocks = v.reshape(v.shape[:-1] + (-1, 32))
    amax = np.abs(blocks).max(-1, keepdims=True)
    byte = np.maximum(np.where(amax > 0, np.frexp(amax)[1] - 1 + 127, 0) - down, 1)
    scale = np.exp2(byte - 127.0)
    codes = (blocks / scale).astype(np.float32).astype(dtype).astype(np.float64)
    return np.moveaxis((codes * scale).reshape(v.shape), -1, axis)


WIDE = False


def mx_kscale(k):
    if not WIDE:
        return np.ones(k)
    levels = np.array([24, -24, 12, -12, 0])
    if k % 512:
        return np.exp2(np.random.permutation(np.resize(levels, k // 32))).repeat(32)
    a = np.empty((k // 512, 16))
    for p in range(k // 512):
        a[p, :8] = np.random.permutation(np.resize(levels, 8))
        for g in range(8):
            far = levels[np.abs(levels - a[p, g]) >= 10]
            a[p, g + 8] = far[np.random.randint(len(far))]
    return np.exp2(a.ravel()).repeat(32)


def f64(x):
    return np.asarray(x).astype(np.float64)


def striped(idx):
    return np.tile(idx.reshape(-1, 16).T, (8, 1)).astype(np.uint16)


def unstriped(offs):
    return offs[:16].T.reshape(-1).astype(np.int64)


E2M1 = np.array([0.0, 0.5, 1.0, 1.5, 2.0, 3.0, 4.0, 6.0, -0.0, -0.5, -1.0, -1.5, -2.0, -3.0, -4.0, -6.0])


def pack_weight(w, fmt):
    k, n = w.shape
    w = f64(np.asarray(w, np.float32).astype(ml_dtypes.bfloat16)).reshape(k // 32, 32, n)
    amax = np.abs(w).max(1)
    if fmt == "e4m3":
        byte = np.frexp(amax)[1] - 1 + 127 - 7
    else:
        mant, ex = np.frexp(amax / 6.0)
        byte = np.where(mant > 0.5, ex, ex - 1) + 127
    byte = np.clip(np.where(amax > 0, byte, 1), 1, 254)
    scaled = (w * np.exp2(127.0 - byte)[:, None, :]).reshape(k, n).astype(np.float32)
    by_word = np.ascontiguousarray(scaled.reshape(k // 512, 128, 4, n).transpose(0, 1, 3, 2))
    if fmt == "e4m3":
        words = by_word.astype(ml_dtypes.float8_e4m3fn).view(np.uint8)
    else:
        c = by_word.astype(ml_dtypes.float4_e2m1fn).view(np.uint8) & 0xF
        words = (c[..., 0::2] | (c[..., 1::2] << 4)).reshape(k // 512, 128, 2 * n)
    return np.ascontiguousarray(words), np.ascontiguousarray(byte.astype(np.uint8).reshape(k // 512, 16, n))


def unpack_weight(words, scales, fmt):
    g, _, n = scales.shape
    words = np.ascontiguousarray(words).reshape(g, 128, n, -1)
    if fmt == "e4m3":
        vals = words.view(ml_dtypes.float8_e4m3fn).astype(np.float64)
    else:
        nib = np.empty((g, 128, n, 4), np.uint8)
        nib[..., 0::2] = words & 0xF
        nib[..., 1::2] = words >> 4
        vals = E2M1[nib]
    vals = vals * np.repeat(np.exp2(scales.astype(np.float64) - 127.0), 8, axis=1)[..., None]
    return vals.transpose(0, 1, 3, 2).reshape(g * 512, n)


def pack_table4(v):
    words, scales = pack_weight(v, "e2m1")
    g, t = words.shape[0] // 2, v.shape[1]
    return np.ascontiguousarray(words.reshape(g, 2, 128, t, 2).transpose(0, 2, 3, 1, 4).reshape(g, 128, t, 4)), scales


def unpack_table4(words, scales):
    g, _, t, _ = words.shape
    return unpack_weight(words.reshape(g, 128, t, 2, 2).transpose(0, 3, 1, 2, 4).reshape(2 * g, 128, 2 * t), scales, "e2m1")


def planes(y):
    n, m = y.shape
    v = y.astype(np.float32).astype(ml_dtypes.bfloat16).astype(np.float64).reshape(n // 32, 32, m)
    top = np.abs(v).max(1)
    byte = np.clip(np.where(top > 0, np.frexp(top)[1] - 1 + 127 - 7, 1), 1, 254)
    codes = (v * np.exp2(127.0 - byte)[:, None, :]).reshape(n, m).astype(np.float32).astype(ml_dtypes.float8_e4m3fn).view(np.uint8)
    words = codes.reshape(n // 512, 128, 4, m).transpose(0, 1, 3, 2)
    return np.ascontiguousarray(words), np.ascontiguousarray(byte.astype(np.uint8).reshape(n // 512, 16, m))


def sigm(f):
    return 1.0 / (1.0 + np.exp(-np.maximum(f, -700.0)))


K, N, T, J = 1024, 512, 2048, 1024


def setup_inputs():
    n = np.random.standard_normal
    s = mx_kscale(K)[:, None]
    p_tab = pack_table4(n((K, T)) * s)
    p_wb = pack_weight(n((K, N)) / np.sqrt(2 * K) / s, "e2m1")
    p_wc = pack_weight(n((K, N)) / np.sqrt(K) / s, "e2m1")
    return {
        "tab_words": p_tab[0],
        "tab_scales": p_tab[1],
        "wa": (n((K, N)) / np.sqrt(2 * K) / s).astype(np.float32),
        "wb_words": p_wb[0],
        "wb_scales": p_wb[1],
        "wc_words": p_wc[0],
        "wc_scales": p_wc[1],
        "wo": (n((K, N)) / np.sqrt(K) / s).astype(np.float32),
        "wgo": np.tile(np.random.uniform(0.5, 2.0, J), (128, 1)).astype(np.float32),
        "offs": striped(np.random.permutation(T)[:J]),
        "offs2": striped(np.random.permutation(T)[:J]),
    }


def reference(tab_words, tab_scales, wa, wb_words, wb_scales, wc_words, wc_scales, wo, wgo, offs, offs2):
    idx = unstriped(offs)
    idx2 = unstriped(offs2)
    tab_ = unpack_table4(tab_words, tab_scales)[:, idx]
    tabb_ = unpack_table4(tab_words, tab_scales)[:, idx2]
    wa_ = mxq(f64(wa), 0, "e4m3")
    wb_ = unpack_weight(wb_words, wb_scales, "e2m1")
    za = wa_.T @ tabb_ + wb_.T @ tab_
    eta = sigm(za)
    wc_ = unpack_weight(wc_words, wc_scales, "e2m1")
    ms = wc_.T @ tab_
    wo_ = mxq(f64(wo), 0, "e4m3")
    ow = wo_.T @ tabb_
    out = np.zeros((N, T))
    out[:, idx2] = f64(wgo)[0] * (np.maximum(ow + eta * ms, 0.0))
    return (out,) + planes(out)

@@ -1,0 +1,215 @@
+from contextlib import ExitStack
+
+import concourse.mybir as mybir
+
+K, N, T, J = 1024, 512, 2048, 1024
+FLOPS = 4 * 2 * K * N * J
+
+F32 = mybir.dt.float32
+BF16 = mybir.dt.bfloat16
+I32 = mybir.dt.int32
+U32 = mybir.dt.uint32
+U16 = mybir.dt.uint16
+U8 = mybir.dt.uint8
+FP8X4 = mybir.dt.float8_e4m3fn_x4
+FP4X4 = mybir.dt.float4_e2m1fn_x4
+ACT = mybir.ActivationFunctionType
+ALU = mybir.AluOpType
+
+P = 128
+PACK = 4
+PASSES = 2
+HALF = 512
+HALVES = J // HALF
+QUADS = 4
+CHUNK = 256
+CHUNKS = T // CHUNK
+SCALAR_CHUNKS = 1
+
+
+def tile_list_rgg_ownreluP_kernel(
+    tc, tab_words, tab_scales, wa, wb_words, wb_scales, wc_words, wc_scales, wo, wgo, offs, offs2, out_0, out_1, out_2
+):
+    nc = tc.nc
+    with ExitStack() as ctx:
+        keep = ctx.enter_context(tc.tile_pool(name="keep", bufs=1))
+        ring = ctx.enter_context(tc.tile_pool(name="ring", bufs=3))
+        psum = ctx.enter_context(tc.psum_pool(name="psum", bufs=2))
+
+        lists = [keep.tile([P, J // 16], U16, name="src_list"), keep.tile([P, J // 16], U16, name="dst_list")]
+        table = keep.tile([P, T], I32, name="table", align_bytes=64)
+        table_sc = keep.tile([P, T], U8, name="table_sc", align_bytes=64)
+        w4_raw = keep.tile([P, 2 * PASSES, 2 * N], U8, name="w4_raw", align_bytes=64)
+        w4 = keep.tile([P, 2 * PASSES, 2 * N], U8, name="w4", align_bytes=64)
+        w4_sc_raw = keep.tile([P, N], U8, name="w4_sc_raw", align_bytes=64)
+        w4_sc = [keep.tile([P, N], U8, name="w4_sc%d" % a, align_bytes=64) for a in range(2 * PASSES)]
+        picked_sc = [[keep.tile([P, J], U8, name="picked_sc%d_%d" % (l, a), align_bytes=64) for a in range(PASSES)] for l in range(2)]
+        gate = keep.tile([P, J], F32, name="gate")
+        pages = [keep.tile([P, T], F32, name="page%d" % i, align_bytes=64) for i in range(2)]
+
+        nc.vector.memset(table_sc[:].bitcast(I32), 0)
+        nc.gpsimd.memset(w4_sc_raw[:].bitcast(I32), 0)
+        for plane in w4_sc[1:] + [picked_sc[0][1], picked_sc[1][1]]:
+            nc.vector.memset(plane[:].bitcast(I32), 0)
+        for page in pages:
+            nc.vector.memset(page[:], 0.0)
+
+        nc.sync.dma_start(lists[0][:], offs)
+        nc.sync.dma_start(lists[1][:], offs2)
+        for q in range(QUADS):
+            nc.sync.dma_start(table_sc[32 * q : 32 * q + 8, :].bitcast(I32), tab_scales[:, 4 * q : 4 * q + 4, :].bitcast(I32))
+        nc.sync.dma_start(table[:], tab_words[0].rearrange("p t b -> p (t b)").bitcast(I32))
+        raws = []
+        for w, weight in enumerate((wa, wo)):
+            for a in range(PASSES):
+                raw = keep.tile([P, PACK, N], F32, name="raw%d_%d" % (w, a))
+                nc.sync.dma_start(raw[:], weight[512 * a : 512 * (a + 1), :].rearrange("(p j) n -> p j n", j=PACK))
+                raws.append(raw)
+                if len(raws) == 1:
+                    for v, words in enumerate((wb_words, wc_words)):
+                        nc.sync.dma_start(w4_raw[:, 2 * v : 2 * v + 2, :].bitcast(I32), words.rearrange("a p c -> p a c").bitcast(I32))
+        for w, scales in enumerate((wb_scales, wc_scales)):
+            for q in range(QUADS):
+                nc.gpsimd.dma_start(
+                    w4_sc_raw[32 * q + 8 * w : 32 * q + 8 * w + 8, :].bitcast(I32), scales[:, 4 * q : 4 * q + 4, :].bitcast(I32)
+                )
+        nc.sync.dma_start(gate[:], wgo)
+
+        for l in range(2):
+            nc.vector.tensor_copy(picked_sc[l][0][:], table_sc[:].indirect(lists[l][:]))
+            nc.scalar.dma_start(picked_sc[l][1][0:100, :].bitcast(I32), picked_sc[l][0][4:104, :].bitcast(I32))
+
+        nc.vector.tensor_copy(
+            w4[:].bitcast(U16).rearrange("p a (i m) -> p a i m", i=PACK),
+            w4_raw[:].bitcast(U16).rearrange("p a (m i) -> p a i m", i=PACK),
+        )
+        nc.vector.tensor_copy(
+            w4_sc[0][:].rearrange("p (i m) -> p m i", i=PACK), w4_sc_raw[:].rearrange("p (m i) -> p m i", i=PACK)
+        )
+        for a in range(1, 2 * PASSES):
+            nc.scalar.dma_start(w4_sc[a][0:100, :].bitcast(I32), w4_sc[0][4 * a : 4 * a + 100, :].bitcast(I32))
+
+        picked = {}
+
+        def pick_words(l, h):
+            pairs = keep.tile([P, HALF], U32, name="pairs%d_%d" % (l, h), tag="pairs%d_%d" % (l, h), align_bytes=64)
+            nc.vector.tensor_copy(pairs[:], table[:].bitcast(U32).indirect(lists[l][:, 32 * h : 32 * (h + 1)]))
+            parted = keep.tile([P, PASSES, 2 * HALF], U8, name="picked%d_%d" % (l, h), align_bytes=64)
+            nc.vector.tensor_copy(
+                parted[:].bitcast(U16), pairs[:].bitcast(U16).rearrange("p (s a) -> p a s", a=PASSES)
+            )
+            picked[(l, h)] = parted
+
+        w8 = []
+
+        def quantize_weight(raw, idx):
+            grouped = keep.tile([P, PACK * N], BF16, name="grouped%d" % idx, tag="grouped%d" % idx, align_bytes=64)
+            nc.scalar.copy(
+                grouped[:].rearrange("p (i m j) -> p m j i", i=PACK, j=PACK), raw[:].rearrange("p j (m i) -> p m j i", i=PACK)
+            )
+            codes = keep.tile([P, N], U32, name="codes%d" % idx, align_bytes=64)
+            scales = keep.tile([P, N], U8, name="scales%d" % idx, align_bytes=64)
+            nc.vector.quantize_mx(out=codes[:].bitcast(FP8X4), scales=scales[:], in_=grouped[:])
+            w8.append((codes, scales))
+
+        pick_words(0, 0)
+        pick_words(1, 0)
+        quantize_weight(raws[0], 0)
+        quantize_weight(raws[1], 1)
+        pick_words(0, 1)
+        quantize_weight(raws[2], 2)
+        quantize_weight(raws[3], 3)
+        pick_words(1, 1)
+        for i, tag in ((2, "pairs1_1"), (3, "grouped3")):
+            page = keep.tile([P, T], F32, name="page%d" % i, tag=tag, align_bytes=64)
+            nc.gpsimd.memset(page[:], 0.0)
+            pages.append(page)
+
+        def mm(acc, w, i, h, start, stop):
+            for a in range(PASSES):
+                cols = slice(P * i, P * (i + 1))
+                if w < 2:
+                    lhs = w4[:, 2 * w + a, 2 * P * i : 2 * P * (i + 1)].bitcast(FP4X4)
+                    lhs_sc = w4_sc[2 * w + a][:, cols]
+                else:
+                    codes, scales = w8[2 * (w - 2) + a]
+                    lhs = codes[:, cols].bitcast(FP8X4)
+                    lhs_sc = scales[:, cols]
+                l = w // 2
+                nc.tensor.matmul_mx(
+                    out=acc[:],
+                    lhsT=lhs,
+                    lhsT_scale=lhs_sc,
+                    rhs=picked[(l, h)][:, a, :].bitcast(FP4X4),
+                    rhs_scale=picked_sc[l][a][:, HALF * h : HALF * (h + 1)],
+                    start=start and a == 0,
+                    stop=stop and a == PASSES - 1,
+                )
+
+        units = [(i, h) for i in range(PACK) for h in range(HALVES)]
+        message, result = {}, {}
+        staged = keep.tile([P, 2, T, 2], BF16, name="staged", align_bytes=64)
+        out_rows = out_0.rearrange("(p i) t -> i p t", i=PACK)
+
+        def gated_message(k):
+            i, h = units[k]
+            za = psum.tile([P, HALF], F32, name="za")
+            mm(za, 0, i, h, True, False)
+            mm(za, 2, i, h, False, True)
+            ms = psum.tile([P, HALF], F32, name="ms")
+            mm(ms, 1, i, h, True, True)
+            eta = ring.tile([P, HALF], F32, name="eta")
+            nc.scalar.activation(eta[:], za[:], ACT.Sigmoid)
+            msg = ring.tile([P, HALF], F32, name="msg")
+            nc.vector.tensor_tensor(msg[:], ms[:], eta[:], ALU.mult)
+            message[k] = msg
+
+        def add_own(k):
+            i, h = units[k]
+            ow = psum.tile([P, HALF], F32, name="ow")
+            mm(ow, 3, i, h, True, True)
+            total = ring.tile([P, HALF], F32, name="total")
+            nc.vector.tensor_tensor(total[:], ow[:], message[k][:], ALU.add)
+            res = ring.tile([P, HALF], F32, name="res")
+            nc.scalar.activation(res[:], total[:], ACT.Relu)
+            result[k] = res
+
+        def place(k):
+            i, h = units[k]
+            nc.vector.tensor_tensor(
+                pages[i][:].indirect(lists[1][:, 32 * h : 32 * (h + 1)]), result[k][:], gate[:, HALF * h : HALF * (h + 1)], ALU.mult
+            )
+            if h == HALVES - 1:
+                nc.sync.dma_start(out_rows[i], pages[i][:])
+                width = HALF if i < PACK - 1 else CHUNK
+                for c in range(0, T, width):
+                    nc.scalar.copy(staged[:, i // 2, c : c + width, i % 2], pages[i][:, c : c + width])
+
+        gated_message(0)
+        for k in range(len(units)):
+            add_own(k)
+            if k + 1 < len(units):
+                gated_message(k + 1)
+            if k >= 1:
+                place(k - 1)
+        place(len(units) - 1)
+
+        y_sc = keep.tile([P, T], U8, name="y_sc", align_bytes=64)
+        words_out = out_1[0].rearrange("p t b -> p (t b)").bitcast(I32)
+        order = list(range(CHUNKS))
+        for c in order:
+            cols = slice(CHUNK * c, CHUNK * (c + 1))
+            woven = keep.tile([P, CHUNK * PACK], BF16, name="woven%d" % c, align_bytes=64)
+            dst = woven[:].bitcast(U32).rearrange("p (c e u) -> p c u e", e=4, u=2)
+            src = staged[:, :, cols, :].rearrange("p u c i -> p u (c i)").bitcast(U32).rearrange("p u (c e) -> p c u e", e=4)
+            if c >= CHUNKS - SCALAR_CHUNKS:
+                nc.scalar.copy(dst, src)
+            else:
+                nc.vector.tensor_copy(dst.bitcast(I32), src.bitcast(I32))
+            if c % 2 == 0:
+                y_codes = keep.tile([P, 2 * CHUNK], I32, name="y_codes%d" % c, align_bytes=64)
+            nc.vector.quantize_mx(out=y_codes[:, CHUNK * (c % 2) : CHUNK * (c % 2 + 1)].bitcast(FP8X4), scales=y_sc[:, cols], in_=woven[:])
+            if c % 2 == 1:
+                nc.sync.dma_start(words_out[:, CHUNK * (c - 1) : CHUNK * (c + 1)], y_codes[:])
+        for q in range(QUADS):
+            nc.sync.dma_start(out_2[0, 4 * q : 4 * q + 4, :].bitcast(I32), y_sc[32 * q : 32 * q + 4, :].bitcast(I32))

@@ -24,7 +24,7 @@ HALVES = J // HALF
 QUADS = 4
 CHUNK = 256
 CHUNKS = T // CHUNK
-SCALAR_CHUNKS = 1
+SCALAR_CHUNKS = 2
 
 
 def tile_list_rgg_ownreluP_kernel(
@@ -42,58 +42,70 @@ def tile_list_rgg_ownreluP_kernel(
         w4_raw = keep.tile([P, 2 * PASSES, 2 * N], U8, name="w4_raw", align_bytes=64)
         w4 = keep.tile([P, 2 * PASSES, 2 * N], U8, name="w4", align_bytes=64)
         w4_sc_raw = keep.tile([P, N], U8, name="w4_sc_raw", align_bytes=64)
-        w4_sc = [keep.tile([P, N], U8, name="w4_sc%d" % a, align_bytes=64) for a in range(2 * PASSES)]
-        picked_sc = [[keep.tile([P, J], U8, name="picked_sc%d_%d" % (l, a), align_bytes=64) for a in range(PASSES)] for l in range(2)]
-        gate = keep.tile([P, J], F32, name="gate")
-        pages = [keep.tile([P, T], F32, name="page%d" % i, align_bytes=64) for i in range(2)]
-
-        nc.vector.memset(table_sc[:].bitcast(I32), 0)
-        nc.gpsimd.memset(w4_sc_raw[:].bitcast(I32), 0)
-        for plane in w4_sc[1:] + [picked_sc[0][1], picked_sc[1][1]]:
-            nc.vector.memset(plane[:].bitcast(I32), 0)
-        for page in pages:
-            nc.vector.memset(page[:], 0.0)
+        w4_sc_dealt = keep.tile([P, N], U8, name="w4_sc_dealt", align_bytes=64)
+        w4_sc = keep.tile([P, 2 * PASSES, N], U8, name="w4_sc", align_bytes=64)
+        picked_rows = [keep.tile([P, J], U8, name="picked_rows%d" % l, align_bytes=64) for l in range(2)]
+        picked_sc = [keep.tile([P, PASSES, J], U8, name="picked_sc%d" % l, align_bytes=64) for l in range(2)]
+        pages = [keep.tile([P, T], F32, name="page0", align_bytes=64)]
 
         nc.sync.dma_start(lists[0][:], offs)
         nc.sync.dma_start(lists[1][:], offs2)
         for q in range(QUADS):
-            nc.sync.dma_start(table_sc[32 * q : 32 * q + 8, :].bitcast(I32), tab_scales[:, 4 * q : 4 * q + 4, :].bitcast(I32))
+            nc.sync.dma_start(table_sc[32 * q + 24 : 32 * q + 32, :].bitcast(I32), tab_scales[:, 4 * q : 4 * q + 4, :].bitcast(I32))
         nc.sync.dma_start(table[:], tab_words[0].rearrange("p t b -> p (t b)").bitcast(I32))
-        raws = []
-        for w, weight in enumerate((wa, wo)):
-            for a in range(PASSES):
-                raw = keep.tile([P, PACK, N], F32, name="raw%d_%d" % (w, a))
-                nc.sync.dma_start(raw[:], weight[512 * a : 512 * (a + 1), :].rearrange("(p j) n -> p j n", j=PACK))
-                raws.append(raw)
-                if len(raws) == 1:
-                    for v, words in enumerate((wb_words, wc_words)):
-                        nc.sync.dma_start(w4_raw[:, 2 * v : 2 * v + 2, :].bitcast(I32), words.rearrange("a p c -> p a c").bitcast(I32))
-        for w, scales in enumerate((wb_scales, wc_scales)):
-            for q in range(QUADS):
-                nc.gpsimd.dma_start(
-                    w4_sc_raw[32 * q + 8 * w : 32 * q + 8 * w + 8, :].bitcast(I32), scales[:, 4 * q : 4 * q + 4, :].bitcast(I32)
-                )
-        nc.sync.dma_start(gate[:], wgo)
+
+        def load_weight(weight, a, tag):
+            raw = keep.tile([P, PACK, N], F32, name=tag, tag=tag, align_bytes=64)
+            nc.sync.dma_start(raw[:], weight[512 * a : 512 * (a + 1), :].rearrange("(p j) n -> p j n", j=PACK))
+            return raw
+
+        def load_scale_rows(first, last):
+            for n in range(first, last):
+                w, q = divmod(n, QUADS)
+                row = 32 * q + 16 + 8 * w
+                scales = (wb_scales, wc_scales)[w]
+                nc.sync.dma_start(w4_sc_raw[row : row + 8, :].bitcast(I32), scales[:, 4 * q : 4 * q + 4, :].bitcast(I32))
+
+        raws = [load_weight(wa, 0, "raw0")]
+        load_scale_rows(0, 6)
+        raws.append(load_weight(wa, 1, "raw1"))
+        load_scale_rows(6, 8)
+        for v, words in enumerate((wb_words, wc_words)):
+            nc.sync.dma_start(w4_raw[:, 2 * v : 2 * v + 2, :].bitcast(I32), words.rearrange("a p c -> p a c").bitcast(I32))
+        raws.append(load_weight(wo, 0, "raw2"))
+        raws.append(load_weight(wo, 1, "raw3"))
+
+        for q in range(QUADS):
+            nc.gpsimd.memset(table_sc[32 * q : 32 * q + 24, :].bitcast(I32), 0)
+        for plane in picked_sc + [w4_sc]:
+            nc.gpsimd.memset(plane[:].bitcast(I32), 0)
+        for q in range(QUADS):
+            nc.gpsimd.memset(w4_sc_raw[32 * q : 32 * q + 16, :].bitcast(I32), 0)
+        nc.vector.memset(pages[0][:], 0.0)
 
         for l in range(2):
-            nc.vector.tensor_copy(picked_sc[l][0][:], table_sc[:].indirect(lists[l][:]))
-            nc.scalar.dma_start(picked_sc[l][1][0:100, :].bitcast(I32), picked_sc[l][0][4:104, :].bitcast(I32))
+            nc.vector.tensor_copy(picked_rows[l][:], table_sc[:].indirect(lists[l][:]))
+            for a in range(PASSES):
+                nc.gpsimd.dma_start(picked_sc[l][0:100, a, :].bitcast(I32), picked_rows[l][24 + 4 * a : 124 + 4 * a, :].bitcast(I32))
 
         nc.vector.tensor_copy(
             w4[:].bitcast(U16).rearrange("p a (i m) -> p a i m", i=PACK),
             w4_raw[:].bitcast(U16).rearrange("p a (m i) -> p a i m", i=PACK),
         )
         nc.vector.tensor_copy(
-            w4_sc[0][:].rearrange("p (i m) -> p m i", i=PACK), w4_sc_raw[:].rearrange("p (m i) -> p m i", i=PACK)
+            w4_sc_dealt[:].rearrange("p (i m) -> p m i", i=PACK), w4_sc_raw[:].rearrange("p (m i) -> p m i", i=PACK)
         )
-        for a in range(1, 2 * PASSES):
-            nc.scalar.dma_start(w4_sc[a][0:100, :].bitcast(I32), w4_sc[0][4 * a : 4 * a + 100, :].bitcast(I32))
+        for c in range(2 * PASSES):
+            nc.sync.dma_start(w4_sc[0:100, c, :].bitcast(I32), w4_sc_dealt[16 + 4 * c : 116 + 4 * c, :].bitcast(I32))
 
         picked = {}
 
-        def pick_words(l, h):
-            pairs = keep.tile([P, HALF], U32, name="pairs%d_%d" % (l, h), tag="pairs%d_%d" % (l, h), align_bytes=64)
+        def pick_words(l, h, tag):
+            pairs = keep.tile([P, HALF], U32, name="pairs%d_%d" % (l, h), tag=tag, align_bytes=64)
             nc.vector.tensor_copy(pairs[:], table[:].bitcast(U32).indirect(lists[l][:, 32 * h : 32 * (h + 1)]))
+            return pairs
+
+        def part_words(l, h, pairs):
             parted = keep.tile([P, PASSES, 2 * HALF], U8, name="picked%d_%d" % (l, h), align_bytes=64)
             nc.vector.tensor_copy(
                 parted[:].bitcast(U16), pairs[:].bitcast(U16).rearrange("p (s a) -> p a s", a=PASSES)
@@ -112,25 +124,31 @@ def tile_list_rgg_ownreluP_kernel(
             nc.vector.quantize_mx(out=codes[:].bitcast(FP8X4), scales=scales[:], in_=grouped[:])
             w8.append((codes, scales))
 
-        pick_words(0, 0)
-        pick_words(1, 0)
+        first = [pick_words(l, 0, "pairs%d" % l) for l in range(2)]
+        for l in range(2):
+            part_words(l, 0, first[l])
         quantize_weight(raws[0], 0)
         quantize_weight(raws[1], 1)
-        pick_words(0, 1)
+        gate = keep.tile([P, J], F32, name="gate", tag="raw1", align_bytes=64)
+        nc.sync.dma_start(gate[:], wgo)
+        part_words(0, 1, pick_words(0, 1, "grouped1"))
         quantize_weight(raws[2], 2)
         quantize_weight(raws[3], 3)
-        pick_words(1, 1)
-        for i, tag in ((2, "pairs1_1"), (3, "grouped3")):
-            page = keep.tile([P, T], F32, name="page%d" % i, tag=tag, align_bytes=64)
+        part_words(1, 1, pick_words(1, 1, "grouped3"))
+
+        def clear_page(tag):
+            page = keep.tile([P, T], F32, name="page%d" % len(pages), tag=tag, align_bytes=64)
             nc.gpsimd.memset(page[:], 0.0)
             pages.append(page)
+
+        clear_page("grouped3")
 
         def mm(acc, w, i, h, start, stop):
             for a in range(PASSES):
                 cols = slice(P * i, P * (i + 1))
                 if w < 2:
                     lhs = w4[:, 2 * w + a, 2 * P * i : 2 * P * (i + 1)].bitcast(FP4X4)
-                    lhs_sc = w4_sc[2 * w + a][:, cols]
+                    lhs_sc = w4_sc[:, 2 * w + a, cols]
                 else:
                     codes, scales = w8[2 * (w - 2) + a]
                     lhs = codes[:, cols].bitcast(FP8X4)
@@ -141,26 +159,26 @@ def tile_list_rgg_ownreluP_kernel(
                     lhsT=lhs,
                     lhsT_scale=lhs_sc,
                     rhs=picked[(l, h)][:, a, :].bitcast(FP4X4),
-                    rhs_scale=picked_sc[l][a][:, HALF * h : HALF * (h + 1)],
+                    rhs_scale=picked_sc[l][:, a, HALF * h : HALF * (h + 1)],
                     start=start and a == 0,
                     stop=stop and a == PASSES - 1,
                 )
 
         units = [(i, h) for i in range(PACK) for h in range(HALVES)]
         message, result = {}, {}
-        staged = keep.tile([P, 2, T, 2], BF16, name="staged", align_bytes=64)
+        staged = [keep.tile([P, 2, CHUNK, 2], BF16, name="staged%d" % c, align_bytes=64) for c in range(CHUNKS)]
         out_rows = out_0.rearrange("(p i) t -> i p t", i=PACK)
 
         def gated_message(k):
             i, h = units[k]
             za = psum.tile([P, HALF], F32, name="za")
-            mm(za, 0, i, h, True, False)
-            mm(za, 2, i, h, False, True)
+            mm(za, 2, i, h, True, False)
+            mm(za, 0, i, h, False, True)
             ms = psum.tile([P, HALF], F32, name="ms")
             mm(ms, 1, i, h, True, True)
             eta = ring.tile([P, HALF], F32, name="eta")
             nc.scalar.activation(eta[:], za[:], ACT.Sigmoid)
-            msg = ring.tile([P, HALF], F32, name="msg")
+            msg = keep.tile([P, HALF], F32, name="msg%d" % k, tag="msg%d" % k, align_bytes=64)
             nc.vector.tensor_tensor(msg[:], ms[:], eta[:], ALU.mult)
             message[k] = msg
 
@@ -173,6 +191,8 @@ def tile_list_rgg_ownreluP_kernel(
             res = ring.tile([P, HALF], F32, name="res")
             nc.scalar.activation(res[:], total[:], ACT.Relu)
             result[k] = res
+            if k < 2:
+                clear_page("msg%d" % k)
 
         def place(k):
             i, h = units[k]
@@ -181,9 +201,8 @@ def tile_list_rgg_ownreluP_kernel(
             )
             if h == HALVES - 1:
                 nc.sync.dma_start(out_rows[i], pages[i][:])
-                width = HALF if i < PACK - 1 else CHUNK
-                for c in range(0, T, width):
-                    nc.scalar.copy(staged[:, i // 2, c : c + width, i % 2], pages[i][:, c : c + width])
+                for c in range(CHUNKS):
+                    nc.scalar.copy(staged[c][:, i // 2, :, i % 2], pages[i][:, CHUNK * c : CHUNK * (c + 1)])
 
         gated_message(0)
         for k in range(len(units)):
@@ -196,20 +215,29 @@ def tile_list_rgg_ownreluP_kernel(
 
         y_sc = keep.tile([P, T], U8, name="y_sc", align_bytes=64)
         words_out = out_1[0].rearrange("p t b -> p (t b)").bitcast(I32)
-        order = list(range(CHUNKS))
-        for c in order:
-            cols = slice(CHUNK * c, CHUNK * (c + 1))
-            woven = keep.tile([P, CHUNK * PACK], BF16, name="woven%d" % c, align_bytes=64)
-            dst = woven[:].bitcast(U32).rearrange("p (c e u) -> p c u e", e=4, u=2)
-            src = staged[:, :, cols, :].rearrange("p u c i -> p u (c i)").bitcast(U32).rearrange("p u (c e) -> p c u e", e=4)
+        woven = [keep.tile([P, CHUNK * PACK], BF16, name="woven%d" % c, align_bytes=64) for c in range(CHUNKS)]
+        y_codes = [keep.tile([P, 2 * CHUNK], I32, name="y_codes%d" % c, align_bytes=64) for c in range(CHUNKS // 2)]
+
+        def weave(c):
+            dst = woven[c][:].bitcast(U32).rearrange("p (c e u) -> p c u e", e=4, u=2)
+            src = staged[c][:].rearrange("p u c i -> p u (c i)").bitcast(U32).rearrange("p u (c e) -> p c u e", e=4)
             if c >= CHUNKS - SCALAR_CHUNKS:
                 nc.scalar.copy(dst, src)
             else:
                 nc.vector.tensor_copy(dst.bitcast(I32), src.bitcast(I32))
-            if c % 2 == 0:
-                y_codes = keep.tile([P, 2 * CHUNK], I32, name="y_codes%d" % c, align_bytes=64)
-            nc.vector.quantize_mx(out=y_codes[:, CHUNK * (c % 2) : CHUNK * (c % 2 + 1)].bitcast(FP8X4), scales=y_sc[:, cols], in_=woven[:])
+
+        def quantize_chunk(c):
+            codes = y_codes[c // 2]
+            nc.vector.quantize_mx(
+                out=codes[:, CHUNK * (c % 2) : CHUNK * (c % 2 + 1)].bitcast(FP8X4), scales=y_sc[:, CHUNK * c : CHUNK * (c + 1)], in_=woven[c][:]
+            )
             if c % 2 == 1:
-                nc.sync.dma_start(words_out[:, CHUNK * (c - 1) : CHUNK * (c + 1)], y_codes[:])
+                nc.sync.dma_start(words_out[:, CHUNK * (c - 1) : CHUNK * (c + 1)], codes[:])
+
+        weave(0)
+        for c in range(CHUNKS):
+            if c + 1 < CHUNKS:
+                weave(c + 1)
+            quantize_chunk(c)
         for q in range(QUADS):
-            nc.sync.dma_start(out_2[0, 4 * q : 4 * q + 4, :].bitcast(I32), y_sc[32 * q : 32 * q + 4, :].bitcast(I32))
+            nc.scalar.dma_start(out_2[0, 4 * q : 4 * q + 4, :].bitcast(I32), y_sc[32 * q : 32 * q + 4, :].bitcast(I32))

@@ -52,7 +52,6 @@ def tile_list_rgg_ownreluP_kernel(
         nc.sync.dma_start(lists[1][:], offs2)
         for q in range(QUADS):
             nc.sync.dma_start(table_sc[32 * q + 24 : 32 * q + 32, :].bitcast(I32), tab_scales[:, 4 * q : 4 * q + 4, :].bitcast(I32))
-        nc.sync.dma_start(table[:], tab_words[0].rearrange("p t b -> p (t b)").bitcast(I32))
 
         def load_weight(weight, a, tag):
             raw = keep.tile([P, PACK, N], F32, name=tag, tag=tag, align_bytes=64)
@@ -67,6 +66,7 @@ def tile_list_rgg_ownreluP_kernel(
                 nc.sync.dma_start(w4_sc_raw[row : row + 8, :].bitcast(I32), scales[:, 4 * q : 4 * q + 4, :].bitcast(I32))
 
         raws = [load_weight(wa, 0, "raw0")]
+        nc.sync.dma_start(table[:], tab_words[0].rearrange("p t b -> p (t b)").bitcast(I32))
         load_scale_rows(0, 6)
         raws.append(load_weight(wa, 1, "raw1"))
         load_scale_rows(6, 8)
@@ -76,17 +76,17 @@ def tile_list_rgg_ownreluP_kernel(
         raws.append(load_weight(wo, 1, "raw3"))
 
         for q in range(QUADS):
-            nc.gpsimd.memset(table_sc[32 * q : 32 * q + 24, :].bitcast(I32), 0)
+            nc.vector.memset(table_sc[32 * q : 32 * q + 24, :].bitcast(I32), 0)
         for plane in picked_sc + [w4_sc]:
-            nc.gpsimd.memset(plane[:].bitcast(I32), 0)
+            nc.vector.memset(plane[:].bitcast(I32), 0)
         for q in range(QUADS):
-            nc.gpsimd.memset(w4_sc_raw[32 * q : 32 * q + 16, :].bitcast(I32), 0)
+            nc.vector.memset(w4_sc_raw[32 * q : 32 * q + 16, :].bitcast(I32), 0)
         nc.vector.memset(pages[0][:], 0.0)
 
         for l in range(2):
             nc.vector.tensor_copy(picked_rows[l][:], table_sc[:].indirect(lists[l][:]))
             for a in range(PASSES):
-                nc.gpsimd.dma_start(picked_sc[l][0:100, a, :].bitcast(I32), picked_rows[l][24 + 4 * a : 124 + 4 * a, :].bitcast(I32))
+                nc.sync.dma_start(picked_sc[l][0:100, a, :].bitcast(I32), picked_rows[l][24 + 4 * a : 124 + 4 * a, :].bitcast(I32))
 
         nc.vector.tensor_copy(
             w4[:].bitcast(U16).rearrange("p a (i m) -> p a i m", i=PACK),
@@ -131,8 +131,8 @@ def tile_list_rgg_ownreluP_kernel(
         quantize_weight(raws[1], 1)
         gate = keep.tile([P, J], F32, name="gate", tag="raw1", align_bytes=64)
         nc.sync.dma_start(gate[:], wgo)
-        part_words(0, 1, pick_words(0, 1, "grouped1"))
         quantize_weight(raws[2], 2)
+        part_words(0, 1, pick_words(0, 1, "grouped2"))
         quantize_weight(raws[3], 3)
         part_words(1, 1, pick_words(1, 1, "grouped3"))
 
@@ -141,7 +141,6 @@ def tile_list_rgg_ownreluP_kernel(
             nc.gpsimd.memset(page[:], 0.0)
             pages.append(page)
 
-        clear_page("grouped3")
 
         def mm(acc, w, i, h, start, stop):
             for a in range(PASSES):
@@ -164,21 +163,21 @@ def tile_list_rgg_ownreluP_kernel(
                     stop=stop and a == PASSES - 1,
                 )
 
-        units = [(i, h) for i in range(PACK) for h in range(HALVES)]
+        units = [(0, 0), (1, 0), (0, 1), (1, 1), (2, 0), (2, 1), (3, 0), (3, 1)]
         message, result = {}, {}
         staged = [keep.tile([P, 2, CHUNK, 2], BF16, name="staged%d" % c, align_bytes=64) for c in range(CHUNKS)]
         out_rows = out_0.rearrange("(p i) t -> i p t", i=PACK)
 
         def gated_message(k):
             i, h = units[k]
-            za = psum.tile([P, HALF], F32, name="za")
+            za = psum.tile([P, HALF], F32, name="za", bufs=3)
             mm(za, 2, i, h, True, False)
             mm(za, 0, i, h, False, True)
-            ms = psum.tile([P, HALF], F32, name="ms")
+            ms = psum.tile([P, HALF], F32, name="ms", bufs=3)
             mm(ms, 1, i, h, True, True)
             eta = ring.tile([P, HALF], F32, name="eta")
             nc.scalar.activation(eta[:], za[:], ACT.Sigmoid)
-            msg = keep.tile([P, HALF], F32, name="msg%d" % k, tag="msg%d" % k, align_bytes=64)
+            msg = keep.tile([P, HALF], F32, name="msg%d" % k, tag="msg%d" % k if k else "grouped3", align_bytes=64)
             nc.vector.tensor_tensor(msg[:], ms[:], eta[:], ALU.mult)
             message[k] = msg
 
@@ -191,8 +190,8 @@ def tile_list_rgg_ownreluP_kernel(
             res = ring.tile([P, HALF], F32, name="res")
             nc.scalar.activation(res[:], total[:], ACT.Relu)
             result[k] = res
-            if k < 2:
-                clear_page("msg%d" % k)
+            if k < PACK - 1:
+                clear_page("msg%d" % k if k else "grouped3")
 
         def place(k):
             i, h = units[k]

@@ -41,12 +41,12 @@ def tile_list_rgg_ownreluP_kernel(
         table_sc = keep.tile([P, T], U8, name="table_sc", align_bytes=64)
         w4_raw = keep.tile([P, 2 * PASSES, 2 * N], U8, name="w4_raw", align_bytes=64)
         w4 = keep.tile([P, 2 * PASSES, 2 * N], U8, name="w4", align_bytes=64)
-        w4_sc_raw = keep.tile([P, N], U8, name="w4_sc_raw", align_bytes=64)
-        w4_sc_dealt = keep.tile([P, N], U8, name="w4_sc_dealt", align_bytes=64)
-        w4_sc = keep.tile([P, 2 * PASSES, N], U8, name="w4_sc", align_bytes=64)
-        picked_rows = [keep.tile([P, J], U8, name="picked_rows%d" % l, align_bytes=64) for l in range(2)]
-        picked_sc = [keep.tile([P, PASSES, J], U8, name="picked_sc%d" % l, align_bytes=64) for l in range(2)]
-        pages = [keep.tile([P, T], F32, name="page0", align_bytes=64)]
+        w4_sc_raw = keep.tile([P, 2, N], U8, name="w4_sc_raw", align_bytes=64)
+        w4_sc_dealt = keep.tile([P, 2 * N], U8, name="w4_sc_dealt", align_bytes=64)
+        w4_sc = keep.tile([P, PASSES, 2 * N], U8, name="w4_sc", align_bytes=64)
+        picked_rows = keep.tile([P, 2 * J], U8, name="picked_rows", align_bytes=64)
+        picked_sc = keep.tile([P, PASSES, 2 * J], U8, name="picked_sc", align_bytes=64)
+        pages = [keep.tile([P, T], F32, name="page%d" % i, align_bytes=64) for i in range(2)]
 
         nc.sync.dma_start(lists[0][:], offs)
         nc.sync.dma_start(lists[1][:], offs2)
@@ -61,9 +61,9 @@ def tile_list_rgg_ownreluP_kernel(
         def load_scale_rows(first, last):
             for n in range(first, last):
                 w, q = divmod(n, QUADS)
-                row = 32 * q + 16 + 8 * w
+                row = 32 * q + 24
                 scales = (wb_scales, wc_scales)[w]
-                nc.sync.dma_start(w4_sc_raw[row : row + 8, :].bitcast(I32), scales[:, 4 * q : 4 * q + 4, :].bitcast(I32))
+                nc.sync.dma_start(w4_sc_raw[row : row + 8, w, :].bitcast(I32), scales[:, 4 * q : 4 * q + 4, :].bitcast(I32))
 
         raws = [load_weight(wa, 0, "raw0")]
         nc.sync.dma_start(table[:], tab_words[0].rearrange("p t b -> p (t b)").bitcast(I32))
@@ -77,26 +77,27 @@ def tile_list_rgg_ownreluP_kernel(
 
         for q in range(QUADS):
             nc.vector.memset(table_sc[32 * q : 32 * q + 24, :].bitcast(I32), 0)
-        for plane in picked_sc + [w4_sc]:
-            nc.vector.memset(plane[:].bitcast(I32), 0)
+        nc.vector.memset(picked_sc[:].bitcast(I32), 0)
+        nc.gpsimd.memset(w4_sc[:].bitcast(I32), 0)
         for q in range(QUADS):
-            nc.vector.memset(w4_sc_raw[32 * q : 32 * q + 16, :].bitcast(I32), 0)
-        nc.vector.memset(pages[0][:], 0.0)
+            nc.vector.memset(w4_sc_raw[32 * q : 32 * q + 24, :, :].bitcast(I32), 0)
+        for page in pages:
+            nc.vector.memset(page[:], 0.0)
 
         for l in range(2):
-            nc.vector.tensor_copy(picked_rows[l][:], table_sc[:].indirect(lists[l][:]))
-            for a in range(PASSES):
-                nc.sync.dma_start(picked_sc[l][0:100, a, :].bitcast(I32), picked_rows[l][24 + 4 * a : 124 + 4 * a, :].bitcast(I32))
+            nc.vector.tensor_copy(picked_rows[:, J * l : J * (l + 1)], table_sc[:].indirect(lists[l][:]))
+        for a in range(PASSES):
+            nc.sync.dma_start(picked_sc[0:100, a, :].bitcast(I32), picked_rows[24 + 4 * a : 124 + 4 * a, :].bitcast(I32))
 
         nc.vector.tensor_copy(
             w4[:].bitcast(U16).rearrange("p a (i m) -> p a i m", i=PACK),
             w4_raw[:].bitcast(U16).rearrange("p a (m i) -> p a i m", i=PACK),
         )
         nc.vector.tensor_copy(
-            w4_sc_dealt[:].rearrange("p (i m) -> p m i", i=PACK), w4_sc_raw[:].rearrange("p (m i) -> p m i", i=PACK)
+            w4_sc_dealt[:].rearrange("p (w i m) -> p w m i", w=2, i=PACK), w4_sc_raw[:].rearrange("p w (m i) -> p w m i", i=PACK)
         )
-        for c in range(2 * PASSES):
-            nc.sync.dma_start(w4_sc[0:100, c, :].bitcast(I32), w4_sc_dealt[16 + 4 * c : 116 + 4 * c, :].bitcast(I32))
+        for a in range(PASSES):
+            nc.sync.dma_start(w4_sc[0:100, a, :].bitcast(I32), w4_sc_dealt[24 + 4 * a : 124 + 4 * a, :].bitcast(I32))
 
         picked = {}
 
@@ -136,18 +137,12 @@ def tile_list_rgg_ownreluP_kernel(
         quantize_weight(raws[3], 3)
         part_words(1, 1, pick_words(1, 1, "grouped3"))
 
-        def clear_page(tag):
-            page = keep.tile([P, T], F32, name="page%d" % len(pages), tag=tag, align_bytes=64)
-            nc.gpsimd.memset(page[:], 0.0)
-            pages.append(page)
-
-
         def mm(acc, w, i, h, start, stop):
             for a in range(PASSES):
                 cols = slice(P * i, P * (i + 1))
                 if w < 2:
                     lhs = w4[:, 2 * w + a, 2 * P * i : 2 * P * (i + 1)].bitcast(FP4X4)
-                    lhs_sc = w4_sc[:, 2 * w + a, cols]
+                    lhs_sc = w4_sc[:, a, N * w + P * i : N * w + P * (i + 1)]
                 else:
                     codes, scales = w8[2 * (w - 2) + a]
                     lhs = codes[:, cols].bitcast(FP8X4)
@@ -158,7 +153,7 @@ def tile_list_rgg_ownreluP_kernel(
                     lhsT=lhs,
                     lhsT_scale=lhs_sc,
                     rhs=picked[(l, h)][:, a, :].bitcast(FP4X4),
-                    rhs_scale=picked_sc[l][:, a, HALF * h : HALF * (h + 1)],
+                    rhs_scale=picked_sc[:, a, J * l + HALF * h : J * l + HALF * (h + 1)],
                     start=start and a == 0,
                     stop=stop and a == PASSES - 1,
                 )
@@ -190,18 +185,16 @@ def tile_list_rgg_ownreluP_kernel(
             res = ring.tile([P, HALF], F32, name="res")
             nc.scalar.activation(res[:], total[:], ACT.Relu)
             result[k] = res
-            if k < PACK - 1:
-                clear_page("msg%d" % k if k else "grouped3")
 
         def place(k):
             i, h = units[k]
             nc.vector.tensor_tensor(
-                pages[i][:].indirect(lists[1][:, 32 * h : 32 * (h + 1)]), result[k][:], gate[:, HALF * h : HALF * (h + 1)], ALU.mult
+                pages[i % 2][:].indirect(lists[1][:, 32 * h : 32 * (h + 1)]), result[k][:], gate[:, HALF * h : HALF * (h + 1)], ALU.mult
             )
             if h == HALVES - 1:
-                nc.sync.dma_start(out_rows[i], pages[i][:])
+                nc.sync.dma_start(out_rows[i], pages[i % 2][:])
                 for c in range(CHUNKS):
-                    nc.scalar.copy(staged[c][:, i // 2, :, i % 2], pages[i][:, CHUNK * c : CHUNK * (c + 1)])
+                    nc.scalar.copy(staged[c][:, i // 2, :, i % 2], pages[i % 2][:, CHUNK * c : CHUNK * (c + 1)])
 
         gated_message(0)
         for k in range(len(units)):

@@ -1,6 +1,7 @@
 from contextlib import ExitStack
 
 import concourse.mybir as mybir
+from concourse.masks import make_identity
 
 K, N, T, J = 1024, 512, 2048, 1024
 FLOPS = 4 * 2 * K * N * J
@@ -20,8 +21,10 @@ P = 128
 PACK = 4
 PASSES = 2
 HALF = 512
-HALVES = J // HALF
 QUADS = 4
+PAIR = 256
+UNIT = 256
+UNITS = J // UNIT
 CHUNK = 256
 CHUNKS = T // CHUNK
 SCALAR_CHUNKS = 2
@@ -35,28 +38,31 @@ def tile_list_rgg_ownreluP_kernel(
         keep = ctx.enter_context(tc.tile_pool(name="keep", bufs=1))
         ring = ctx.enter_context(tc.tile_pool(name="ring", bufs=3))
         psum = ctx.enter_context(tc.psum_pool(name="psum", bufs=2))
+        placed = ctx.enter_context(tc.tile_pool(name="placed", bufs=1))
 
         lists = [keep.tile([P, J // 16], U16, name="src_list"), keep.tile([P, J // 16], U16, name="dst_list")]
-        table = keep.tile([P, T], I32, name="table", align_bytes=64)
+        table = keep.tile([P, T], I32, name="table", tag="table", align_bytes=64)
         table_sc = keep.tile([P, T], U8, name="table_sc", align_bytes=64)
         w4_raw = keep.tile([P, 2 * PASSES, 2 * N], U8, name="w4_raw", align_bytes=64)
         w4 = keep.tile([P, 2 * PASSES, 2 * N], U8, name="w4", align_bytes=64)
         w4_sc_raw = keep.tile([P, 2, N], U8, name="w4_sc_raw", align_bytes=64)
         w4_sc_dealt = keep.tile([P, 2 * N], U8, name="w4_sc_dealt", align_bytes=64)
         w4_sc = keep.tile([P, PASSES, 2 * N], U8, name="w4_sc", align_bytes=64)
-        picked_rows = keep.tile([P, 2 * J], U8, name="picked_rows", align_bytes=64)
+        picked_rows = keep.tile([P, 2 * J], U8, name="picked_rows", tag="picked_rows", align_bytes=64)
         picked_sc = keep.tile([P, PASSES, 2 * J], U8, name="picked_sc", align_bytes=64)
-        pages = [keep.tile([P, T], F32, name="page%d" % i, align_bytes=64) for i in range(2)]
+        ident = keep.tile([P, P], F32, name="ident", align_bytes=64)
 
         nc.sync.dma_start(lists[0][:], offs)
         nc.sync.dma_start(lists[1][:], offs2)
         for q in range(QUADS):
             nc.sync.dma_start(table_sc[32 * q + 24 : 32 * q + 32, :].bitcast(I32), tab_scales[:, 4 * q : 4 * q + 4, :].bitcast(I32))
 
-        def load_weight(weight, a, tag):
-            raw = keep.tile([P, PACK, N], F32, name=tag, tag=tag, align_bytes=64)
-            nc.sync.dma_start(raw[:], weight[512 * a : 512 * (a + 1), :].rearrange("(p j) n -> p j n", j=PACK))
-            return raw
+        raws = {}
+
+        def load_weight(w, a):
+            raw = keep.tile([P, PACK, N], F32, name="raw%d_%d" % (w, a), align_bytes=64)
+            nc.sync.dma_start(raw[:], (wa, wo)[w][512 * a : 512 * (a + 1), :].rearrange("(p j) n -> p j n", j=PACK))
+            raws[(w, a)] = raw
 
         def load_scale_rows(first, last):
             for n in range(first, last):
@@ -65,145 +71,195 @@ def tile_list_rgg_ownreluP_kernel(
                 scales = (wb_scales, wc_scales)[w]
                 nc.sync.dma_start(w4_sc_raw[row : row + 8, w, :].bitcast(I32), scales[:, 4 * q : 4 * q + 4, :].bitcast(I32))
 
-        raws = [load_weight(wa, 0, "raw0")]
+        load_weight(0, 0)
         nc.sync.dma_start(table[:], tab_words[0].rearrange("p t b -> p (t b)").bitcast(I32))
         load_scale_rows(0, 6)
-        raws.append(load_weight(wa, 1, "raw1"))
+        load_weight(1, 0)
+        load_weight(0, 1)
         load_scale_rows(6, 8)
         for v, words in enumerate((wb_words, wc_words)):
             nc.sync.dma_start(w4_raw[:, 2 * v : 2 * v + 2, :].bitcast(I32), words.rearrange("a p c -> p a c").bitcast(I32))
-        raws.append(load_weight(wo, 0, "raw2"))
-        raws.append(load_weight(wo, 1, "raw3"))
+        load_weight(1, 1)
 
         for q in range(QUADS):
             nc.vector.memset(table_sc[32 * q : 32 * q + 24, :].bitcast(I32), 0)
-        nc.vector.memset(picked_sc[:].bitcast(I32), 0)
-        nc.gpsimd.memset(w4_sc[:].bitcast(I32), 0)
         for q in range(QUADS):
             nc.vector.memset(w4_sc_raw[32 * q : 32 * q + 24, :, :].bitcast(I32), 0)
-        for page in pages:
-            nc.vector.memset(page[:], 0.0)
+        nc.gpsimd.memset(w4_sc[96:128].bitcast(I32), 0)
+        nc.gpsimd.memset(picked_sc[96:128].bitcast(I32), 0)
+        make_identity(nc, ident[:])
 
         for l in range(2):
             nc.vector.tensor_copy(picked_rows[:, J * l : J * (l + 1)], table_sc[:].indirect(lists[l][:]))
+        nc.vector.tensor_copy(
+            w4_sc_dealt[:].bitcast(U16).rearrange("p (w u m) -> p w u m", w=2, u=2),
+            w4_sc_raw[:].bitcast(U16).rearrange("p w (m u) -> p w u m", u=2),
+        )
         for a in range(PASSES):
             nc.sync.dma_start(picked_sc[0:100, a, :].bitcast(I32), picked_rows[24 + 4 * a : 124 + 4 * a, :].bitcast(I32))
-
-        nc.vector.tensor_copy(
-            w4[:].bitcast(U16).rearrange("p a (i m) -> p a i m", i=PACK),
-            w4_raw[:].bitcast(U16).rearrange("p a (m i) -> p a i m", i=PACK),
-        )
-        nc.vector.tensor_copy(
-            w4_sc_dealt[:].rearrange("p (w i m) -> p w m i", w=2, i=PACK), w4_sc_raw[:].rearrange("p w (m i) -> p w m i", i=PACK)
-        )
         for a in range(PASSES):
             nc.sync.dma_start(w4_sc[0:100, a, :].bitcast(I32), w4_sc_dealt[24 + 4 * a : 124 + 4 * a, :].bitcast(I32))
 
+        gate = keep.tile([P, J], F32, name="gate", tag="picked_rows", align_bytes=64)
+        nc.sync.dma_start(gate[:], wgo)
+
         picked = {}
 
-        def pick_words(l, h, tag):
-            pairs = keep.tile([P, HALF], U32, name="pairs%d_%d" % (l, h), tag=tag, align_bytes=64)
-            nc.vector.tensor_copy(pairs[:], table[:].bitcast(U32).indirect(lists[l][:, 32 * h : 32 * (h + 1)]))
+        def pick_words(h, tag):
+            pairs = keep.tile([P, 2, HALF], U32, name="pairs%d" % h, tag=tag, align_bytes=64)
+            for l in (1, 0):
+                nc.vector.tensor_copy(pairs[:, l, :], table[:].bitcast(U32).indirect(lists[l][:, 32 * h : 32 * (h + 1)]))
             return pairs
 
-        def part_words(l, h, pairs):
-            parted = keep.tile([P, PASSES, 2 * HALF], U8, name="picked%d_%d" % (l, h), align_bytes=64)
-            nc.vector.tensor_copy(
-                parted[:].bitcast(U16), pairs[:].bitcast(U16).rearrange("p (s a) -> p a s", a=PASSES)
-            )
-            picked[(l, h)] = parted
+        def part_words(h, pairs, tag):
+            parted = keep.tile([P, 2, PASSES, 2 * HALF], U8, name="picked%d" % h, tag=tag, align_bytes=64)
+            nc.vector.tensor_copy(parted[:].bitcast(U16), pairs[:].bitcast(U16).rearrange("p l (s a) -> p l a s", a=PASSES))
+            picked[h] = parted
 
-        w8 = []
+        w8 = {}
 
-        def quantize_weight(raw, idx):
-            grouped = keep.tile([P, PACK * N], BF16, name="grouped%d" % idx, tag="grouped%d" % idx, align_bytes=64)
-            nc.scalar.copy(
-                grouped[:].rearrange("p (i m j) -> p m j i", i=PACK, j=PACK), raw[:].rearrange("p j (m i) -> p m j i", i=PACK)
-            )
-            codes = keep.tile([P, N], U32, name="codes%d" % idx, align_bytes=64)
-            scales = keep.tile([P, N], U8, name="scales%d" % idx, align_bytes=64)
-            nc.vector.quantize_mx(out=codes[:].bitcast(FP8X4), scales=scales[:], in_=grouped[:])
-            w8.append((codes, scales))
-
-        first = [pick_words(l, 0, "pairs%d" % l) for l in range(2)]
-        for l in range(2):
-            part_words(l, 0, first[l])
-        quantize_weight(raws[0], 0)
-        quantize_weight(raws[1], 1)
-        gate = keep.tile([P, J], F32, name="gate", tag="raw1", align_bytes=64)
-        nc.sync.dma_start(gate[:], wgo)
-        quantize_weight(raws[2], 2)
-        part_words(0, 1, pick_words(0, 1, "grouped2"))
-        quantize_weight(raws[3], 3)
-        part_words(1, 1, pick_words(1, 1, "grouped3"))
-
-        def mm(acc, w, i, h, start, stop):
-            for a in range(PASSES):
-                cols = slice(P * i, P * (i + 1))
-                if w < 2:
-                    lhs = w4[:, 2 * w + a, 2 * P * i : 2 * P * (i + 1)].bitcast(FP4X4)
-                    lhs_sc = w4_sc[:, a, N * w + P * i : N * w + P * (i + 1)]
-                else:
-                    codes, scales = w8[2 * (w - 2) + a]
-                    lhs = codes[:, cols].bitcast(FP8X4)
-                    lhs_sc = scales[:, cols]
-                l = w // 2
-                nc.tensor.matmul_mx(
-                    out=acc[:],
-                    lhsT=lhs,
-                    lhsT_scale=lhs_sc,
-                    rhs=picked[(l, h)][:, a, :].bitcast(FP4X4),
-                    rhs_scale=picked_sc[:, a, J * l + HALF * h : J * l + HALF * (h + 1)],
-                    start=start and a == 0,
-                    stop=stop and a == PASSES - 1,
+        def round_weight(grouped, u, a):
+            for w in range(2):
+                nc.scalar.copy(
+                    grouped[:, w * PAIR * PACK : (w + 1) * PAIR * PACK].rearrange("p (m e j) -> p m j e", e=2, j=PACK),
+                    raws[(w, a)][:].rearrange("p j (m u e) -> p u m j e", u=2, e=2)[:, u],
                 )
 
-        units = [(0, 0), (1, 0), (0, 1), (1, 1), (2, 0), (2, 1), (3, 0), (3, 1)]
-        message, result = {}, {}
-        staged = [keep.tile([P, 2, CHUNK, 2], BF16, name="staged%d" % c, align_bytes=64) for c in range(CHUNKS)]
+        def quantize_weight(grouped, u, a):
+            codes = keep.tile([P, 2 * PAIR], U32, name="codes%d_%d" % (u, a), align_bytes=64)
+            scales = keep.tile([P, 2 * PAIR], U8, name="scales%d_%d" % (u, a), align_bytes=64)
+            nc.vector.quantize_mx(out=codes[:].bitcast(FP8X4), scales=scales[:], in_=grouped)
+            w8[(u, a)] = (codes, scales)
+
+        part_words(0, pick_words(0, "pairs0"), "picked0")
+        nc.vector.tensor_copy(
+            w4[:].bitcast(I32).rearrange("p v (u m) -> p v u m", u=2),
+            w4_raw[:].bitcast(I32).rearrange("p v (m u) -> p v u m", u=2),
+        )
+        pages = [keep.tile([P, T], F32, name="page%d" % i, align_bytes=64) for i in range(2)]
+        for page in pages:
+            nc.vector.memset(page[:], 0.0)
+        for a in range(PASSES):
+            grouped = keep.tile([P, 2 * PAIR * PACK], BF16, name="grouped%d" % a, tag="grouped%d" % a, align_bytes=64)
+            round_weight(grouped[:], 0, a)
+            quantize_weight(grouped[:], 0, a)
+        late_pairs = pick_words(1, "grouped1")
+        for a in range(PASSES):
+            grouped = keep.tile([P, 2 * PAIR * PACK], BF16, name="late%d" % a, align_bytes=64)
+            round_weight(grouped[:], 1, a)
+            quantize_weight(grouped[:], 1, a)
+        pages.append(keep.tile([P, T], F32, name="page2", tag="table", align_bytes=64))
+        nc.vector.memset(pages[2][:], 0.0)
+        pages.append(pages[0])
+
+        def mm(out, l, block, a, rhs, rhs_scale, start, stop):
+            h, b = divmod(block, 4)
+            nc.tensor.matmul_mx(
+                out=out,
+                lhsT=picked[h][:, l, a, 2 * P * b : 2 * P * (b + 1)].bitcast(FP4X4),
+                lhsT_scale=picked_sc[:, a, J * l + P * block : J * l + P * (block + 1)],
+                rhs=rhs,
+                rhs_scale=rhs_scale,
+                start=start,
+                stop=stop,
+            )
+
+        def mm4(out, w, u, block, a, start, stop):
+            mm(
+                out, 0, block, a,
+                w4[:, 2 * w + a, 2 * PAIR * u : 2 * PAIR * (u + 1)].bitcast(FP4X4),
+                w4_sc[:, a, N * w + PAIR * u : N * w + PAIR * (u + 1)],
+                start, stop,
+            )
+
+        def mm8(out, u, block, a, start, stop):
+            codes, scales = w8[(u, a)]
+            mm(out, 1, block, a, codes[:].bitcast(FP8X4), scales[:], start, stop)
+
+        summands = {}
+        results = [keep.tile([P, 2, J], F32, name="result%d" % u, align_bytes=64) for u in range(2)]
+        staged = []
         out_rows = out_0.rearrange("(p i) t -> i p t", i=PACK)
 
-        def gated_message(k):
-            i, h = units[k]
-            za = psum.tile([P, HALF], F32, name="za", bufs=3)
-            mm(za, 2, i, h, True, False)
-            mm(za, 0, i, h, False, True)
-            ms = psum.tile([P, HALF], F32, name="ms", bufs=3)
-            mm(ms, 1, i, h, True, True)
-            eta = ring.tile([P, HALF], F32, name="eta")
-            nc.scalar.activation(eta[:], za[:], ACT.Sigmoid)
-            msg = keep.tile([P, HALF], F32, name="msg%d" % k, tag="msg%d" % k if k else "grouped3", align_bytes=64)
-            nc.vector.tensor_tensor(msg[:], ms[:], eta[:], ALU.mult)
-            message[k] = msg
-
-        def add_own(k):
-            i, h = units[k]
-            ow = psum.tile([P, HALF], F32, name="ow")
-            mm(ow, 3, i, h, True, True)
-            total = ring.tile([P, HALF], F32, name="total")
-            nc.vector.tensor_tensor(total[:], ow[:], message[k][:], ALU.add)
-            res = ring.tile([P, HALF], F32, name="res")
-            nc.scalar.activation(res[:], total[:], ACT.Relu)
-            result[k] = res
-
-        def place(k):
-            i, h = units[k]
+        def products(k):
+            u, q = divmod(k, UNITS)
+            if k == 0:
+                eta = keep.tile([P, 2, PAIR], F32, name="eta0", tag="eta0", align_bytes=64)
+            else:
+                eta = ring.tile([P, 2, PAIR], F32, name="eta")
+            if k == UNITS:
+                own = placed.tile([P, 2 * CHUNKS, PAIR], F32, name="own4", offset=0)
+            else:
+                own = ring.tile([P, 2, PAIR], F32, name="own")
+            msg = ring.tile([P, 2, PAIR], F32, name="msg")
+            ms = psum.tile([P, 2, PAIR], F32, name="ms")
+            for b in range(2):
+                block = 2 * q + b
+                zo = psum.tile([P, 2, PAIR], F32, name="zo", bufs=4)
+                both = zo[:].rearrange("p w c -> p (w c)")
+                mm8(both, u, block, 0, True, False)
+                mm4(zo[:, 0, :], 0, u, block, 0, False, False)
+                mm4(zo[:, 0, :], 0, u, block, 1, False, False)
+                mm8(both, u, block, 1, False, True)
+                mm4(ms[:, b, :], 1, u, block, 0, True, False)
+                mm4(ms[:, b, :], 1, u, block, 1, False, True)
+                nc.scalar.activation(
+                    eta[:, b, :].rearrange("p (e m) -> p e m", e=2), zo[:, 0, :].rearrange("p (m e) -> p e m", e=2), ACT.Sigmoid
+                )
+                nc.scalar.copy(own[:, b, :].rearrange("p (e m) -> p e m", e=2), zo[:, 1, :].rearrange("p (m e) -> p e m", e=2))
             nc.vector.tensor_tensor(
-                pages[i % 2][:].indirect(lists[1][:, 32 * h : 32 * (h + 1)]), result[k][:], gate[:, HALF * h : HALF * (h + 1)], ALU.mult
+                msg[:].rearrange("p b (e m) -> p b e m", e=2),
+                ms[:].rearrange("p b (m e) -> p b e m", e=2),
+                eta[:].rearrange("p b (e m) -> p b e m", e=2),
+                ALU.mult,
             )
-            if h == HALVES - 1:
-                nc.sync.dma_start(out_rows[i], pages[i % 2][:])
-                for c in range(CHUNKS):
-                    nc.scalar.copy(staged[c][:, i // 2, :, i % 2], pages[i % 2][:, CHUNK * c : CHUNK * (c + 1)])
+            summands[k] = (own, msg)
 
-        gated_message(0)
-        for k in range(len(units)):
-            add_own(k)
-            if k + 1 < len(units):
-                gated_message(k + 1)
-            if k >= 1:
-                place(k - 1)
-        place(len(units) - 1)
+        def turn_and_add(k):
+            u, q = divmod(k, UNITS)
+            total = psum.tile([P, 2, UNIT], F32, name="total")
+            for e in range(2):
+                for b in range(2):
+                    for s, summand in enumerate(summands[k]):
+                        nc.tensor.matmul(
+                            total[:, e, P * b : P * (b + 1)], summand[:, b, P * e : P * (e + 1)], ident[:],
+                            start=s == 0, stop=s == 1, is_transpose=True,
+                        )
+            nc.scalar.activation(results[u][:, :, UNIT * q : UNIT * (q + 1)], total[:], ACT.Relu)
+
+        def place(i, first, last):
+            u, e = divmod(i, 2)
+            edges = slice(UNIT * first, UNIT * last)
+            nc.vector.tensor_tensor(
+                pages[i][:].indirect(lists[1][:, 16 * first : 16 * last]), results[u][:, e, edges], gate[:, edges], ALU.mult
+            )
+            if last == UNITS:
+                nc.sync.dma_start(out_rows[i], pages[i][:])
+
+        def round_plane(i):
+            u, e = divmod(i, 2)
+            for c in range(CHUNKS):
+                nc.scalar.copy(staged[c][:, u, :, e], pages[i][:, CHUNK * c : CHUNK * (c + 1)])
+
+        products(0)
+        part_words(1, late_pairs, "eta0")
+        for k in range(2 * UNITS):
+            u, q = divmod(k, UNITS)
+            if k + 1 < 2 * UNITS:
+                products(k + 1)
+            turn_and_add(k)
+            if k == UNITS:
+                for c in range(CHUNKS):
+                    staged.append(placed.tile([P, 2, CHUNK, 2], BF16, name="staged%d" % c, offset=8 * CHUNK * c))
+            if k == UNITS + 1:
+                round_plane(0)
+            place(2 * u, q, q + 1)
+            if u == 0:
+                place(1, q, q + 1)
+            elif q % 2 == 1:
+                place(3, q - 1, q + 1)
+        for i in range(1, PACK):
+            round_plane(i)
 
         y_sc = keep.tile([P, T], U8, name="y_sc", align_bytes=64)
         words_out = out_1[0].rearrange("p t b -> p (t b)").bitcast(I32)

@@ -42,12 +42,11 @@ def tile_list_rgg_ownreluP_kernel(
 
         lists = [keep.tile([P, J // 16], U16, name="src_list"), keep.tile([P, J // 16], U16, name="dst_list")]
         table = keep.tile([P, T], I32, name="table", tag="table", align_bytes=64)
-        table_sc = keep.tile([P, T], U8, name="table_sc", align_bytes=64)
+        table_sc = placed.tile([P, T], U8, name="table_sc", offset=7168, align_bytes=64)
         w4_raw = keep.tile([P, 2 * PASSES, 2 * N], U8, name="w4_raw", align_bytes=64)
         w4 = keep.tile([P, 2 * PASSES, 2 * N], U8, name="w4", align_bytes=64)
-        w4_sc_raw = keep.tile([P, 2, N], U8, name="w4_sc_raw", align_bytes=64)
-        w4_sc_dealt = keep.tile([P, 2 * N], U8, name="w4_sc_dealt", align_bytes=64)
-        w4_sc = keep.tile([P, PASSES, 2 * N], U8, name="w4_sc", align_bytes=64)
+        w4_sc_raw = keep.tile([P, 2 * PASSES, N], U8, name="w4_sc_raw", align_bytes=64)
+        w4_sc = keep.tile([P, 2 * PASSES, N], U8, name="w4_sc", align_bytes=64)
         picked_rows = keep.tile([P, 2 * J], U8, name="picked_rows", tag="picked_rows", align_bytes=64)
         picked_sc = keep.tile([P, PASSES, 2 * J], U8, name="picked_sc", align_bytes=64)
         ident = keep.tile([P, P], F32, name="ident", align_bytes=64)
@@ -60,53 +59,45 @@ def tile_list_rgg_ownreluP_kernel(
         raws = {}
 
         def load_weight(w, a):
-            raw = keep.tile([P, PACK, N], F32, name="raw%d_%d" % (w, a), align_bytes=64)
+            if (w, a) == (1, 1):
+                raw = placed.tile([P, PACK, N], F32, name="raw1_1", offset=0, align_bytes=64)
+            else:
+                raw = keep.tile([P, PACK, N], F32, name="raw%d_%d" % (w, a), align_bytes=64)
             nc.sync.dma_start(raw[:], (wa, wo)[w][512 * a : 512 * (a + 1), :].rearrange("(p j) n -> p j n", j=PACK))
             raws[(w, a)] = raw
 
-        def load_scale_rows(first, last):
-            for n in range(first, last):
-                w, q = divmod(n, QUADS)
-                row = 32 * q + 24
-                scales = (wb_scales, wc_scales)[w]
-                nc.sync.dma_start(w4_sc_raw[row : row + 8, w, :].bitcast(I32), scales[:, 4 * q : 4 * q + 4, :].bitcast(I32))
-
         load_weight(0, 0)
         nc.sync.dma_start(table[:], tab_words[0].rearrange("p t b -> p (t b)").bitcast(I32))
-        load_scale_rows(0, 6)
         load_weight(1, 0)
         load_weight(0, 1)
-        load_scale_rows(6, 8)
         for v, words in enumerate((wb_words, wc_words)):
             nc.sync.dma_start(w4_raw[:, 2 * v : 2 * v + 2, :].bitcast(I32), words.rearrange("a p c -> p a c").bitcast(I32))
-        load_weight(1, 1)
 
         for q in range(QUADS):
             nc.vector.memset(table_sc[32 * q : 32 * q + 24, :].bitcast(I32), 0)
-        for q in range(QUADS):
-            nc.vector.memset(w4_sc_raw[32 * q : 32 * q + 24, :, :].bitcast(I32), 0)
-        nc.gpsimd.memset(w4_sc[96:128].bitcast(I32), 0)
-        nc.gpsimd.memset(picked_sc[96:128].bitcast(I32), 0)
+        nc.gpsimd.memset(w4_sc_raw[:].bitcast(I32), 0)
+        nc.vector.memset(picked_sc[96:128].bitcast(I32), 0)
+        for w, scales in enumerate((wb_scales, wc_scales)):
+            for q in range(QUADS):
+                nc.gpsimd.dma_start(
+                    w4_sc_raw[32 * q : 32 * q + 4, 2 * w : 2 * w + 2, :].bitcast(I32),
+                    scales[:, 4 * q : 4 * q + 4, :].rearrange("a r n -> r a n").bitcast(I32),
+                )
         make_identity(nc, ident[:])
 
         for l in range(2):
             nc.vector.tensor_copy(picked_rows[:, J * l : J * (l + 1)], table_sc[:].indirect(lists[l][:]))
-        nc.vector.tensor_copy(
-            w4_sc_dealt[:].bitcast(U16).rearrange("p (w u m) -> p w u m", w=2, u=2),
-            w4_sc_raw[:].bitcast(U16).rearrange("p w (m u) -> p w u m", u=2),
-        )
         for a in range(PASSES):
             nc.sync.dma_start(picked_sc[0:100, a, :].bitcast(I32), picked_rows[24 + 4 * a : 124 + 4 * a, :].bitcast(I32))
-        for a in range(PASSES):
-            nc.sync.dma_start(w4_sc[0:100, a, :].bitcast(I32), w4_sc_dealt[24 + 4 * a : 124 + 4 * a, :].bitcast(I32))
-
+        load_weight(1, 1)
+        pages = [placed.tile([P, T], F32, name="page0", offset=8192, align_bytes=64)]
+        nc.gpsimd.memset(pages[0][:], 0.0)
         gate = keep.tile([P, J], F32, name="gate", tag="picked_rows", align_bytes=64)
         nc.sync.dma_start(gate[:], wgo)
 
         picked = {}
 
-        def pick_words(h, tag):
-            pairs = keep.tile([P, 2, HALF], U32, name="pairs%d" % h, tag=tag, align_bytes=64)
+        def pick_words(h, pairs):
             for l in (1, 0):
                 nc.vector.tensor_copy(pairs[:, l, :], table[:].bitcast(U32).indirect(lists[l][:, 32 * h : 32 * (h + 1)]))
             return pairs
@@ -131,26 +122,29 @@ def tile_list_rgg_ownreluP_kernel(
             nc.vector.quantize_mx(out=codes[:].bitcast(FP8X4), scales=scales[:], in_=grouped)
             w8[(u, a)] = (codes, scales)
 
-        part_words(0, pick_words(0, "pairs0"), "picked0")
+        part_words(0, pick_words(0, keep.tile([P, 2, HALF], U32, name="pairs0", align_bytes=64)), "picked0")
         nc.vector.tensor_copy(
             w4[:].bitcast(I32).rearrange("p v (u m) -> p v u m", u=2),
             w4_raw[:].bitcast(I32).rearrange("p v (m u) -> p v u m", u=2),
         )
-        pages = [keep.tile([P, T], F32, name="page%d" % i, align_bytes=64) for i in range(2)]
-        for page in pages:
-            nc.vector.memset(page[:], 0.0)
+        nc.vector.tensor_copy(
+            w4_sc[:].bitcast(U16).rearrange("p v (u m) -> p v u m", u=2),
+            w4_sc_raw[:].bitcast(U16).rearrange("p v (m u) -> p v u m", u=2),
+        )
         for a in range(PASSES):
-            grouped = keep.tile([P, 2 * PAIR * PACK], BF16, name="grouped%d" % a, tag="grouped%d" % a, align_bytes=64)
+            if a == 0:
+                grouped = keep.tile([P, 2 * PAIR * PACK], BF16, name="grouped0", align_bytes=64)
+            else:
+                grouped = placed.tile([P, 2 * PAIR * PACK], BF16, name="grouped1", offset=18432, align_bytes=64)
             round_weight(grouped[:], 0, a)
             quantize_weight(grouped[:], 0, a)
-        late_pairs = pick_words(1, "grouped1")
+        late_pairs = pick_words(1, placed.tile([P, 2, HALF], U32, name="pairs1", offset=16384, align_bytes=64))
+        pages.append(placed.tile([P, T], F32, name="page1", offset=20480, align_bytes=64))
+        nc.gpsimd.memset(pages[1][:], 0.0)
         for a in range(PASSES):
             grouped = keep.tile([P, 2 * PAIR * PACK], BF16, name="late%d" % a, align_bytes=64)
             round_weight(grouped[:], 1, a)
             quantize_weight(grouped[:], 1, a)
-        pages.append(keep.tile([P, T], F32, name="page2", tag="table", align_bytes=64))
-        nc.vector.memset(pages[2][:], 0.0)
-        pages.append(pages[0])
 
         def mm(out, l, block, a, rhs, rhs_scale, start, stop):
             h, b = divmod(block, 4)
@@ -168,7 +162,7 @@ def tile_list_rgg_ownreluP_kernel(
             mm(
                 out, 0, block, a,
                 w4[:, 2 * w + a, 2 * PAIR * u : 2 * PAIR * (u + 1)].bitcast(FP4X4),
-                w4_sc[:, a, N * w + PAIR * u : N * w + PAIR * (u + 1)],
+                w4_sc[:, 2 * w + a, PAIR * u : PAIR * (u + 1)],
                 start, stop,
             )
 
@@ -183,12 +177,14 @@ def tile_list_rgg_ownreluP_kernel(
 
         def products(k):
             u, q = divmod(k, UNITS)
-            if k == 0:
-                eta = keep.tile([P, 2, PAIR], F32, name="eta0", tag="eta0", align_bytes=64)
+            if k < 3:
+                eta = keep.tile([P, 2, PAIR], F32, name="eta%d" % k, tag="eta%d" % k, align_bytes=64)
+            elif k == 6:
+                eta = placed.tile([P, 2, PAIR], F32, name="eta6", offset=8192, align_bytes=64)
             else:
                 eta = ring.tile([P, 2, PAIR], F32, name="eta")
             if k == UNITS:
-                own = placed.tile([P, 2 * CHUNKS, PAIR], F32, name="own4", offset=0)
+                own = placed.tile([P, 2 * CHUNKS, PAIR], F32, name="own4", offset=28672, align_bytes=64)
             else:
                 own = ring.tile([P, 2, PAIR], F32, name="own")
             msg = ring.tile([P, 2, PAIR], F32, name="msg")
@@ -245,19 +241,22 @@ def tile_list_rgg_ownreluP_kernel(
         part_words(1, late_pairs, "eta0")
         for k in range(2 * UNITS):
             u, q = divmod(k, UNITS)
+            if k == UNITS + 1:
+                round_plane(0)
             if k + 1 < 2 * UNITS:
                 products(k + 1)
+            if k < 2:
+                pages.append(keep.tile([P, T], F32, name="page%d" % (k + 2), tag="eta%d" % (k + 1), align_bytes=64))
+                nc.gpsimd.memset(pages[k + 2][:], 0.0)
             turn_and_add(k)
             if k == UNITS:
                 for c in range(CHUNKS):
-                    staged.append(placed.tile([P, 2, CHUNK, 2], BF16, name="staged%d" % c, offset=8 * CHUNK * c))
-            if k == UNITS + 1:
-                round_plane(0)
+                    staged.append(placed.tile([P, 2, CHUNK, 2], BF16, name="staged%d" % c, offset=28672 + 8 * CHUNK * c, align_bytes=64))
             place(2 * u, q, q + 1)
-            if u == 0:
-                place(1, q, q + 1)
-            elif q % 2 == 1:
-                place(3, q - 1, q + 1)
+            if q < 2:
+                place(2 * u + 1, q, q + 1)
+            elif q == 3:
+                place(2 * u + 1, 2, 4)
         for i in range(1, PACK):
             round_plane(i)
 

@@ -25,9 +25,9 @@ QUADS = 4
 PAIR = 256
 UNIT = 256
 UNITS = J // UNIT
-CHUNK = 256
+CHUNK = 512
 CHUNKS = T // CHUNK
-SCALAR_CHUNKS = 2
+SCALAR_CHUNKS = 1
 
 
 def tile_list_rgg_ownreluP_kernel(
@@ -42,13 +42,11 @@ def tile_list_rgg_ownreluP_kernel(
 
         lists = [keep.tile([P, J // 16], U16, name="src_list"), keep.tile([P, J // 16], U16, name="dst_list")]
         table = keep.tile([P, T], I32, name="table", tag="table", align_bytes=64)
-        table_sc = placed.tile([P, T], U8, name="table_sc", offset=7168, align_bytes=64)
+        table_sc = keep.tile([P, T], U8, name="table_sc", align_bytes=64)
         w4_raw = keep.tile([P, 2 * PASSES, 2 * N], U8, name="w4_raw", align_bytes=64)
         w4 = keep.tile([P, 2 * PASSES, 2 * N], U8, name="w4", align_bytes=64)
         w4_sc_raw = keep.tile([P, 2 * PASSES, N], U8, name="w4_sc_raw", align_bytes=64)
-        w4_sc = keep.tile([P, 2 * PASSES, N], U8, name="w4_sc", align_bytes=64)
         picked_rows = keep.tile([P, 2 * J], U8, name="picked_rows", tag="picked_rows", align_bytes=64)
-        picked_sc = keep.tile([P, PASSES, 2 * J], U8, name="picked_sc", align_bytes=64)
         ident = keep.tile([P, P], F32, name="ident", align_bytes=64)
 
         nc.sync.dma_start(lists[0][:], offs)
@@ -59,8 +57,8 @@ def tile_list_rgg_ownreluP_kernel(
         raws = {}
 
         def load_weight(w, a):
-            if (w, a) == (1, 1):
-                raw = placed.tile([P, PACK, N], F32, name="raw1_1", offset=0, align_bytes=64)
+            if (w, a) == (0, 0):
+                raw = placed.tile([P, PACK, N], F32, name="raw0_0", offset=45056, align_bytes=64)
             else:
                 raw = keep.tile([P, PACK, N], F32, name="raw%d_%d" % (w, a), align_bytes=64)
             nc.sync.dma_start(raw[:], (wa, wo)[w][512 * a : 512 * (a + 1), :].rearrange("(p j) n -> p j n", j=PACK))
@@ -68,61 +66,81 @@ def tile_list_rgg_ownreluP_kernel(
 
         load_weight(0, 0)
         nc.sync.dma_start(table[:], tab_words[0].rearrange("p t b -> p (t b)").bitcast(I32))
-        load_weight(1, 0)
-        load_weight(0, 1)
+        nc.gpsimd.memset(w4_sc_raw[:].bitcast(I32), 0)
+        for w, scales in enumerate((wb_scales, wc_scales)):
+            nc.sync.dma_start(w4_sc_raw[0:128:8, 2 * w : 2 * w + 2, :].bitcast(I32), scales.rearrange("a s n -> s a n").bitcast(I32))
         for v, words in enumerate((wb_words, wc_words)):
             nc.sync.dma_start(w4_raw[:, 2 * v : 2 * v + 2, :].bitcast(I32), words.rearrange("a p c -> p a c").bitcast(I32))
+        load_weight(1, 0)
+        load_weight(0, 1)
+        last_raw = []
+        for half in range(2):
+            raw = keep.tile([P, PACK, N // 2], F32, name="last_raw%d" % half, align_bytes=64)
+            nc.sync.dma_start(raw[:], wo[512:1024, 256 * half : 256 * (half + 1)].rearrange("(p j) n -> p j n", j=PACK))
+            last_raw.append(raw)
+
+        warm = keep.tile([P, 2], F32, name="warm")
+        nc.vector.memset(warm[:, 0:1], 0.0)
+        nc.scalar.activation(warm[:, 1:2], warm[:, 0:1], ACT.Sigmoid)
+
+        for r in range(1, 4):
+            nc.scalar.dma_start(w4_sc_raw[r:128:32].bitcast(I32), w4_sc_raw[8 * r : 128 : 32].bitcast(I32))
 
         for q in range(QUADS):
-            nc.vector.memset(table_sc[32 * q : 32 * q + 24, :].bitcast(I32), 0)
-        nc.gpsimd.memset(w4_sc_raw[:].bitcast(I32), 0)
-        nc.vector.memset(picked_sc[96:128].bitcast(I32), 0)
-        for w, scales in enumerate((wb_scales, wc_scales)):
-            for q in range(QUADS):
-                nc.gpsimd.dma_start(
-                    w4_sc_raw[32 * q : 32 * q + 4, 2 * w : 2 * w + 2, :].bitcast(I32),
-                    scales[:, 4 * q : 4 * q + 4, :].rearrange("a r n -> r a n").bitcast(I32),
-                )
+            nc.gpsimd.memset(table_sc[32 * q : 32 * q + 24, :].bitcast(I32), 0)
         make_identity(nc, ident[:])
+        pages = [placed.tile([P, T], F32, name="page0", offset=8192, align_bytes=64)]
+        nc.gpsimd.memset(pages[0][:], 0.0)
 
         for l in range(2):
             nc.vector.tensor_copy(picked_rows[:, J * l : J * (l + 1)], table_sc[:].indirect(lists[l][:]))
-        for a in range(PASSES):
-            nc.sync.dma_start(picked_sc[0:100, a, :].bitcast(I32), picked_rows[24 + 4 * a : 124 + 4 * a, :].bitcast(I32))
-        load_weight(1, 1)
-        pages = [placed.tile([P, T], F32, name="page0", offset=8192, align_bytes=64)]
-        nc.gpsimd.memset(pages[0][:], 0.0)
-        gate = keep.tile([P, J], F32, name="gate", tag="picked_rows", align_bytes=64)
-        nc.sync.dma_start(gate[:], wgo)
 
         picked = {}
 
-        def pick_words(h, pairs):
-            for l in (1, 0):
-                nc.vector.tensor_copy(pairs[:, l, :], table[:].bitcast(U32).indirect(lists[l][:, 32 * h : 32 * (h + 1)]))
-            return pairs
+        def pick_words(l, h, pairs):
+            nc.vector.tensor_copy(pairs, table[:].bitcast(U32).indirect(lists[l][:, 32 * h : 32 * (h + 1)]))
 
-        def part_words(h, pairs, tag):
-            parted = keep.tile([P, 2, PASSES, 2 * HALF], U8, name="picked%d" % h, tag=tag, align_bytes=64)
-            nc.vector.tensor_copy(parted[:].bitcast(U16), pairs[:].bitcast(U16).rearrange("p l (s a) -> p l a s", a=PASSES))
-            picked[h] = parted
+        def part_words(parted, pairs, pattern):
+            nc.vector.tensor_copy(parted.bitcast(U16), pairs.bitcast(U16).rearrange(pattern, a=PASSES))
 
         w8 = {}
-
-        def round_weight(grouped, u, a):
-            for w in range(2):
-                nc.scalar.copy(
-                    grouped[:, w * PAIR * PACK : (w + 1) * PAIR * PACK].rearrange("p (m e j) -> p m j e", e=2, j=PACK),
-                    raws[(w, a)][:].rearrange("p j (m u e) -> p u m j e", u=2, e=2)[:, u],
+        for u in range(2):
+            for a in range(PASSES):
+                w8[(u, a)] = (
+                    keep.tile([P, 2 * PAIR], U32, name="codes%d_%d" % (u, a), align_bytes=64),
+                    keep.tile([P, 2 * PAIR], U8, name="scales%d_%d" % (u, a), align_bytes=64),
                 )
 
-        def quantize_weight(grouped, u, a):
-            codes = keep.tile([P, 2 * PAIR], U32, name="codes%d_%d" % (u, a), align_bytes=64)
-            scales = keep.tile([P, 2 * PAIR], U8, name="scales%d_%d" % (u, a), align_bytes=64)
-            nc.vector.quantize_mx(out=codes[:].bitcast(FP8X4), scales=scales[:], in_=grouped)
-            w8[(u, a)] = (codes, scales)
+        def quantize_weight(grouped, u, w, a):
+            codes, scales = w8[(u, a)]
+            cols = slice(PAIR * w, PAIR * (w + 1))
+            nc.vector.quantize_mx(out=codes[:, cols].bitcast(FP8X4), scales=scales[:, cols], in_=grouped)
 
-        part_words(0, pick_words(0, keep.tile([P, 2, HALF], U32, name="pairs0", align_bytes=64)), "picked0")
+        def round_both_pairs(w, a):
+            grouped = keep.tile([P, 2, PAIR * PACK], BF16, name="grouped%d_%d" % (w, a), align_bytes=64)
+            nc.scalar.copy(
+                grouped[:].rearrange("p u (m e j) -> p m j u e", e=2, j=PACK),
+                raws[(w, a)][:].rearrange("p j (m u e) -> p m j u e", u=2, e=2),
+            )
+            for u in range(2):
+                quantize_weight(grouped[:, u, :], u, w, a)
+
+        def round_last(grouped, u):
+            for half in range(2):
+                nc.scalar.copy(
+                    grouped[:, 512 * half : 512 * (half + 1)].rearrange("p (m e j) -> p m j e", e=2, j=PACK),
+                    last_raw[half][:].rearrange("p j (m u e) -> p u m j e", u=2, e=2)[:, u],
+                )
+            quantize_weight(grouped[:], u, 1, 1)
+
+        pairs0 = keep.tile([P, 2, HALF], U32, name="pairs0", tag="pairs0", align_bytes=64)
+        for l in (1, 0):
+            pick_words(l, 0, pairs0[:, l, :])
+        picked0 = keep.tile([P, 2, PASSES, 2 * HALF], U8, name="picked0", align_bytes=64)
+        part_words(picked0[:], pairs0[:], "p l (s a) -> p l a s")
+        for l in range(2):
+            picked[(l, 0)] = picked0[:, l]
+        w4_sc = keep.tile([P, 2 * PASSES, N], U8, name="w4_sc", tag="pairs0", align_bytes=64)
         nc.vector.tensor_copy(
             w4[:].bitcast(I32).rearrange("p v (u m) -> p v u m", u=2),
             w4_raw[:].bitcast(I32).rearrange("p v (m u) -> p v u m", u=2),
@@ -131,26 +149,33 @@ def tile_list_rgg_ownreluP_kernel(
             w4_sc[:].bitcast(U16).rearrange("p v (u m) -> p v u m", u=2),
             w4_sc_raw[:].bitcast(U16).rearrange("p v (m u) -> p v u m", u=2),
         )
+        round_both_pairs(0, 0)
+        picked_sc = placed.tile([P, PASSES, 2 * J], U8, name="picked_sc", offset=45056, align_bytes=64)
+        nc.gpsimd.memset(picked_sc[96:128].bitcast(I32), 0)
         for a in range(PASSES):
-            if a == 0:
-                grouped = keep.tile([P, 2 * PAIR * PACK], BF16, name="grouped0", align_bytes=64)
-            else:
-                grouped = placed.tile([P, 2 * PAIR * PACK], BF16, name="grouped1", offset=18432, align_bytes=64)
-            round_weight(grouped[:], 0, a)
-            quantize_weight(grouped[:], 0, a)
-        late_pairs = pick_words(1, placed.tile([P, 2, HALF], U32, name="pairs1", offset=16384, align_bytes=64))
-        pages.append(placed.tile([P, T], F32, name="page1", offset=20480, align_bytes=64))
+            nc.scalar.dma_start(picked_sc[0:100, a, :].bitcast(I32), picked_rows[24 + 4 * a : 124 + 4 * a, :].bitcast(I32))
+        pages.append(placed.tile([P, T], F32, name="page1", offset=49152, align_bytes=64))
         nc.gpsimd.memset(pages[1][:], 0.0)
-        for a in range(PASSES):
-            grouped = keep.tile([P, 2 * PAIR * PACK], BF16, name="late%d" % a, align_bytes=64)
-            round_weight(grouped[:], 1, a)
-            quantize_weight(grouped[:], 1, a)
+        gate = keep.tile([P, J], F32, name="gate", tag="picked_rows", align_bytes=64)
+        nc.sync.dma_start(gate[:], wgo)
+        round_both_pairs(1, 0)
+        round_both_pairs(0, 1)
+        round_last(placed.tile([P, PAIR * PACK], BF16, name="last_first", offset=19456, align_bytes=64), 0)
+        late_pairs = [
+            placed.tile([P, HALF], U32, name="pairs1_0", offset=18432, align_bytes=64),
+            keep.tile([P, HALF], U32, name="pairs1_1", align_bytes=64),
+        ]
+        for l in (1, 0):
+            pick_words(l, 1, late_pairs[l][:])
+        parted = placed.tile([P, PASSES, 2 * HALF], U8, name="picked1_1", offset=19456 + 1024, align_bytes=64)
+        part_words(parted[:], late_pairs[1][:], "p (s a) -> p a s")
+        picked[(1, 1)] = parted[:]
 
         def mm(out, l, block, a, rhs, rhs_scale, start, stop):
             h, b = divmod(block, 4)
             nc.tensor.matmul_mx(
                 out=out,
-                lhsT=picked[h][:, l, a, 2 * P * b : 2 * P * (b + 1)].bitcast(FP4X4),
+                lhsT=picked[(l, h)][:, a, 2 * P * b : 2 * P * (b + 1)].bitcast(FP4X4),
                 lhsT_scale=picked_sc[:, a, J * l + P * block : J * l + P * (block + 1)],
                 rhs=rhs,
                 rhs_scale=rhs_scale,
@@ -183,12 +208,15 @@ def tile_list_rgg_ownreluP_kernel(
                 eta = placed.tile([P, 2, PAIR], F32, name="eta6", offset=8192, align_bytes=64)
             else:
                 eta = ring.tile([P, 2, PAIR], F32, name="eta")
-            if k == UNITS:
-                own = placed.tile([P, 2 * CHUNKS, PAIR], F32, name="own4", offset=28672, align_bytes=64)
+            if k == 0:
+                own = keep.tile([P, 2, PAIR], F32, name="own0", tag="own0", align_bytes=64)
+            elif k == UNITS:
+                own = placed.tile([P, 4 * CHUNKS, PAIR], F32, name="own4", offset=28672, align_bytes=64)
             else:
                 own = ring.tile([P, 2, PAIR], F32, name="own")
             msg = ring.tile([P, 2, PAIR], F32, name="msg")
             ms = psum.tile([P, 2, PAIR], F32, name="ms")
+            banks = []
             for b in range(2):
                 block = 2 * q + b
                 zo = psum.tile([P, 2, PAIR], F32, name="zo", bufs=4)
@@ -202,6 +230,8 @@ def tile_list_rgg_ownreluP_kernel(
                 nc.scalar.activation(
                     eta[:, b, :].rearrange("p (e m) -> p e m", e=2), zo[:, 0, :].rearrange("p (m e) -> p e m", e=2), ACT.Sigmoid
                 )
+                banks.append(zo)
+            for b, zo in enumerate(banks):
                 nc.scalar.copy(own[:, b, :].rearrange("p (e m) -> p e m", e=2), zo[:, 1, :].rearrange("p (m e) -> p e m", e=2))
             nc.vector.tensor_tensor(
                 msg[:].rearrange("p b (e m) -> p b e m", e=2),
@@ -235,10 +265,15 @@ def tile_list_rgg_ownreluP_kernel(
         def round_plane(i):
             u, e = divmod(i, 2)
             for c in range(CHUNKS):
-                nc.scalar.copy(staged[c][:, u, :, e], pages[i][:, CHUNK * c : CHUNK * (c + 1)])
+                if u == 1 and c == 0:
+                    nc.vector.tensor_copy(staged[c][:, u, :, e], pages[i][:, CHUNK * c : CHUNK * (c + 1)])
+                else:
+                    nc.scalar.copy(staged[c][:, u, :, e], pages[i][:, CHUNK * c : CHUNK * (c + 1)])
 
         products(0)
-        part_words(1, late_pairs, "eta0")
+        parted = keep.tile([P, PASSES, 2 * HALF], U8, name="picked1_0", tag="eta0", align_bytes=64)
+        part_words(parted[:], late_pairs[0][:], "p (s a) -> p a s")
+        picked[(0, 1)] = parted[:]
         for k in range(2 * UNITS):
             u, q = divmod(k, UNITS)
             if k == UNITS + 1:
@@ -249,6 +284,8 @@ def tile_list_rgg_ownreluP_kernel(
                 pages.append(keep.tile([P, T], F32, name="page%d" % (k + 2), tag="eta%d" % (k + 1), align_bytes=64))
                 nc.gpsimd.memset(pages[k + 2][:], 0.0)
             turn_and_add(k)
+            if k == 0:
+                round_last(keep.tile([P, PAIR * PACK], BF16, name="last_second", tag="own0", align_bytes=64), 1)
             if k == UNITS:
                 for c in range(CHUNKS):
                     staged.append(placed.tile([P, 2, CHUNK, 2], BF16, name="staged%d" % c, offset=28672 + 8 * CHUNK * c, align_bytes=64))
@@ -263,7 +300,7 @@ def tile_list_rgg_ownreluP_kernel(
         y_sc = keep.tile([P, T], U8, name="y_sc", align_bytes=64)
         words_out = out_1[0].rearrange("p t b -> p (t b)").bitcast(I32)
         woven = [keep.tile([P, CHUNK * PACK], BF16, name="woven%d" % c, align_bytes=64) for c in range(CHUNKS)]
-        y_codes = [keep.tile([P, 2 * CHUNK], I32, name="y_codes%d" % c, align_bytes=64) for c in range(CHUNKS // 2)]
+        y_codes = [keep.tile([P, CHUNK], I32, name="y_codes%d" % c, align_bytes=64) for c in range(CHUNKS)]
 
         def weave(c):
             dst = woven[c][:].bitcast(U32).rearrange("p (c e u) -> p c u e", e=4, u=2)
@@ -274,12 +311,8 @@ def tile_list_rgg_ownreluP_kernel(
                 nc.vector.tensor_copy(dst.bitcast(I32), src.bitcast(I32))
 
         def quantize_chunk(c):
-            codes = y_codes[c // 2]
-            nc.vector.quantize_mx(
-                out=codes[:, CHUNK * (c % 2) : CHUNK * (c % 2 + 1)].bitcast(FP8X4), scales=y_sc[:, CHUNK * c : CHUNK * (c + 1)], in_=woven[c][:]
-            )
-            if c % 2 == 1:
-                nc.sync.dma_start(words_out[:, CHUNK * (c - 1) : CHUNK * (c + 1)], codes[:])
+            nc.vector.quantize_mx(out=y_codes[c][:].bitcast(FP8X4), scales=y_sc[:, CHUNK * c : CHUNK * (c + 1)], in_=woven[c][:])
+            nc.sync.dma_start(words_out[:, CHUNK * c : CHUNK * (c + 1)], y_codes[c][:])
 
         weave(0)
         for c in range(CHUNKS):

@@ -42,7 +42,8 @@ def tile_list_rgg_ownreluP_kernel(
 
         lists = [keep.tile([P, J // 16], U16, name="src_list"), keep.tile([P, J // 16], U16, name="dst_list")]
         table = keep.tile([P, T], I32, name="table", tag="table", align_bytes=64)
-        table_sc = keep.tile([P, T], U8, name="table_sc", align_bytes=64)
+        table_sc = placed.tile([P, T], U8, name="table_sc", offset=3072, align_bytes=64)
+        picked_sc = keep.tile([P, PASSES, 2 * J], U8, name="picked_sc", align_bytes=64)
         w4_raw = keep.tile([P, 2 * PASSES, 2 * N], U8, name="w4_raw", align_bytes=64)
         w4 = keep.tile([P, 2 * PASSES, 2 * N], U8, name="w4", align_bytes=64)
         w4_sc_raw = keep.tile([P, 2 * PASSES, N], U8, name="w4_sc_raw", align_bytes=64)
@@ -57,10 +58,7 @@ def tile_list_rgg_ownreluP_kernel(
         raws = {}
 
         def load_weight(w, a):
-            if (w, a) == (0, 0):
-                raw = placed.tile([P, PACK, N], F32, name="raw0_0", offset=45056, align_bytes=64)
-            else:
-                raw = keep.tile([P, PACK, N], F32, name="raw%d_%d" % (w, a), align_bytes=64)
+            raw = keep.tile([P, PACK, N], F32, name="raw%d_%d" % (w, a), align_bytes=64)
             nc.sync.dma_start(raw[:], (wa, wo)[w][512 * a : 512 * (a + 1), :].rearrange("(p j) n -> p j n", j=PACK))
             raws[(w, a)] = raw
 
@@ -73,11 +71,6 @@ def tile_list_rgg_ownreluP_kernel(
             nc.sync.dma_start(w4_raw[:, 2 * v : 2 * v + 2, :].bitcast(I32), words.rearrange("a p c -> p a c").bitcast(I32))
         load_weight(1, 0)
         load_weight(0, 1)
-        last_raw = []
-        for half in range(2):
-            raw = keep.tile([P, PACK, N // 2], F32, name="last_raw%d" % half, align_bytes=64)
-            nc.sync.dma_start(raw[:], wo[512:1024, 256 * half : 256 * (half + 1)].rearrange("(p j) n -> p j n", j=PACK))
-            last_raw.append(raw)
 
         warm = keep.tile([P, 2], F32, name="warm")
         nc.vector.memset(warm[:, 0:1], 0.0)
@@ -87,13 +80,23 @@ def tile_list_rgg_ownreluP_kernel(
             nc.scalar.dma_start(w4_sc_raw[r:128:32].bitcast(I32), w4_sc_raw[8 * r : 128 : 32].bitcast(I32))
 
         for q in range(QUADS):
-            nc.gpsimd.memset(table_sc[32 * q : 32 * q + 24, :].bitcast(I32), 0)
+            nc.vector.memset(table_sc[32 * q : 32 * q + 24, :].bitcast(I32), 0)
+        pages = [keep.tile([P, T], F32, name="page0", align_bytes=64)]
+        nc.vector.memset(pages[0][:].bitcast(I32), 0)
+        nc.vector.memset(picked_sc[96:128].bitcast(I32), 0)
         make_identity(nc, ident[:])
-        pages = [placed.tile([P, T], F32, name="page0", offset=8192, align_bytes=64)]
-        nc.gpsimd.memset(pages[0][:], 0.0)
 
         for l in range(2):
             nc.vector.tensor_copy(picked_rows[:, J * l : J * (l + 1)], table_sc[:].indirect(lists[l][:]))
+        for a in range(PASSES):
+            nc.sync.dma_start(picked_sc[0:100, a, :].bitcast(I32), picked_rows[24 + 4 * a : 124 + 4 * a, :].bitcast(I32))
+        last_raw = []
+        for half in range(2):
+            raw = placed.tile([P, PACK, N // 2], F32, name="last_raw%d" % half, offset=4096 * half, align_bytes=64)
+            nc.sync.dma_start(raw[:], wo[512:1024, 256 * half : 256 * (half + 1)].rearrange("(p j) n -> p j n", j=PACK))
+            last_raw.append(raw)
+        gate = keep.tile([P, J], F32, name="gate", tag="picked_rows", align_bytes=64)
+        nc.sync.dma_start(gate[:], wgo)
 
         picked = {}
 
@@ -117,7 +120,10 @@ def tile_list_rgg_ownreluP_kernel(
             nc.vector.quantize_mx(out=codes[:, cols].bitcast(FP8X4), scales=scales[:, cols], in_=grouped)
 
         def round_both_pairs(w, a):
-            grouped = keep.tile([P, 2, PAIR * PACK], BF16, name="grouped%d_%d" % (w, a), align_bytes=64)
+            if (w, a) == (1, 0):
+                grouped = placed.tile([P, 2, PAIR * PACK], BF16, name="grouped1_0", offset=45056, align_bytes=64)
+            else:
+                grouped = keep.tile([P, 2, PAIR * PACK], BF16, name="grouped%d_%d" % (w, a), align_bytes=64)
             nc.scalar.copy(
                 grouped[:].rearrange("p u (m e j) -> p m j u e", e=2, j=PACK),
                 raws[(w, a)][:].rearrange("p j (m u e) -> p m j u e", u=2, e=2),
@@ -133,14 +139,14 @@ def tile_list_rgg_ownreluP_kernel(
                 )
             quantize_weight(grouped[:], u, 1, 1)
 
-        pairs0 = keep.tile([P, 2, HALF], U32, name="pairs0", tag="pairs0", align_bytes=64)
+        pairs0 = placed.tile([P, 2, HALF], U32, name="pairs0", offset=8192, align_bytes=64)
         for l in (1, 0):
             pick_words(l, 0, pairs0[:, l, :])
         picked0 = keep.tile([P, 2, PASSES, 2 * HALF], U8, name="picked0", align_bytes=64)
         part_words(picked0[:], pairs0[:], "p l (s a) -> p l a s")
         for l in range(2):
             picked[(l, 0)] = picked0[:, l]
-        w4_sc = keep.tile([P, 2 * PASSES, N], U8, name="w4_sc", tag="pairs0", align_bytes=64)
+        w4_sc = placed.tile([P, 2 * PASSES, N], U8, name="w4_sc", offset=8192, align_bytes=64)
         nc.vector.tensor_copy(
             w4[:].bitcast(I32).rearrange("p v (u m) -> p v u m", u=2),
             w4_raw[:].bitcast(I32).rearrange("p v (m u) -> p v u m", u=2),
@@ -150,20 +156,14 @@ def tile_list_rgg_ownreluP_kernel(
             w4_sc_raw[:].bitcast(U16).rearrange("p v (m u) -> p v u m", u=2),
         )
         round_both_pairs(0, 0)
-        picked_sc = placed.tile([P, PASSES, 2 * J], U8, name="picked_sc", offset=45056, align_bytes=64)
-        nc.gpsimd.memset(picked_sc[96:128].bitcast(I32), 0)
-        for a in range(PASSES):
-            nc.scalar.dma_start(picked_sc[0:100, a, :].bitcast(I32), picked_rows[24 + 4 * a : 124 + 4 * a, :].bitcast(I32))
-        pages.append(placed.tile([P, T], F32, name="page1", offset=49152, align_bytes=64))
-        nc.gpsimd.memset(pages[1][:], 0.0)
-        gate = keep.tile([P, J], F32, name="gate", tag="picked_rows", align_bytes=64)
-        nc.sync.dma_start(gate[:], wgo)
         round_both_pairs(1, 0)
         round_both_pairs(0, 1)
         round_last(placed.tile([P, PAIR * PACK], BF16, name="last_first", offset=19456, align_bytes=64), 0)
+        pages.append(placed.tile([P, T], F32, name="page1", offset=47104, align_bytes=64))
+        nc.vector.memset(pages[1][:].bitcast(I32), 0)
         late_pairs = [
             placed.tile([P, HALF], U32, name="pairs1_0", offset=18432, align_bytes=64),
-            keep.tile([P, HALF], U32, name="pairs1_1", align_bytes=64),
+            placed.tile([P, HALF], U32, name="pairs1_1", offset=45056, align_bytes=64),
         ]
         for l in (1, 0):
             pick_words(l, 1, late_pairs[l][:])
@@ -202,10 +202,8 @@ def tile_list_rgg_ownreluP_kernel(
 
         def products(k):
             u, q = divmod(k, UNITS)
-            if k < 3:
+            if k < 2:
                 eta = keep.tile([P, 2, PAIR], F32, name="eta%d" % k, tag="eta%d" % k, align_bytes=64)
-            elif k == 6:
-                eta = placed.tile([P, 2, PAIR], F32, name="eta6", offset=8192, align_bytes=64)
             else:
                 eta = ring.tile([P, 2, PAIR], F32, name="eta")
             if k == 0:
@@ -280,9 +278,10 @@ def tile_list_rgg_ownreluP_kernel(
                 round_plane(0)
             if k + 1 < 2 * UNITS:
                 products(k + 1)
-            if k < 2:
-                pages.append(keep.tile([P, T], F32, name="page%d" % (k + 2), tag="eta%d" % (k + 1), align_bytes=64))
-                nc.gpsimd.memset(pages[k + 2][:], 0.0)
+            if k == 0:
+                pages.append(keep.tile([P, T], F32, name="page2", tag="eta1", align_bytes=64))
+                nc.vector.memset(pages[2][:].bitcast(I32), 0)
+                pages.append(pages[0])
             turn_and_add(k)
             if k == 0:
                 round_last(keep.tile([P, PAIR * PACK], BF16, name="last_second", tag="own0", align_bytes=64), 1)
@@ -290,10 +289,10 @@ def tile_list_rgg_ownreluP_kernel(
                 for c in range(CHUNKS):
                     staged.append(placed.tile([P, 2, CHUNK, 2], BF16, name="staged%d" % c, offset=28672 + 8 * CHUNK * c, align_bytes=64))
             place(2 * u, q, q + 1)
-            if q < 2:
-                place(2 * u + 1, q, q + 1)
-            elif q == 3:
-                place(2 * u + 1, 2, 4)
+            if u == 0 and q < 2:
+                place(1, q, q + 1)
+            elif q % 2 == 1:
+                place(2 * u + 1, q - 1, q + 1)
         for i in range(1, PACK):
             round_plane(i)
 

@@ -25,9 +25,11 @@ QUADS = 4
 PAIR = 256
 UNIT = 256
 UNITS = J // UNIT
-CHUNK = 512
-CHUNKS = T // CHUNK
-SCALAR_CHUNKS = 1
+WIDTHS = (512, 512, 256, 512, 256)
+STARTS = [sum(WIDTHS[:c]) for c in range(len(WIDTHS))]
+CHUNKS = len(WIDTHS)
+VECTOR_CHUNKS = 3
+EARLY = 2
 
 
 def tile_list_rgg_ownreluP_kernel(
@@ -69,8 +71,8 @@ def tile_list_rgg_ownreluP_kernel(
             nc.sync.dma_start(w4_sc_raw[0:128:8, 2 * w : 2 * w + 2, :].bitcast(I32), scales.rearrange("a s n -> s a n").bitcast(I32))
         for v, words in enumerate((wb_words, wc_words)):
             nc.sync.dma_start(w4_raw[:, 2 * v : 2 * v + 2, :].bitcast(I32), words.rearrange("a p c -> p a c").bitcast(I32))
-        load_weight(1, 0)
         load_weight(0, 1)
+        load_weight(1, 0)
 
         warm = keep.tile([P, 2], F32, name="warm")
         nc.vector.memset(warm[:, 0:1], 0.0)
@@ -120,8 +122,8 @@ def tile_list_rgg_ownreluP_kernel(
             nc.vector.quantize_mx(out=codes[:, cols].bitcast(FP8X4), scales=scales[:, cols], in_=grouped)
 
         def round_both_pairs(w, a):
-            if (w, a) == (1, 0):
-                grouped = placed.tile([P, 2, PAIR * PACK], BF16, name="grouped1_0", offset=45056, align_bytes=64)
+            if (w, a) == (0, 1):
+                grouped = placed.tile([P, 2, PAIR * PACK], BF16, name="grouped0_1", offset=45056, align_bytes=64)
             else:
                 grouped = keep.tile([P, 2, PAIR * PACK], BF16, name="grouped%d_%d" % (w, a), align_bytes=64)
             nc.scalar.copy(
@@ -137,7 +139,7 @@ def tile_list_rgg_ownreluP_kernel(
                     grouped[:, 512 * half : 512 * (half + 1)].rearrange("p (m e j) -> p m j e", e=2, j=PACK),
                     last_raw[half][:].rearrange("p j (m u e) -> p u m j e", u=2, e=2)[:, u],
                 )
-            quantize_weight(grouped[:], u, 1, 1)
+            quantize_weight(grouped, u, 1, 1)
 
         pairs0 = placed.tile([P, 2, HALF], U32, name="pairs0", offset=8192, align_bytes=64)
         for l in (1, 0):
@@ -156,20 +158,20 @@ def tile_list_rgg_ownreluP_kernel(
             w4_sc_raw[:].bitcast(U16).rearrange("p v (m u) -> p v u m", u=2),
         )
         round_both_pairs(0, 0)
-        round_both_pairs(1, 0)
         round_both_pairs(0, 1)
-        round_last(placed.tile([P, PAIR * PACK], BF16, name="last_first", offset=19456, align_bytes=64), 0)
-        pages.append(placed.tile([P, T], F32, name="page1", offset=47104, align_bytes=64))
-        nc.vector.memset(pages[1][:].bitcast(I32), 0)
-        late_pairs = [
-            placed.tile([P, HALF], U32, name="pairs1_0", offset=18432, align_bytes=64),
-            placed.tile([P, HALF], U32, name="pairs1_1", offset=45056, align_bytes=64),
-        ]
+        round_both_pairs(1, 0)
+        round_last(placed.tile([P, 2112], BF16, name="last_first", offset=57344, align_bytes=64)[:, 0 : PAIR * PACK], 0)
+        pairs1 = placed.tile([P, 2, HALF], U32, name="pairs1", offset=45056 - 2048, align_bytes=64)
         for l in (1, 0):
-            pick_words(l, 1, late_pairs[l][:])
-        parted = placed.tile([P, PASSES, 2 * HALF], U8, name="picked1_1", offset=19456 + 1024, align_bytes=64)
-        part_words(parted[:], late_pairs[1][:], "p (s a) -> p a s")
-        picked[(1, 1)] = parted[:]
+            pick_words(l, 1, pairs1[:, l, :])
+        picked1 = placed.tile([P, 2, PASSES, 2 * HALF], U8, name="picked1", offset=57344 + 64, align_bytes=64)
+        part_words(picked1[:], pairs1[:], "p l (s a) -> p l a s")
+        for l in range(2):
+            picked[(l, 1)] = picked1[:, l]
+        for i, offset in ((1, 57344 + 64 - 8192), (2, 57344 + 4160)):
+            pages.append(placed.tile([P, T], F32, name="page%d" % i, offset=offset, align_bytes=64))
+            nc.vector.memset(pages[i][:].bitcast(I32), 0)
+        pages.append(pages[0])
 
         def mm(out, l, block, a, rhs, rhs_scale, start, stop):
             h, b = divmod(block, 4)
@@ -195,6 +197,16 @@ def tile_list_rgg_ownreluP_kernel(
             codes, scales = w8[(u, a)]
             mm(out, 1, block, a, codes[:].bitcast(FP8X4), scales[:], start, stop)
 
+        def mm8_narrow(out, w, block, start, stop):
+            for a in range(PASSES):
+                codes, scales = w8[(0, a)]
+                for c in range(2):
+                    cols = slice(PAIR * w + P * c, PAIR * w + P * (c + 1))
+                    mm(
+                        out[:, P * c : P * (c + 1)], 1, block, a, codes[:, cols].bitcast(FP8X4), scales[:, cols],
+                        start and a == 0 and c == 0, stop and a == PASSES - 1 and c == 1,
+                    )
+
         summands = {}
         results = [keep.tile([P, 2, J], F32, name="result%d" % u, align_bytes=64) for u in range(2)]
         staged = []
@@ -202,33 +214,43 @@ def tile_list_rgg_ownreluP_kernel(
 
         def products(k):
             u, q = divmod(k, UNITS)
-            if k < 2:
-                eta = keep.tile([P, 2, PAIR], F32, name="eta%d" % k, tag="eta%d" % k, align_bytes=64)
-            else:
-                eta = ring.tile([P, 2, PAIR], F32, name="eta")
+            eta = ring.tile([P, 2, PAIR], F32, name="eta")
             if k == 0:
                 own = keep.tile([P, 2, PAIR], F32, name="own0", tag="own0", align_bytes=64)
             elif k == UNITS:
-                own = placed.tile([P, 4 * CHUNKS, PAIR], F32, name="own4", offset=28672, align_bytes=64)
+                own = placed.tile([P, 16, PAIR], F32, name="own4", offset=26624, align_bytes=64)
             else:
                 own = ring.tile([P, 2, PAIR], F32, name="own")
             msg = ring.tile([P, 2, PAIR], F32, name="msg")
             ms = psum.tile([P, 2, PAIR], F32, name="ms")
             banks = []
-            for b in range(2):
-                block = 2 * q + b
-                zo = psum.tile([P, 2, PAIR], F32, name="zo", bufs=4)
-                both = zo[:].rearrange("p w c -> p (w c)")
-                mm8(both, u, block, 0, True, False)
-                mm4(zo[:, 0, :], 0, u, block, 0, False, False)
-                mm4(zo[:, 0, :], 0, u, block, 1, False, False)
-                mm8(both, u, block, 1, False, True)
-                mm4(ms[:, b, :], 1, u, block, 0, True, False)
-                mm4(ms[:, b, :], 1, u, block, 1, False, True)
+            if k < EARLY:
+                za = psum.tile([P, 2, PAIR], F32, name="zo", bufs=4)
+                for b in range(2):
+                    block = 2 * q + b
+                    mm4(za[:, b, :], 0, u, block, 0, True, False)
+                    mm4(za[:, b, :], 0, u, block, 1, False, False)
+                    mm8_narrow(za[:, b, :], 0, block, False, True)
+                    mm4(ms[:, b, :], 1, u, block, 0, True, False)
+                    mm4(ms[:, b, :], 1, u, block, 1, False, True)
                 nc.scalar.activation(
-                    eta[:, b, :].rearrange("p (e m) -> p e m", e=2), zo[:, 0, :].rearrange("p (m e) -> p e m", e=2), ACT.Sigmoid
+                    eta[:].rearrange("p b (e m) -> p b e m", e=2), za[:].rearrange("p b (m e) -> p b e m", e=2), ACT.Sigmoid
                 )
-                banks.append(zo)
+            else:
+                for b in range(2):
+                    block = 2 * q + b
+                    zo = psum.tile([P, 2, PAIR], F32, name="zo", bufs=4)
+                    both = zo[:].rearrange("p w c -> p (w c)")
+                    mm8(both, u, block, 0, True, False)
+                    mm4(zo[:, 0, :], 0, u, block, 0, False, False)
+                    mm4(zo[:, 0, :], 0, u, block, 1, False, False)
+                    mm8(both, u, block, 1, False, True)
+                    mm4(ms[:, b, :], 1, u, block, 0, True, False)
+                    mm4(ms[:, b, :], 1, u, block, 1, False, True)
+                    nc.scalar.activation(
+                        eta[:, b, :].rearrange("p (e m) -> p e m", e=2), zo[:, 0, :].rearrange("p (m e) -> p e m", e=2), ACT.Sigmoid
+                    )
+                    banks.append(zo)
             for b, zo in enumerate(banks):
                 nc.scalar.copy(own[:, b, :].rearrange("p (e m) -> p e m", e=2), zo[:, 1, :].rearrange("p (m e) -> p e m", e=2))
             nc.vector.tensor_tensor(
@@ -241,6 +263,13 @@ def tile_list_rgg_ownreluP_kernel(
 
         def turn_and_add(k):
             u, q = divmod(k, UNITS)
+            if k < EARLY:
+                ow = psum.tile([P, 2, PAIR], F32, name="zo", bufs=4)
+                for b in range(2):
+                    mm8_narrow(ow[:, b, :], 1, 2 * q + b, True, True)
+                nc.scalar.copy(
+                    summands[k][0][:].rearrange("p b (e m) -> p b e m", e=2), ow[:].rearrange("p b (m e) -> p b e m", e=2)
+                )
             total = psum.tile([P, 2, UNIT], F32, name="total")
             for e in range(2):
                 for b in range(2):
@@ -261,33 +290,26 @@ def tile_list_rgg_ownreluP_kernel(
                 nc.sync.dma_start(out_rows[i], pages[i][:])
 
         def round_plane(i):
-            u, e = divmod(i, 2)
             for c in range(CHUNKS):
-                if u == 1 and c == 0:
-                    nc.vector.tensor_copy(staged[c][:, u, :, e], pages[i][:, CHUNK * c : CHUNK * (c + 1)])
+                cols = slice(STARTS[c], STARTS[c] + WIDTHS[c])
+                if i == PACK - 1 and c == 0:
+                    nc.vector.tensor_copy(staged[c][:, i, :], pages[i][:, cols])
                 else:
-                    nc.scalar.copy(staged[c][:, u, :, e], pages[i][:, CHUNK * c : CHUNK * (c + 1)])
+                    nc.scalar.copy(staged[c][:, i, :], pages[i][:, cols])
 
         products(0)
-        parted = keep.tile([P, PASSES, 2 * HALF], U8, name="picked1_0", tag="eta0", align_bytes=64)
-        part_words(parted[:], late_pairs[0][:], "p (s a) -> p a s")
-        picked[(0, 1)] = parted[:]
         for k in range(2 * UNITS):
             u, q = divmod(k, UNITS)
             if k == UNITS + 1:
                 round_plane(0)
             if k + 1 < 2 * UNITS:
                 products(k + 1)
-            if k == 0:
-                pages.append(keep.tile([P, T], F32, name="page2", tag="eta1", align_bytes=64))
-                nc.vector.memset(pages[2][:].bitcast(I32), 0)
-                pages.append(pages[0])
             turn_and_add(k)
             if k == 0:
-                round_last(keep.tile([P, PAIR * PACK], BF16, name="last_second", tag="own0", align_bytes=64), 1)
+                round_last(keep.tile([P, PAIR * PACK], BF16, name="last_second", tag="own0", align_bytes=64)[:], 1)
             if k == UNITS:
                 for c in range(CHUNKS):
-                    staged.append(placed.tile([P, 2, CHUNK, 2], BF16, name="staged%d" % c, offset=28672 + 8 * CHUNK * c, align_bytes=64))
+                    staged.append(placed.tile([P, PACK, WIDTHS[c]], BF16, name="staged%d" % c, offset=26624 + 8 * STARTS[c], align_bytes=64))
             place(2 * u, q, q + 1)
             if u == 0 and q < 2:
                 place(1, q, q + 1)
@@ -298,20 +320,21 @@ def tile_list_rgg_ownreluP_kernel(
 
         y_sc = keep.tile([P, T], U8, name="y_sc", align_bytes=64)
         words_out = out_1[0].rearrange("p t b -> p (t b)").bitcast(I32)
-        woven = [keep.tile([P, CHUNK * PACK], BF16, name="woven%d" % c, align_bytes=64) for c in range(CHUNKS)]
-        y_codes = [keep.tile([P, CHUNK], I32, name="y_codes%d" % c, align_bytes=64) for c in range(CHUNKS)]
+        woven = [keep.tile([P, WIDTHS[c] * PACK], BF16, name="woven%d" % c, align_bytes=64) for c in range(CHUNKS)]
+        y_codes = [keep.tile([P, WIDTHS[c]], I32, name="y_codes%d" % c, align_bytes=64) for c in range(CHUNKS)]
 
         def weave(c):
-            dst = woven[c][:].bitcast(U32).rearrange("p (c e u) -> p c u e", e=4, u=2)
-            src = staged[c][:].rearrange("p u c i -> p u (c i)").bitcast(U32).rearrange("p u (c e) -> p c u e", e=4)
-            if c >= CHUNKS - SCALAR_CHUNKS:
+            dst = woven[c][:].rearrange("p (g e i) -> p g i e", e=4, i=PACK)
+            src = staged[c][:].rearrange("p i (g e) -> p g i e", e=4)
+            if c >= VECTOR_CHUNKS:
                 nc.scalar.copy(dst, src)
             else:
-                nc.vector.tensor_copy(dst.bitcast(I32), src.bitcast(I32))
+                nc.vector.tensor_copy(dst, src)
 
         def quantize_chunk(c):
-            nc.vector.quantize_mx(out=y_codes[c][:].bitcast(FP8X4), scales=y_sc[:, CHUNK * c : CHUNK * (c + 1)], in_=woven[c][:])
-            nc.sync.dma_start(words_out[:, CHUNK * c : CHUNK * (c + 1)], y_codes[c][:])
+            cols = slice(STARTS[c], STARTS[c] + WIDTHS[c])
+            nc.vector.quantize_mx(out=y_codes[c][:].bitcast(FP8X4), scales=y_sc[:, cols], in_=woven[c][:])
+            nc.sync.dma_start(words_out[:, cols], y_codes[c][:])
 
         weave(0)
         for c in range(CHUNKS):

@@ -47,7 +47,6 @@ def tile_list_rgg_ownreluP_kernel(
         table_sc = placed.tile([P, T], U8, name="table_sc", offset=3072, align_bytes=64)
         picked_sc = keep.tile([P, PASSES, 2 * J], U8, name="picked_sc", align_bytes=64)
         w4_raw = keep.tile([P, 2 * PASSES, 2 * N], U8, name="w4_raw", align_bytes=64)
-        w4 = keep.tile([P, 2 * PASSES, 2 * N], U8, name="w4", align_bytes=64)
         w4_sc_raw = keep.tile([P, 2 * PASSES, N], U8, name="w4_sc_raw", align_bytes=64)
         picked_rows = keep.tile([P, 2 * J], U8, name="picked_rows", tag="picked_rows", align_bytes=64)
         ident = keep.tile([P, P], F32, name="ident", align_bytes=64)
@@ -82,10 +81,11 @@ def tile_list_rgg_ownreluP_kernel(
             nc.scalar.dma_start(w4_sc_raw[r:128:32].bitcast(I32), w4_sc_raw[8 * r : 128 : 32].bitcast(I32))
 
         for q in range(QUADS):
-            nc.vector.memset(table_sc[32 * q : 32 * q + 24, :].bitcast(I32), 0)
-        pages = [keep.tile([P, T], F32, name="page0", align_bytes=64)]
-        nc.vector.memset(pages[0][:].bitcast(I32), 0)
-        nc.vector.memset(picked_sc[96:128].bitcast(I32), 0)
+            nc.gpsimd.memset(table_sc[32 * q : 32 * q + 24, :].bitcast(I32), 0)
+        nc.gpsimd.memset(picked_sc[96:128].bitcast(I32), 0)
+        pages = [keep.tile([P, T], F32, name="page%d" % i, align_bytes=64) for i in range(2)]
+        for page in pages:
+            nc.gpsimd.memset(page[:].bitcast(I32), 0)
         make_identity(nc, ident[:])
 
         for l in range(2):
@@ -149,6 +149,7 @@ def tile_list_rgg_ownreluP_kernel(
         for l in range(2):
             picked[(l, 0)] = picked0[:, l]
         w4_sc = placed.tile([P, 2 * PASSES, N], U8, name="w4_sc", offset=8192, align_bytes=64)
+        w4 = placed.tile([P, 2 * PASSES, 2 * N], U8, name="w4", offset=10240, align_bytes=64)
         nc.vector.tensor_copy(
             w4[:].bitcast(I32).rearrange("p v (u m) -> p v u m", u=2),
             w4_raw[:].bitcast(I32).rearrange("p v (m u) -> p v u m", u=2),
@@ -160,17 +161,16 @@ def tile_list_rgg_ownreluP_kernel(
         round_both_pairs(0, 0)
         round_both_pairs(0, 1)
         round_both_pairs(1, 0)
-        round_last(placed.tile([P, 2112], BF16, name="last_first", offset=57344, align_bytes=64)[:, 0 : PAIR * PACK], 0)
+        round_last(keep.tile([P, PAIR * PACK], BF16, name="last_first", tag="last_first", align_bytes=64)[:], 0)
         pairs1 = placed.tile([P, 2, HALF], U32, name="pairs1", offset=45056 - 2048, align_bytes=64)
         for l in (1, 0):
             pick_words(l, 1, pairs1[:, l, :])
-        picked1 = placed.tile([P, 2, PASSES, 2 * HALF], U8, name="picked1", offset=57344 + 64, align_bytes=64)
+        picked1 = keep.tile([P, 2, PASSES, 2 * HALF], U8, name="picked1", tag="last_first", align_bytes=64)
         part_words(picked1[:], pairs1[:], "p l (s a) -> p l a s")
         for l in range(2):
             picked[(l, 1)] = picked1[:, l]
-        for i, offset in ((1, 57344 + 64 - 8192), (2, 57344 + 4160)):
-            pages.append(placed.tile([P, T], F32, name="page%d" % i, offset=offset, align_bytes=64))
-            nc.vector.memset(pages[i][:].bitcast(I32), 0)
+        pages.append(placed.tile([P, T], F32, name="page2", offset=47104, align_bytes=64))
+        nc.gpsimd.memset(pages[2][:].bitcast(I32), 0)
         pages.append(pages[0])
 
         def mm(out, l, block, a, rhs, rhs_scale, start, stop):
@@ -263,22 +263,28 @@ def tile_list_rgg_ownreluP_kernel(
 
         def turn_and_add(k):
             u, q = divmod(k, UNITS)
+            own, msg = summands[k]
+            edges = slice(UNIT * q, UNIT * (q + 1))
+            steps = [(0, 1), (1, 2)] if k == 0 else [(0, 2)]
             if k < EARLY:
                 ow = psum.tile([P, 2, PAIR], F32, name="zo", bufs=4)
                 for b in range(2):
                     mm8_narrow(ow[:, b, :], 1, 2 * q + b, True, True)
-                nc.scalar.copy(
-                    summands[k][0][:].rearrange("p b (e m) -> p b e m", e=2), ow[:].rearrange("p b (m e) -> p b e m", e=2)
-                )
-            total = psum.tile([P, 2, UNIT], F32, name="total")
-            for e in range(2):
-                for b in range(2):
-                    for s, summand in enumerate(summands[k]):
-                        nc.tensor.matmul(
-                            total[:, e, P * b : P * (b + 1)], summand[:, b, P * e : P * (e + 1)], ident[:],
-                            start=s == 0, stop=s == 1, is_transpose=True,
-                        )
-            nc.scalar.activation(results[u][:, :, UNIT * q : UNIT * (q + 1)], total[:], ACT.Relu)
+                for first, last in steps:
+                    nc.scalar.copy(
+                        own[:].rearrange("p b (e m) -> p b e m", e=2)[:, :, first:last],
+                        ow[:].rearrange("p b (m e) -> p b e m", e=2)[:, :, first:last],
+                    )
+            for first, last in steps:
+                total = psum.tile([P, 2, UNIT], F32, name="total")
+                for e in range(first, last):
+                    for b in range(2):
+                        for s, summand in enumerate((own, msg)):
+                            nc.tensor.matmul(
+                                total[:, e, P * b : P * (b + 1)], summand[:, b, P * e : P * (e + 1)], ident[:],
+                                start=s == 0, stop=s == 1, is_transpose=True,
+                            )
+                nc.scalar.activation(results[u][:, first:last, edges], total[:, first:last, :], ACT.Relu)
 
         def place(i, first, last):
             u, e = divmod(i, 2)

@@ -19,17 +19,33 @@ ALU = mybir.AluOpType
 
 P = 128
 PACK = 4
-PASSES = 2
-HALF = 512
+PASSES = K // (P * PACK)
 QUADS = 4
-PAIR = 256
-UNIT = 256
+PARKED = 24
+HALF = J // 2
+PAIR = N // 2
+UNIT = 2 * P
 UNITS = J // UNIT
-WIDTHS = (512, 512, 256, 512, 256)
+EARLY = 2
+SRC, DST = 0, 1
+WA, WO = 0, 1
+WB, WC = 0, 1
+
+WIDTHS = (256, 512, 512, 512, 256)
 STARTS = [sum(WIDTHS[:c]) for c in range(len(WIDTHS))]
 CHUNKS = len(WIDTHS)
 VECTOR_CHUNKS = 3
-EARLY = 2
+
+KIB = 1024
+LAST_RAW_AT = (0, 4 * KIB)
+TABLE_SC_AT = 3 * KIB
+PAIRS0_AT = 8 * KIB
+W4_SC_AT = 8 * KIB
+W4_AT = 10 * KIB
+STAGED_AT = 26 * KIB
+PAIRS1_AT = 42 * KIB
+ROUNDED_WA1_AT = 44 * KIB
+PAGE2_AT = 46 * KIB
 
 
 def tile_list_rgg_ownreluP_kernel(
@@ -43,18 +59,20 @@ def tile_list_rgg_ownreluP_kernel(
         placed = ctx.enter_context(tc.tile_pool(name="placed", bufs=1))
 
         lists = [keep.tile([P, J // 16], U16, name="src_list"), keep.tile([P, J // 16], U16, name="dst_list")]
-        table = keep.tile([P, T], I32, name="table", tag="table", align_bytes=64)
-        table_sc = placed.tile([P, T], U8, name="table_sc", offset=3072, align_bytes=64)
+        table = keep.tile([P, T], I32, name="table", align_bytes=64)
+        table_sc = placed.tile([P, T], U8, name="table_sc", offset=TABLE_SC_AT, align_bytes=64)
         picked_sc = keep.tile([P, PASSES, 2 * J], U8, name="picked_sc", align_bytes=64)
         w4_raw = keep.tile([P, 2 * PASSES, 2 * N], U8, name="w4_raw", align_bytes=64)
         w4_sc_raw = keep.tile([P, 2 * PASSES, N], U8, name="w4_sc_raw", align_bytes=64)
         picked_rows = keep.tile([P, 2 * J], U8, name="picked_rows", tag="picked_rows", align_bytes=64)
         ident = keep.tile([P, P], F32, name="ident", align_bytes=64)
 
-        nc.sync.dma_start(lists[0][:], offs)
-        nc.sync.dma_start(lists[1][:], offs2)
+        nc.sync.dma_start(lists[SRC][:], offs)
+        nc.sync.dma_start(lists[DST][:], offs2)
         for q in range(QUADS):
-            nc.sync.dma_start(table_sc[32 * q + 24 : 32 * q + 32, :].bitcast(I32), tab_scales[:, 4 * q : 4 * q + 4, :].bitcast(I32))
+            nc.sync.dma_start(
+                table_sc[32 * q + PARKED : 32 * (q + 1), :].bitcast(I32), tab_scales[:, 4 * q : 4 * q + 4, :].bitcast(I32)
+            )
 
         raws = {}
 
@@ -63,38 +81,43 @@ def tile_list_rgg_ownreluP_kernel(
             nc.sync.dma_start(raw[:], (wa, wo)[w][512 * a : 512 * (a + 1), :].rearrange("(p j) n -> p j n", j=PACK))
             raws[(w, a)] = raw
 
-        load_weight(0, 0)
+        load_weight(WA, 0)
         nc.sync.dma_start(table[:], tab_words[0].rearrange("p t b -> p (t b)").bitcast(I32))
         nc.gpsimd.memset(w4_sc_raw[:].bitcast(I32), 0)
         for w, scales in enumerate((wb_scales, wc_scales)):
-            nc.sync.dma_start(w4_sc_raw[0:128:8, 2 * w : 2 * w + 2, :].bitcast(I32), scales.rearrange("a s n -> s a n").bitcast(I32))
-        for v, words in enumerate((wb_words, wc_words)):
-            nc.sync.dma_start(w4_raw[:, 2 * v : 2 * v + 2, :].bitcast(I32), words.rearrange("a p c -> p a c").bitcast(I32))
-        load_weight(0, 1)
-        load_weight(1, 0)
+            nc.sync.dma_start(
+                w4_sc_raw[0:P:8, PASSES * w : PASSES * (w + 1), :].bitcast(I32), scales.rearrange("a s n -> s a n").bitcast(I32)
+            )
+        for w, words in enumerate((wb_words, wc_words)):
+            nc.sync.dma_start(
+                w4_raw[:, PASSES * w : PASSES * (w + 1), :].bitcast(I32), words.rearrange("a p c -> p a c").bitcast(I32)
+            )
+        load_weight(WA, 1)
+        load_weight(WO, 0)
 
         warm = keep.tile([P, 2], F32, name="warm")
         nc.vector.memset(warm[:, 0:1], 0.0)
         nc.scalar.activation(warm[:, 1:2], warm[:, 0:1], ACT.Sigmoid)
 
         for r in range(1, 4):
-            nc.scalar.dma_start(w4_sc_raw[r:128:32].bitcast(I32), w4_sc_raw[8 * r : 128 : 32].bitcast(I32))
+            nc.scalar.dma_start(w4_sc_raw[r:P:32].bitcast(I32), w4_sc_raw[8 * r : P : 32].bitcast(I32))
 
         for q in range(QUADS):
-            nc.gpsimd.memset(table_sc[32 * q : 32 * q + 24, :].bitcast(I32), 0)
-        nc.gpsimd.memset(picked_sc[96:128].bitcast(I32), 0)
+            nc.gpsimd.memset(table_sc[32 * q : 32 * q + PARKED, :].bitcast(I32), 0)
+        nc.gpsimd.memset(picked_sc[96:P].bitcast(I32), 0)
         pages = [keep.tile([P, T], F32, name="page%d" % i, align_bytes=64) for i in range(2)]
         for page in pages:
             nc.gpsimd.memset(page[:].bitcast(I32), 0)
         make_identity(nc, ident[:])
 
-        for l in range(2):
+        for l in (SRC, DST):
             nc.vector.tensor_copy(picked_rows[:, J * l : J * (l + 1)], table_sc[:].indirect(lists[l][:]))
         for a in range(PASSES):
-            nc.sync.dma_start(picked_sc[0:100, a, :].bitcast(I32), picked_rows[24 + 4 * a : 124 + 4 * a, :].bitcast(I32))
+            shift = PARKED + 4 * a
+            nc.sync.dma_start(picked_sc[0:100, a, :].bitcast(I32), picked_rows[shift : shift + 100, :].bitcast(I32))
         last_raw = []
         for half in range(2):
-            raw = placed.tile([P, PACK, N // 2], F32, name="last_raw%d" % half, offset=4096 * half, align_bytes=64)
+            raw = placed.tile([P, PACK, N // 2], F32, name="last_raw%d" % half, offset=LAST_RAW_AT[half], align_bytes=64)
             nc.sync.dma_start(raw[:], wo[512:1024, 256 * half : 256 * (half + 1)].rearrange("(p j) n -> p j n", j=PACK))
             last_raw.append(raw)
         gate = keep.tile([P, J], F32, name="gate", tag="picked_rows", align_bytes=64)
@@ -102,11 +125,11 @@ def tile_list_rgg_ownreluP_kernel(
 
         picked = {}
 
-        def pick_words(l, h, pairs):
-            nc.vector.tensor_copy(pairs, table[:].bitcast(U32).indirect(lists[l][:, 32 * h : 32 * (h + 1)]))
-
-        def part_words(parted, pairs, pattern):
-            nc.vector.tensor_copy(parted.bitcast(U16), pairs.bitcast(U16).rearrange(pattern, a=PASSES))
+        def pick_words(h, pairs, parted):
+            for l in (DST, SRC):
+                nc.vector.tensor_copy(pairs[:, l, :], table[:].bitcast(U32).indirect(lists[l][:, 32 * h : 32 * (h + 1)]))
+            nc.vector.tensor_copy(parted[:].bitcast(U16), pairs[:].bitcast(U16).rearrange("p l (s a) -> p l a s", a=PASSES))
+            picked[h] = parted
 
         w8 = {}
         for u in range(2):
@@ -116,40 +139,34 @@ def tile_list_rgg_ownreluP_kernel(
                     keep.tile([P, 2 * PAIR], U8, name="scales%d_%d" % (u, a), align_bytes=64),
                 )
 
-        def quantize_weight(grouped, u, w, a):
+        def quantize_columns(rounded, u, a, first, last):
             codes, scales = w8[(u, a)]
-            cols = slice(PAIR * w, PAIR * (w + 1))
-            nc.vector.quantize_mx(out=codes[:, cols].bitcast(FP8X4), scales=scales[:, cols], in_=grouped)
+            nc.vector.quantize_mx(out=codes[:, first:last].bitcast(FP8X4), scales=scales[:, first:last], in_=rounded)
 
-        def round_both_pairs(w, a):
-            if (w, a) == (0, 1):
-                grouped = placed.tile([P, 2, PAIR * PACK], BF16, name="grouped0_1", offset=45056, align_bytes=64)
-            else:
-                grouped = keep.tile([P, 2, PAIR * PACK], BF16, name="grouped%d_%d" % (w, a), align_bytes=64)
+        def round_weight(w, a, rounded):
             nc.scalar.copy(
-                grouped[:].rearrange("p u (m e j) -> p m j u e", e=2, j=PACK),
+                rounded[:].rearrange("p u (m e j) -> p m j u e", e=2, j=PACK),
                 raws[(w, a)][:].rearrange("p j (m u e) -> p m j u e", u=2, e=2),
             )
             for u in range(2):
-                quantize_weight(grouped[:, u, :], u, w, a)
+                quantize_columns(rounded[:, u, :], u, a, PAIR * w, PAIR * (w + 1))
 
-        def round_last(grouped, u):
+        def round_last_weight(u, rounded):
             for half in range(2):
+                part = rounded[:, P * PACK * half : P * PACK * (half + 1)]
                 nc.scalar.copy(
-                    grouped[:, 512 * half : 512 * (half + 1)].rearrange("p (m e j) -> p m j e", e=2, j=PACK),
+                    part.rearrange("p (m e j) -> p m j e", e=2, j=PACK),
                     last_raw[half][:].rearrange("p j (m u e) -> p u m j e", u=2, e=2)[:, u],
                 )
-            quantize_weight(grouped, u, 1, 1)
+                quantize_columns(part, u, 1, PAIR + P * half, PAIR + P * (half + 1))
 
-        pairs0 = placed.tile([P, 2, HALF], U32, name="pairs0", offset=8192, align_bytes=64)
-        for l in (1, 0):
-            pick_words(l, 0, pairs0[:, l, :])
-        picked0 = keep.tile([P, 2, PASSES, 2 * HALF], U8, name="picked0", align_bytes=64)
-        part_words(picked0[:], pairs0[:], "p l (s a) -> p l a s")
-        for l in range(2):
-            picked[(l, 0)] = picked0[:, l]
-        w4_sc = placed.tile([P, 2 * PASSES, N], U8, name="w4_sc", offset=8192, align_bytes=64)
-        w4 = placed.tile([P, 2 * PASSES, 2 * N], U8, name="w4", offset=10240, align_bytes=64)
+        pick_words(
+            0,
+            placed.tile([P, 2, HALF], U32, name="pairs0", offset=PAIRS0_AT, align_bytes=64),
+            keep.tile([P, 2, PASSES, 2 * HALF], U8, name="picked0", align_bytes=64),
+        )
+        w4_sc = placed.tile([P, 2 * PASSES, N], U8, name="w4_sc", offset=W4_SC_AT, align_bytes=64)
+        w4 = placed.tile([P, 2 * PASSES, 2 * N], U8, name="w4", offset=W4_AT, align_bytes=64)
         nc.vector.tensor_copy(
             w4[:].bitcast(I32).rearrange("p v (u m) -> p v u m", u=2),
             w4_raw[:].bitcast(I32).rearrange("p v (m u) -> p v u m", u=2),
@@ -158,26 +175,24 @@ def tile_list_rgg_ownreluP_kernel(
             w4_sc[:].bitcast(U16).rearrange("p v (u m) -> p v u m", u=2),
             w4_sc_raw[:].bitcast(U16).rearrange("p v (m u) -> p v u m", u=2),
         )
-        round_both_pairs(0, 0)
-        round_both_pairs(0, 1)
-        round_both_pairs(1, 0)
-        round_last(keep.tile([P, PAIR * PACK], BF16, name="last_first", tag="last_first", align_bytes=64)[:], 0)
-        pairs1 = placed.tile([P, 2, HALF], U32, name="pairs1", offset=45056 - 2048, align_bytes=64)
-        for l in (1, 0):
-            pick_words(l, 1, pairs1[:, l, :])
-        picked1 = keep.tile([P, 2, PASSES, 2 * HALF], U8, name="picked1", tag="last_first", align_bytes=64)
-        part_words(picked1[:], pairs1[:], "p l (s a) -> p l a s")
-        for l in range(2):
-            picked[(l, 1)] = picked1[:, l]
-        pages.append(placed.tile([P, T], F32, name="page2", offset=47104, align_bytes=64))
+        round_weight(WA, 0, keep.tile([P, 2, PAIR * PACK], BF16, name="rounded_wa0", align_bytes=64))
+        round_weight(WA, 1, placed.tile([P, 2, PAIR * PACK], BF16, name="rounded_wa1", offset=ROUNDED_WA1_AT, align_bytes=64))
+        round_weight(WO, 0, keep.tile([P, 2, PAIR * PACK], BF16, name="rounded_wo0", align_bytes=64))
+        round_last_weight(0, keep.tile([P, PAIR * PACK], BF16, name="rounded_wo1_pair0", tag="wo1_pair0", align_bytes=64))
+        pick_words(
+            1,
+            placed.tile([P, 2, HALF], U32, name="pairs1", offset=PAIRS1_AT, align_bytes=64),
+            keep.tile([P, 2, PASSES, 2 * HALF], U8, name="picked1", tag="wo1_pair0", align_bytes=64),
+        )
+        pages.append(placed.tile([P, T], F32, name="page2", offset=PAGE2_AT, align_bytes=64))
         nc.gpsimd.memset(pages[2][:].bitcast(I32), 0)
         pages.append(pages[0])
 
         def mm(out, l, block, a, rhs, rhs_scale, start, stop):
-            h, b = divmod(block, 4)
+            h, b = divmod(block, HALF // P)
             nc.tensor.matmul_mx(
                 out=out,
-                lhsT=picked[(l, h)][:, a, 2 * P * b : 2 * P * (b + 1)].bitcast(FP4X4),
+                lhsT=picked[h][:, l, a, 2 * P * b : 2 * P * (b + 1)].bitcast(FP4X4),
                 lhsT_scale=picked_sc[:, a, J * l + P * block : J * l + P * (block + 1)],
                 rhs=rhs,
                 rhs_scale=rhs_scale,
@@ -185,96 +200,96 @@ def tile_list_rgg_ownreluP_kernel(
                 stop=stop,
             )
 
-        def mm4(out, w, u, block, a, start, stop):
-            mm(
-                out, 0, block, a,
-                w4[:, 2 * w + a, 2 * PAIR * u : 2 * PAIR * (u + 1)].bitcast(FP4X4),
-                w4_sc[:, 2 * w + a, PAIR * u : PAIR * (u + 1)],
-                start, stop,
-            )
+        def mm_packed(out, w, u, block, start, stop):
+            for a in range(PASSES):
+                mm(
+                    out, SRC, block, a,
+                    w4[:, PASSES * w + a, 2 * PAIR * u : 2 * PAIR * (u + 1)].bitcast(FP4X4),
+                    w4_sc[:, PASSES * w + a, PAIR * u : PAIR * (u + 1)],
+                    start and a == 0, stop and a == PASSES - 1,
+                )
 
-        def mm8(out, u, block, a, start, stop):
+        def mm_wide(out, u, block, a, start, stop):
             codes, scales = w8[(u, a)]
-            mm(out, 1, block, a, codes[:].bitcast(FP8X4), scales[:], start, stop)
+            mm(out, DST, block, a, codes[:].bitcast(FP8X4), scales[:], start, stop)
 
-        def mm8_narrow(out, w, block, start, stop):
+        def mm_narrow(out, w, block, start, stop):
             for a in range(PASSES):
                 codes, scales = w8[(0, a)]
                 for c in range(2):
                     cols = slice(PAIR * w + P * c, PAIR * w + P * (c + 1))
                     mm(
-                        out[:, P * c : P * (c + 1)], 1, block, a, codes[:, cols].bitcast(FP8X4), scales[:, cols],
+                        out[:, P * c : P * (c + 1)], DST, block, a, codes[:, cols].bitcast(FP8X4), scales[:, cols],
                         start and a == 0 and c == 0, stop and a == PASSES - 1 and c == 1,
                     )
+
+        def from_bank(ap):
+            return ap.rearrange("p (m e) -> p e m", e=2)
+
+        def by_plane(ap):
+            return ap.rearrange("p (e m) -> p e m", e=2)
+
+        def from_bank_blocks(ap):
+            return ap.rearrange("p b (m e) -> p b e m", e=2)
+
+        def by_plane_blocks(ap):
+            return ap.rearrange("p b (e m) -> p b e m", e=2)
 
         summands = {}
         results = [keep.tile([P, 2, J], F32, name="result%d" % u, align_bytes=64) for u in range(2)]
         staged = []
         out_rows = out_0.rearrange("(p i) t -> i p t", i=PACK)
 
-        def products(k):
-            u, q = divmod(k, UNITS)
+        def products(unit):
+            u, q = divmod(unit, UNITS)
             eta = ring.tile([P, 2, PAIR], F32, name="eta")
-            if k == 0:
-                own = keep.tile([P, 2, PAIR], F32, name="own0", tag="own0", align_bytes=64)
-            elif k == UNITS:
-                own = placed.tile([P, 16, PAIR], F32, name="own4", offset=26624, align_bytes=64)
+            if unit == 0:
+                own = keep.tile([P, 2, PAIR], F32, name="own_first", tag="own_first", align_bytes=64)
+            elif unit == UNITS:
+                own = placed.tile([P, T * PACK * 2 // (PAIR * 4), PAIR], F32, name="own_pair1", offset=STAGED_AT, align_bytes=64)
             else:
                 own = ring.tile([P, 2, PAIR], F32, name="own")
             msg = ring.tile([P, 2, PAIR], F32, name="msg")
             ms = psum.tile([P, 2, PAIR], F32, name="ms")
-            banks = []
-            if k < EARLY:
+            if unit < EARLY:
                 za = psum.tile([P, 2, PAIR], F32, name="zo", bufs=4)
                 for b in range(2):
                     block = 2 * q + b
-                    mm4(za[:, b, :], 0, u, block, 0, True, False)
-                    mm4(za[:, b, :], 0, u, block, 1, False, False)
-                    mm8_narrow(za[:, b, :], 0, block, False, True)
-                    mm4(ms[:, b, :], 1, u, block, 0, True, False)
-                    mm4(ms[:, b, :], 1, u, block, 1, False, True)
-                nc.scalar.activation(
-                    eta[:].rearrange("p b (e m) -> p b e m", e=2), za[:].rearrange("p b (m e) -> p b e m", e=2), ACT.Sigmoid
-                )
+                    mm_packed(za[:, b, :], WB, u, block, True, False)
+                    mm_narrow(za[:, b, :], WA, block, False, True)
+                    mm_packed(ms[:, b, :], WC, u, block, True, True)
+                nc.scalar.activation(by_plane_blocks(eta[:]), from_bank_blocks(za[:]), ACT.Sigmoid)
             else:
+                banks = []
                 for b in range(2):
                     block = 2 * q + b
                     zo = psum.tile([P, 2, PAIR], F32, name="zo", bufs=4)
                     both = zo[:].rearrange("p w c -> p (w c)")
-                    mm8(both, u, block, 0, True, False)
-                    mm4(zo[:, 0, :], 0, u, block, 0, False, False)
-                    mm4(zo[:, 0, :], 0, u, block, 1, False, False)
-                    mm8(both, u, block, 1, False, True)
-                    mm4(ms[:, b, :], 1, u, block, 0, True, False)
-                    mm4(ms[:, b, :], 1, u, block, 1, False, True)
-                    nc.scalar.activation(
-                        eta[:, b, :].rearrange("p (e m) -> p e m", e=2), zo[:, 0, :].rearrange("p (m e) -> p e m", e=2), ACT.Sigmoid
-                    )
+                    mm_wide(both, u, block, 0, True, False)
+                    mm_packed(zo[:, WA, :], WB, u, block, False, False)
+                    mm_wide(both, u, block, 1, False, True)
+                    mm_packed(ms[:, b, :], WC, u, block, True, True)
+                    nc.scalar.activation(by_plane(eta[:, b, :]), from_bank(zo[:, WA, :]), ACT.Sigmoid)
                     banks.append(zo)
-            for b, zo in enumerate(banks):
-                nc.scalar.copy(own[:, b, :].rearrange("p (e m) -> p e m", e=2), zo[:, 1, :].rearrange("p (m e) -> p e m", e=2))
-            nc.vector.tensor_tensor(
-                msg[:].rearrange("p b (e m) -> p b e m", e=2),
-                ms[:].rearrange("p b (m e) -> p b e m", e=2),
-                eta[:].rearrange("p b (e m) -> p b e m", e=2),
-                ALU.mult,
-            )
-            summands[k] = (own, msg)
+                for b, zo in enumerate(banks):
+                    nc.scalar.copy(by_plane(own[:, b, :]), from_bank(zo[:, WO, :]))
+            nc.vector.tensor_tensor(by_plane_blocks(msg[:]), from_bank_blocks(ms[:]), by_plane_blocks(eta[:]), ALU.mult)
+            summands[unit] = (own, msg)
 
-        def turn_and_add(k):
-            u, q = divmod(k, UNITS)
-            own, msg = summands[k]
+        def turn_and_add(unit):
+            u, q = divmod(unit, UNITS)
+            own, msg = summands[unit]
             edges = slice(UNIT * q, UNIT * (q + 1))
-            steps = [(0, 1), (1, 2)] if k == 0 else [(0, 2)]
-            if k < EARLY:
-                ow = psum.tile([P, 2, PAIR], F32, name="zo", bufs=4)
+            steps = [(0, 1), (1, 2)] if unit == 0 else [(0, 2)]
+            if unit < EARLY:
+                banks = []
                 for b in range(2):
-                    mm8_narrow(ow[:, b, :], 1, 2 * q + b, True, True)
+                    ow = psum.tile([P, 2, PAIR], F32, name="zo", bufs=4)
+                    mm_narrow(ow[:, 0, :], WO, 2 * q + b, True, True)
+                    banks.append(ow)
                 for first, last in steps:
-                    nc.scalar.copy(
-                        own[:].rearrange("p b (e m) -> p b e m", e=2)[:, :, first:last],
-                        ow[:].rearrange("p b (m e) -> p b e m", e=2)[:, :, first:last],
-                    )
+                    for b, ow in enumerate(banks):
+                        nc.scalar.copy(by_plane(own[:, b, :])[:, first:last], from_bank(ow[:, 0, :])[:, first:last])
             for first, last in steps:
                 total = psum.tile([P, 2, UNIT], F32, name="total")
                 for e in range(first, last):
@@ -290,34 +305,36 @@ def tile_list_rgg_ownreluP_kernel(
             u, e = divmod(i, 2)
             edges = slice(UNIT * first, UNIT * last)
             nc.vector.tensor_tensor(
-                pages[i][:].indirect(lists[1][:, 16 * first : 16 * last]), results[u][:, e, edges], gate[:, edges], ALU.mult
+                pages[i][:].indirect(lists[DST][:, 16 * first : 16 * last]), results[u][:, e, edges], gate[:, edges], ALU.mult
             )
             if last == UNITS:
                 nc.sync.dma_start(out_rows[i], pages[i][:])
 
         def round_plane(i):
+            u, e = divmod(i, 2)
             for c in range(CHUNKS):
                 cols = slice(STARTS[c], STARTS[c] + WIDTHS[c])
-                if i == PACK - 1 and c == 0:
-                    nc.vector.tensor_copy(staged[c][:, i, :], pages[i][:, cols])
+                if u == 1 and c == 0:
+                    nc.vector.tensor_copy(staged[c][:, u, :, e], pages[i][:, cols])
                 else:
-                    nc.scalar.copy(staged[c][:, i, :], pages[i][:, cols])
+                    nc.scalar.copy(staged[c][:, u, :, e], pages[i][:, cols])
 
         products(0)
-        for k in range(2 * UNITS):
-            u, q = divmod(k, UNITS)
-            if k == UNITS + 1:
+        for unit in range(2 * UNITS):
+            u, q = divmod(unit, UNITS)
+            if unit == UNITS + 1:
                 round_plane(0)
-            if k + 1 < 2 * UNITS:
-                products(k + 1)
-            turn_and_add(k)
-            if k == 0:
-                round_last(keep.tile([P, PAIR * PACK], BF16, name="last_second", tag="own0", align_bytes=64)[:], 1)
-            if k == UNITS:
+            if unit + 1 < 2 * UNITS:
+                products(unit + 1)
+            turn_and_add(unit)
+            if unit == 0:
+                round_last_weight(1, keep.tile([P, PAIR * PACK], BF16, name="rounded_wo1_pair1", tag="own_first", align_bytes=64))
+            if unit == UNITS:
                 for c in range(CHUNKS):
-                    staged.append(placed.tile([P, PACK, WIDTHS[c]], BF16, name="staged%d" % c, offset=26624 + 8 * STARTS[c], align_bytes=64))
+                    at = STAGED_AT + PACK * 2 * STARTS[c]
+                    staged.append(placed.tile([P, 2, WIDTHS[c], 2], BF16, name="staged%d" % c, offset=at, align_bytes=64))
             place(2 * u, q, q + 1)
-            if u == 0 and q < 2:
+            if unit < EARLY:
                 place(1, q, q + 1)
             elif q % 2 == 1:
                 place(2 * u + 1, q - 1, q + 1)
@@ -330,12 +347,12 @@ def tile_list_rgg_ownreluP_kernel(
         y_codes = [keep.tile([P, WIDTHS[c]], I32, name="y_codes%d" % c, align_bytes=64) for c in range(CHUNKS)]
 
         def weave(c):
-            dst = woven[c][:].rearrange("p (g e i) -> p g i e", e=4, i=PACK)
-            src = staged[c][:].rearrange("p i (g e) -> p g i e", e=4)
+            dst = woven[c][:].bitcast(U32).rearrange("p (g s u) -> p g u s", s=4, u=2)
+            src = staged[c][:].rearrange("p u t e -> p u (t e)").bitcast(U32).rearrange("p u (g s) -> p g u s", s=4)
             if c >= VECTOR_CHUNKS:
                 nc.scalar.copy(dst, src)
             else:
-                nc.vector.tensor_copy(dst, src)
+                nc.vector.tensor_copy(dst.bitcast(I32), src.bitcast(I32))
 
         def quantize_chunk(c):
             cols = slice(STARTS[c], STARTS[c] + WIDTHS[c])

@@ -37,15 +37,21 @@ CHUNKS = len(WIDTHS)
 VECTOR_CHUNKS = 3
 
 KIB = 1024
-LAST_RAW_AT = (0, 4 * KIB)
-TABLE_SC_AT = 3 * KIB
 PAIRS0_AT = 8 * KIB
-W4_SC_AT = 8 * KIB
-W4_AT = 10 * KIB
-STAGED_AT = 26 * KIB
-PAIRS1_AT = 42 * KIB
-ROUNDED_WA1_AT = 44 * KIB
-PAGE2_AT = 46 * KIB
+PAGE1_AT = PAIRS0_AT + 64 - 8 * KIB
+ROWS1_AT = PAIRS0_AT + 64
+RAW_WO1_AT = (ROWS1_AT + KIB, ROWS1_AT + 5 * KIB)
+RAW_WO0_AT = ROWS1_AT + 9 * KIB
+ROUNDED_WA1_AT = 36 * KIB
+PAGE2_AT = ROUNDED_WA1_AT + 64 - 8 * KIB
+PAIRS1_DST_AT = ROUNDED_WA1_AT + 64
+GATE_AT = PAIRS1_DST_AT + 2 * KIB
+ROUNDED_WO1_AT = 48 * KIB
+PICKED1_AT = ROUNDED_WO1_AT + 64 - 4 * KIB
+MSG1_AT = ROUNDED_WO1_AT + 64
+STAGED_AT = 54 * KIB
+
+UNIT_LIST = [(0, 2, 2 * q, 2) for q in range(4)] + [(i, 1, 4 * h, 4) for i in (2, 3) for h in range(2)]
 
 
 def tile_list_rgg_ownreluP_kernel(
@@ -54,18 +60,21 @@ def tile_list_rgg_ownreluP_kernel(
     nc = tc.nc
     with ExitStack() as ctx:
         keep = ctx.enter_context(tc.tile_pool(name="keep", bufs=1))
-        ring = ctx.enter_context(tc.tile_pool(name="ring", bufs=3))
-        psum = ctx.enter_context(tc.psum_pool(name="psum", bufs=2))
+        ring = ctx.enter_context(tc.tile_pool(name="ring", bufs=2))
+        psum = ctx.enter_context(tc.psum_pool(name="psum", bufs=1))
         placed = ctx.enter_context(tc.tile_pool(name="placed", bufs=1))
 
         lists = [keep.tile([P, J // 16], U16, name="src_list"), keep.tile([P, J // 16], U16, name="dst_list")]
         table = keep.tile([P, T], I32, name="table", align_bytes=64)
-        table_sc = placed.tile([P, T], U8, name="table_sc", offset=TABLE_SC_AT, align_bytes=64)
-        picked_sc = keep.tile([P, PASSES, 2 * J], U8, name="picked_sc", align_bytes=64)
-        w4_raw = keep.tile([P, 2 * PASSES, 2 * N], U8, name="w4_raw", align_bytes=64)
-        w4_sc_raw = keep.tile([P, 2 * PASSES, N], U8, name="w4_sc_raw", align_bytes=64)
-        picked_rows = keep.tile([P, 2 * J], U8, name="picked_rows", tag="picked_rows", align_bytes=64)
+        table_sc = keep.tile([P, T], U8, name="table_sc", align_bytes=64)
+        picked_sc = [keep.tile([P, PASSES, 2 * HALF], U8, name="picked_sc%d" % h, align_bytes=64) for h in range(2)]
+        w4 = keep.tile([P, 2 * PASSES, 2 * N], U8, name="w4", align_bytes=64)
+        w4_sc = keep.tile([P, 2 * PASSES, N], U8, name="w4_sc", align_bytes=64)
         ident = keep.tile([P, P], F32, name="ident", align_bytes=64)
+
+        for q in range(QUADS):
+            nc.gpsimd.memset(table_sc[32 * q : 32 * q + PARKED, :].bitcast(I32), 0)
+        nc.gpsimd.memset(w4_sc[:].bitcast(I32), 0)
 
         nc.sync.dma_start(lists[SRC][:], offs)
         nc.sync.dma_start(lists[DST][:], offs2)
@@ -73,241 +82,239 @@ def tile_list_rgg_ownreluP_kernel(
             nc.sync.dma_start(
                 table_sc[32 * q + PARKED : 32 * (q + 1), :].bitcast(I32), tab_scales[:, 4 * q : 4 * q + 4, :].bitcast(I32)
             )
-
-        raws = {}
-
-        def load_weight(w, a):
-            raw = keep.tile([P, PACK, N], F32, name="raw%d_%d" % (w, a), align_bytes=64)
-            nc.sync.dma_start(raw[:], (wa, wo)[w][512 * a : 512 * (a + 1), :].rearrange("(p j) n -> p j n", j=PACK))
-            raws[(w, a)] = raw
-
-        load_weight(WA, 0)
         nc.sync.dma_start(table[:], tab_words[0].rearrange("p t b -> p (t b)").bitcast(I32))
-        nc.gpsimd.memset(w4_sc_raw[:].bitcast(I32), 0)
+
+        def load_first_pass(weight, raw):
+            nc.sync.dma_start(raw[:], weight[0:512, :].rearrange("(p j) n -> p j n", j=PACK))
+            return raw
+
+        def load_second_pass(weight, halves):
+            for c, raw in enumerate(halves):
+                nc.sync.dma_start(raw[:], weight[512:1024, PAIR * c : PAIR * (c + 1)].rearrange("(p j) n -> p j n", j=PACK))
+            return halves
+
+        def load_words(w):
+            nc.sync.dma_start(
+                w4[:, PASSES * w : PASSES * (w + 1), :].bitcast(I32),
+                (wb_words, wc_words)[w].rearrange("a p c -> p a c").bitcast(I32),
+            )
+
+        load_words(WC)
         for w, scales in enumerate((wb_scales, wc_scales)):
             nc.sync.dma_start(
-                w4_sc_raw[0:P:8, PASSES * w : PASSES * (w + 1), :].bitcast(I32), scales.rearrange("a s n -> s a n").bitcast(I32)
+                w4_sc[0:P:8, PASSES * w : PASSES * (w + 1), :].bitcast(I32), scales.rearrange("a s n -> s a n").bitcast(I32)
             )
-        for w, words in enumerate((wb_words, wc_words)):
-            nc.sync.dma_start(
-                w4_raw[:, PASSES * w : PASSES * (w + 1), :].bitcast(I32), words.rearrange("a p c -> p a c").bitcast(I32)
-            )
-        load_weight(WA, 1)
-        load_weight(WO, 0)
+        load_words(WB)
+        raw_wa0 = load_first_pass(wa, keep.tile([P, PACK, N], F32, name="raw_wa0", align_bytes=64))
+        raw_wa1 = load_second_pass(
+            wa, [keep.tile([P, PACK, PAIR], F32, name="raw_wa1_%d" % c, align_bytes=64) for c in range(2)]
+        )
 
         warm = keep.tile([P, 2], F32, name="warm")
         nc.vector.memset(warm[:, 0:1], 0.0)
         nc.scalar.activation(warm[:, 1:2], warm[:, 0:1], ACT.Sigmoid)
 
-        for r in range(1, 4):
-            nc.scalar.dma_start(w4_sc_raw[r:P:32].bitcast(I32), w4_sc_raw[8 * r : P : 32].bitcast(I32))
-
-        for q in range(QUADS):
-            nc.gpsimd.memset(table_sc[32 * q : 32 * q + PARKED, :].bitcast(I32), 0)
-        nc.gpsimd.memset(picked_sc[96:P].bitcast(I32), 0)
-        pages = [keep.tile([P, T], F32, name="page%d" % i, align_bytes=64) for i in range(2)]
-        for page in pages:
-            nc.gpsimd.memset(page[:].bitcast(I32), 0)
+        for h in range(2):
+            nc.gpsimd.memset(picked_sc[h][96:P].bitcast(I32), 0)
+        pages = [keep.tile([P, T], F32, name="page0", align_bytes=64)]
+        nc.gpsimd.memset(pages[0][:].bitcast(I32), 0)
         make_identity(nc, ident[:])
 
-        for l in (SRC, DST):
-            nc.vector.tensor_copy(picked_rows[:, J * l : J * (l + 1)], table_sc[:].indirect(lists[l][:]))
-        for a in range(PASSES):
-            shift = PARKED + 4 * a
-            nc.sync.dma_start(picked_sc[0:100, a, :].bitcast(I32), picked_rows[shift : shift + 100, :].bitcast(I32))
-        last_raw = []
-        for half in range(2):
-            raw = placed.tile([P, PACK, N // 2], F32, name="last_raw%d" % half, offset=LAST_RAW_AT[half], align_bytes=64)
-            nc.sync.dma_start(raw[:], wo[512:1024, 256 * half : 256 * (half + 1)].rearrange("(p j) n -> p j n", j=PACK))
-            last_raw.append(raw)
-        gate = keep.tile([P, J], F32, name="gate", tag="picked_rows", align_bytes=64)
-        nc.sync.dma_start(gate[:], wgo)
+        def half_list(l, h):
+            return lists[l][:, 32 * h : 32 * (h + 1)]
+
+        def pick_scales(h, rows, queue):
+            for l in (SRC, DST):
+                nc.vector.tensor_copy(rows[:, HALF * l : HALF * (l + 1)], table_sc[:].indirect(half_list(l, h)))
+            for a in range(PASSES):
+                shift = PARKED + 4 * a
+                queue.dma_start(picked_sc[h][0:100, a, :].bitcast(I32), rows[shift : shift + 100, :].bitcast(I32))
 
         picked = {}
 
-        def pick_words(h, pairs, parted):
-            for l in (DST, SRC):
-                nc.vector.tensor_copy(pairs[:, l, :], table[:].bitcast(U32).indirect(lists[l][:, 32 * h : 32 * (h + 1)]))
-            nc.vector.tensor_copy(parted[:].bitcast(U16), pairs[:].bitcast(U16).rearrange("p l (s a) -> p l a s", a=PASSES))
-            picked[h] = parted
+        def pick_words(l, h, pairs):
+            nc.vector.tensor_copy(pairs, table[:].bitcast(U32).indirect(half_list(l, h)))
 
-        w8 = {}
-        for u in range(2):
-            for a in range(PASSES):
-                w8[(u, a)] = (
-                    keep.tile([P, 2 * PAIR], U32, name="codes%d_%d" % (u, a), align_bytes=64),
-                    keep.tile([P, 2 * PAIR], U8, name="scales%d_%d" % (u, a), align_bytes=64),
-                )
+        def part_words(parted, pairs):
+            nc.vector.tensor_copy(parted.bitcast(U16), pairs.bitcast(U16).rearrange("p l (s a) -> p l a s", a=PASSES))
 
-        def quantize_columns(rounded, u, a, first, last):
-            codes, scales = w8[(u, a)]
-            nc.vector.quantize_mx(out=codes[:, first:last].bitcast(FP8X4), scales=scales[:, first:last], in_=rounded)
+        pick_scales(0, keep.tile([P, 2 * HALF], U8, name="rows0", align_bytes=64), nc.scalar)
+        for r in range(1, 4):
+            nc.scalar.dma_start(w4_sc[r:P:32].bitcast(I32), w4_sc[8 * r : P : 32].bitcast(I32))
+        pairs0 = placed.tile([P, 5, HALF], U32, name="pairs0", offset=PAIRS0_AT, align_bytes=64)
+        for l in (SRC, DST):
+            pick_words(l, 0, pairs0[:, l, :])
+        picked[0] = keep.tile([P, 2, PASSES, 2 * HALF], U8, name="picked0", align_bytes=64)
+        part_words(picked[0][:], pairs0[:, 0:2, :])
+        raw_wo0 = load_first_pass(wo, placed.tile([P, PACK, N], F32, name="raw_wo0", offset=RAW_WO0_AT, align_bytes=64))
+        raw_wo1 = load_second_pass(
+            wo, [placed.tile([P, PACK, PAIR], F32, name="raw_wo1_%d" % c, offset=RAW_WO1_AT[c], align_bytes=64) for c in range(2)]
+        )
+        pick_scales(1, placed.tile([P, 2 * HALF], U8, name="rows1", offset=ROWS1_AT, align_bytes=64), nc.sync)
+        pages.append(placed.tile([P, T], F32, name="page1", offset=PAGE1_AT, align_bytes=64))
+        nc.gpsimd.memset(pages[1][:].bitcast(I32), 0)
 
-        def round_weight(w, a, rounded):
-            nc.scalar.copy(
-                rounded[:].rearrange("p u (m e j) -> p m j u e", e=2, j=PACK),
-                raws[(w, a)][:].rearrange("p j (m u e) -> p m j u e", u=2, e=2),
+        def mx_tiles(name, shape):
+            return (
+                keep.tile(shape, U32, name=name + "_codes", align_bytes=64),
+                keep.tile(shape, U8, name=name + "_scales", align_bytes=64),
             )
-            for u in range(2):
-                quantize_columns(rounded[:, u, :], u, a, PAIR * w, PAIR * (w + 1))
 
-        def round_last_weight(u, rounded):
-            for half in range(2):
-                part = rounded[:, P * PACK * half : P * PACK * (half + 1)]
-                nc.scalar.copy(
-                    part.rearrange("p (m e j) -> p m j e", e=2, j=PACK),
-                    last_raw[half][:].rearrange("p j (m u e) -> p u m j e", u=2, e=2)[:, u],
-                )
-                quantize_columns(part, u, 1, PAIR + P * half, PAIR + P * (half + 1))
+        def quantize(operand, a, cols, rounded):
+            codes, scales = operand
+            nc.vector.quantize_mx(out=codes[:, a, cols].bitcast(FP8X4), scales=scales[:, a, cols], in_=rounded)
 
-        pick_words(
-            0,
-            placed.tile([P, 2, HALF], U32, name="pairs0", offset=PAIRS0_AT, align_bytes=64),
-            keep.tile([P, 2, PASSES, 2 * HALF], U8, name="picked0", align_bytes=64),
-        )
-        w4_sc = placed.tile([P, 2 * PASSES, N], U8, name="w4_sc", offset=W4_SC_AT, align_bytes=64)
-        w4 = placed.tile([P, 2 * PASSES, 2 * N], U8, name="w4", offset=W4_AT, align_bytes=64)
-        nc.vector.tensor_copy(
-            w4[:].bitcast(I32).rearrange("p v (u m) -> p v u m", u=2),
-            w4_raw[:].bitcast(I32).rearrange("p v (m u) -> p v u m", u=2),
-        )
-        nc.vector.tensor_copy(
-            w4_sc[:].bitcast(U16).rearrange("p v (u m) -> p v u m", u=2),
-            w4_sc_raw[:].bitcast(U16).rearrange("p v (m u) -> p v u m", u=2),
-        )
-        round_weight(WA, 0, keep.tile([P, 2, PAIR * PACK], BF16, name="rounded_wa0", align_bytes=64))
-        round_weight(WA, 1, placed.tile([P, 2, PAIR * PACK], BF16, name="rounded_wa1", offset=ROUNDED_WA1_AT, align_bytes=64))
-        round_weight(WO, 0, keep.tile([P, 2, PAIR * PACK], BF16, name="rounded_wo0", align_bytes=64))
-        round_last_weight(0, keep.tile([P, PAIR * PACK], BF16, name="rounded_wo1_pair0", tag="wo1_pair0", align_bytes=64))
-        pick_words(
-            1,
-            placed.tile([P, 2, HALF], U32, name="pairs1", offset=PAIRS1_AT, align_bytes=64),
-            keep.tile([P, 2, PASSES, 2 * HALF], U8, name="picked1", tag="wo1_pair0", align_bytes=64),
-        )
+        def round_columns(rounded, raw):
+            nc.scalar.copy(
+                rounded.rearrange("p (c i j) -> p c j i", i=4, j=PACK), raw.rearrange("p j (c i) -> p c j i", i=4)
+            )
+
+        wa8 = mx_tiles("wa8", [P, PASSES, N])
+        rounded = keep.tile([P, N * PACK], BF16, name="rounded_wa0", tag="rounded_wa0", align_bytes=64)
+        round_columns(rounded[:], raw_wa0[:])
+        quantize(wa8, 0, slice(0, N), rounded[:])
+        pairs1 = [keep.tile([P, 1, HALF], U32, name="pairs1_src", tag="rounded_wa0", align_bytes=64)]
+        pick_words(SRC, 1, pairs1[SRC][:, 0, :])
+        for c in range(2):
+            if c == 0:
+                rounded = keep.tile([P, PAIR * PACK], BF16, name="rounded_wa1_0", align_bytes=64)
+            else:
+                rounded = placed.tile([P, N * PACK], BF16, name="rounded_wa1_1", offset=ROUNDED_WA1_AT, align_bytes=64)
+            round_columns(rounded[:, 0 : PAIR * PACK], raw_wa1[c][:])
+            quantize(wa8, 1, slice(PAIR * c, PAIR * (c + 1)), rounded[:, 0 : PAIR * PACK])
+        pairs1.append(placed.tile([P, 1, HALF], U32, name="pairs1_dst", offset=PAIRS1_DST_AT, align_bytes=64))
+        pick_words(DST, 1, pairs1[DST][:, 0, :])
+        gate = placed.tile([P, J], F32, name="gate", offset=GATE_AT, align_bytes=64)
+        nc.sync.dma_start(gate[:], wgo)
         pages.append(placed.tile([P, T], F32, name="page2", offset=PAGE2_AT, align_bytes=64))
         nc.gpsimd.memset(pages[2][:].bitcast(I32), 0)
         pages.append(pages[0])
+
+        wo8_first = mx_tiles("wo8_first", [P, PASSES, PAIR])
+        rounded = keep.tile([P, PAIR * PACK], BF16, name="rounded_wo0", align_bytes=64)
+        nc.scalar.copy(
+            rounded[:].rearrange("p (m e j) -> p m j e", e=2, j=PACK),
+            raw_wo0[:].rearrange("p j (m u e) -> p u m j e", u=2, e=2)[:, 0],
+        )
+        quantize(wo8_first, 0, slice(0, PAIR), rounded[:])
+        rounded = placed.tile([P, PAIR * PACK], BF16, name="rounded_wo1", offset=ROUNDED_WO1_AT, align_bytes=64)
+        for c in range(2):
+            part = rounded[:, P * PACK * c : P * PACK * (c + 1)]
+            nc.scalar.copy(
+                part.rearrange("p (m e j) -> p m j e", e=2, j=PACK),
+                raw_wo1[c][:].rearrange("p j (m u e) -> p u m j e", u=2, e=2)[:, 0],
+            )
+            quantize(wo8_first, 1, slice(P * c, P * (c + 1)), part)
+        picked[1] = placed.tile([P, 2, PASSES, 2 * HALF], U8, name="picked1", offset=PICKED1_AT, align_bytes=64)
+        for l in (SRC, DST):
+            part_words(picked[1][:, l : l + 1], pairs1[l][:])
+
+        wo8_second = mx_tiles("wo8_second", [P, PASSES, PAIR])
+
+        def round_second_planes():
+            both = keep.tile([P, PASSES, 2, P * PACK], BF16, name="rounded_wo_second", tag="own_first", align_bytes=64)
+            nc.scalar.copy(
+                both[:, 0].rearrange("p e (m j) -> p m j e", j=PACK),
+                raw_wo0[:].rearrange("p j (m u e) -> p u m j e", u=2, e=2)[:, 1],
+            )
+            for c in range(2):
+                nc.scalar.copy(
+                    both[:, 1, :, PAIR * c : PAIR * (c + 1)].rearrange("p e (m j) -> p m j e", j=PACK),
+                    raw_wo1[c][:].rearrange("p j (m u e) -> p u m j e", u=2, e=2)[:, 1],
+                )
+            codes, scales = wo8_second
+            nc.vector.quantize_mx(
+                out=codes[:].rearrange("p a c -> p (a c)").bitcast(FP8X4),
+                scales=scales[:].rearrange("p a c -> p (a c)"),
+                in_=both[:].rearrange("p a e c -> p (a e c)"),
+            )
 
         def mm(out, l, block, a, rhs, rhs_scale, start, stop):
             h, b = divmod(block, HALF // P)
             nc.tensor.matmul_mx(
                 out=out,
                 lhsT=picked[h][:, l, a, 2 * P * b : 2 * P * (b + 1)].bitcast(FP4X4),
-                lhsT_scale=picked_sc[:, a, J * l + P * block : J * l + P * (block + 1)],
+                lhsT_scale=picked_sc[h][:, a, HALF * l + P * b : HALF * l + P * (b + 1)],
                 rhs=rhs,
                 rhs_scale=rhs_scale,
                 start=start,
                 stop=stop,
             )
 
-        def mm_packed(out, w, u, block, start, stop):
-            for a in range(PASSES):
-                mm(
-                    out, SRC, block, a,
-                    w4[:, PASSES * w + a, 2 * PAIR * u : 2 * PAIR * (u + 1)].bitcast(FP4X4),
-                    w4_sc[:, PASSES * w + a, PAIR * u : PAIR * (u + 1)],
-                    start and a == 0, stop and a == PASSES - 1,
-                )
-
-        def mm_wide(out, u, block, a, start, stop):
-            codes, scales = w8[(u, a)]
-            mm(out, DST, block, a, codes[:].bitcast(FP8X4), scales[:], start, stop)
-
-        def mm_narrow(out, w, block, start, stop):
-            for a in range(PASSES):
-                codes, scales = w8[(0, a)]
-                for c in range(2):
-                    cols = slice(PAIR * w + P * c, PAIR * w + P * (c + 1))
-                    mm(
-                        out[:, P * c : P * (c + 1)], DST, block, a, codes[:, cols].bitcast(FP8X4), scales[:, cols],
-                        start and a == 0 and c == 0, stop and a == PASSES - 1 and c == 1,
-                    )
-
-        def from_bank(ap):
-            return ap.rearrange("p (m e) -> p e m", e=2)
-
-        def by_plane(ap):
-            return ap.rearrange("p (e m) -> p e m", e=2)
-
-        def from_bank_blocks(ap):
-            return ap.rearrange("p b (m e) -> p b e m", e=2)
-
-        def by_plane_blocks(ap):
-            return ap.rearrange("p b (e m) -> p b e m", e=2)
-
-        summands = {}
-        results = [keep.tile([P, 2, J], F32, name="result%d" % u, align_bytes=64) for u in range(2)]
+        msgs = []
+        for q in range(4):
+            if q == 1:
+                msgs.append(placed.tile([P, 2, PACK, P], F32, name="msg1", offset=MSG1_AT, align_bytes=64))
+            else:
+                msgs.append(keep.tile([P, 2, PACK, P], F32, name="msg%d" % q, align_bytes=64))
+        results = keep.tile([P, PACK, J], F32, name="results", align_bytes=64)
         staged = []
         out_rows = out_0.rearrange("(p i) t -> i p t", i=PACK)
 
-        def products(unit):
-            u, q = divmod(unit, UNITS)
-            eta = ring.tile([P, 2, PAIR], F32, name="eta")
-            if unit == 0:
-                own = keep.tile([P, 2, PAIR], F32, name="own_first", tag="own_first", align_bytes=64)
-            elif unit == UNITS:
-                own = placed.tile([P, T * PACK * 2 // (PAIR * 4), PAIR], F32, name="own_pair1", offset=STAGED_AT, align_bytes=64)
-            else:
-                own = ring.tile([P, 2, PAIR], F32, name="own")
-            msg = ring.tile([P, 2, PAIR], F32, name="msg")
-            ms = psum.tile([P, 2, PAIR], F32, name="ms")
-            if unit < EARLY:
-                za = psum.tile([P, 2, PAIR], F32, name="zo", bufs=4)
-                for b in range(2):
-                    block = 2 * q + b
-                    mm_packed(za[:, b, :], WB, u, block, True, False)
-                    mm_narrow(za[:, b, :], WA, block, False, True)
-                    mm_packed(ms[:, b, :], WC, u, block, True, True)
-                nc.scalar.activation(by_plane_blocks(eta[:]), from_bank_blocks(za[:]), ACT.Sigmoid)
-            else:
-                banks = []
-                for b in range(2):
-                    block = 2 * q + b
-                    zo = psum.tile([P, 2, PAIR], F32, name="zo", bufs=4)
-                    both = zo[:].rearrange("p w c -> p (w c)")
-                    mm_wide(both, u, block, 0, True, False)
-                    mm_packed(zo[:, WA, :], WB, u, block, False, False)
-                    mm_wide(both, u, block, 1, False, True)
-                    mm_packed(ms[:, b, :], WC, u, block, True, True)
-                    nc.scalar.activation(by_plane(eta[:, b, :]), from_bank(zo[:, WA, :]), ACT.Sigmoid)
-                    banks.append(zo)
-                for b, zo in enumerate(banks):
-                    nc.scalar.copy(by_plane(own[:, b, :]), from_bank(zo[:, WO, :]))
-            nc.vector.tensor_tensor(by_plane_blocks(msg[:]), from_bank_blocks(ms[:]), by_plane_blocks(eta[:]), ALU.mult)
-            summands[unit] = (own, msg)
+        def gated_message(block):
+            ms = psum.tile([P, N], F32, name="ms", tag="ms%d" % (block % 4))
+            za = psum.tile([P, N], F32, name="za", tag="za%d" % (block % 2))
+            for out, w in ((ms, WC), (za, WB)):
+                for a in range(PASSES):
+                    v = PASSES * w + a
+                    mm(out[:], SRC, block, a, w4[:, v, :].bitcast(FP4X4), w4_sc[:, v, :], a == 0, w == WC and a == PASSES - 1)
+            for a in range(PASSES):
+                mm(za[:], DST, block, a, wa8[0][:, a, :].bitcast(FP8X4), wa8[1][:, a, :], False, a == PASSES - 1)
+            eta = ring.tile([P, PACK, P], F32, name="eta")
+            nc.scalar.activation(eta[:], za[:].rearrange("p (m i) -> p i m", i=PACK), ACT.Sigmoid)
+            nc.vector.tensor_tensor(
+                msgs[block // 2][:, block % 2], ms[:].rearrange("p (m i) -> p i m", i=PACK), eta[:], ALU.mult
+            )
 
-        def turn_and_add(unit):
-            u, q = divmod(unit, UNITS)
-            own, msg = summands[unit]
-            edges = slice(UNIT * q, UNIT * (q + 1))
-            steps = [(0, 1), (1, 2)] if unit == 0 else [(0, 2)]
-            if unit < EARLY:
-                banks = []
-                for b in range(2):
-                    ow = psum.tile([P, 2, PAIR], F32, name="zo", bufs=4)
-                    mm_narrow(ow[:, 0, :], WO, 2 * q + b, True, True)
-                    banks.append(ow)
-                for first, last in steps:
-                    for b, ow in enumerate(banks):
-                        nc.scalar.copy(by_plane(own[:, b, :])[:, first:last], from_bank(ow[:, 0, :])[:, first:last])
+        held = {}
+
+        def project(unit, banks):
+            plane0, planes, block0, blocks = UNIT_LIST[unit]
+            codes, scales = wo8_first if plane0 == 0 else wo8_second
+            ow = psum.tile([P, blocks, planes * P], F32, name="ow", tag=banks[0])
+            for a in range(PASSES):
+                for c in range(planes):
+                    at = P * (plane0 % 2 + c)
+                    for b in range(blocks):
+                        mm(
+                            ow[:, b, P * c : P * (c + 1)], DST, block0 + b, a,
+                            codes[:, a, at : at + P].bitcast(FP8X4), scales[:, a, at : at + P],
+                            a == 0 and c == 0 and b == 0, a == PASSES - 1 and c == planes - 1 and b == blocks - 1,
+                        )
+            if unit == 0:
+                own = keep.tile([P, 2 * blocks, planes, P], F32, name="own_first", tag="own_first", align_bytes=64)
+            elif unit == 7:
+                own = placed.tile([P, 8 * blocks, planes, P], F32, name="own_held", offset=STAGED_AT, align_bytes=64)
+            else:
+                own = ring.tile([P, blocks, planes, P], F32, name="own")
+            total = psum.tile([P, planes, blocks * P], F32, name="total", tag=banks[1])
+            steps = [(0, 1), (1, 2)] if unit == 0 else [(0, planes)]
             for first, last in steps:
-                total = psum.tile([P, 2, UNIT], F32, name="total")
-                for e in range(first, last):
-                    for b in range(2):
-                        for s, summand in enumerate((own, msg)):
-                            nc.tensor.matmul(
-                                total[:, e, P * b : P * (b + 1)], summand[:, b, P * e : P * (e + 1)], ident[:],
-                                start=s == 0, stop=s == 1, is_transpose=True,
-                            )
-                nc.scalar.activation(results[u][:, first:last, edges], total[:, first:last, :], ACT.Relu)
+                nc.scalar.copy(own[:, 0:blocks, first:last], ow[:].rearrange("p b (m e) -> p b e m", e=planes)[:, :, first:last])
+            held[unit] = (own, total)
+
+        def turn(unit, first, last):
+            plane0, planes, block0, blocks = UNIT_LIST[unit]
+            own, total = held[unit]
+            edges = slice(P * block0, P * (block0 + blocks))
+            for e in range(first, last):
+                for b in range(blocks):
+                    block = block0 + b
+                    for s, summand in enumerate((own[:, b, e], msgs[block // 2][:, block % 2, plane0 + e])):
+                        nc.tensor.matmul(
+                            total[:, e, P * b : P * (b + 1)], summand, ident[:], start=s == 0, stop=s == 1, is_transpose=True
+                        )
+            nc.scalar.activation(results[:, plane0 + first : plane0 + last, edges], total[:, first:last, :], ACT.Relu)
+
+        def whole_unit(unit, banks):
+            project(unit, banks)
+            turn(unit, 0, UNIT_LIST[unit][1])
 
         def place(i, first, last):
-            u, e = divmod(i, 2)
-            edges = slice(UNIT * first, UNIT * last)
             nc.vector.tensor_tensor(
-                pages[i][:].indirect(lists[DST][:, 16 * first : 16 * last]), results[u][:, e, edges], gate[:, edges], ALU.mult
+                pages[i][:].indirect(lists[DST][:, first // 16 : last // 16]), results[:, i, first:last], gate[:, first:last], ALU.mult
             )
-            if last == UNITS:
+            if last == J:
                 nc.sync.dma_start(out_rows[i], pages[i][:])
 
         def round_plane(i):
@@ -319,25 +326,40 @@ def tile_list_rgg_ownreluP_kernel(
                 else:
                     nc.scalar.copy(staged[c][:, u, :, e], pages[i][:, cols])
 
-        products(0)
-        for unit in range(2 * UNITS):
-            u, q = divmod(unit, UNITS)
-            if unit == UNITS + 1:
-                round_plane(0)
-            if unit + 1 < 2 * UNITS:
-                products(unit + 1)
-            turn_and_add(unit)
-            if unit == 0:
-                round_last_weight(1, keep.tile([P, PAIR * PACK], BF16, name="rounded_wo1_pair1", tag="own_first", align_bytes=64))
-            if unit == UNITS:
-                for c in range(CHUNKS):
-                    at = STAGED_AT + PACK * 2 * STARTS[c]
-                    staged.append(placed.tile([P, 2, WIDTHS[c], 2], BF16, name="staged%d" % c, offset=at, align_bytes=64))
-            place(2 * u, q, q + 1)
-            if unit < EARLY:
-                place(1, q, q + 1)
-            elif q % 2 == 1:
-                place(2 * u + 1, q - 1, q + 1)
+        own_banks, gate_banks = ("ow", "total"), ("za0", "za1")
+        for block in range(3):
+            gated_message(block)
+        project(0, own_banks)
+        turn(0, 0, 1)
+        place(0, 0, UNIT)
+        gated_message(3)
+        turn(0, 1, 2)
+        place(1, 0, UNIT)
+        round_second_planes()
+        whole_unit(1, own_banks)
+        for i in range(2):
+            place(i, UNIT, 2 * UNIT)
+        gated_message(4)
+        gated_message(5)
+        whole_unit(4, own_banks)
+        place(2, 0, HALF)
+        gated_message(6)
+        gated_message(7)
+        whole_unit(2, own_banks)
+        for i in range(2):
+            place(i, 2 * UNIT, 3 * UNIT)
+        whole_unit(6, gate_banks)
+        whole_unit(3, own_banks)
+        for i in range(2):
+            place(i, 3 * UNIT, J)
+        whole_unit(5, gate_banks)
+        place(2, HALF, J)
+        whole_unit(7, own_banks)
+        for c in range(CHUNKS):
+            at = STAGED_AT + PACK * 2 * STARTS[c]
+            staged.append(placed.tile([P, 2, WIDTHS[c], 2], BF16, name="staged%d" % c, offset=at, align_bytes=64))
+        round_plane(0)
+        place(3, 0, J)
         for i in range(1, PACK):
             round_plane(i)
 

@@ -51,6 +51,7 @@ PICKED1_AT = ROUNDED_WO1_AT + 64 - 4 * KIB
 MSG1_AT = ROUNDED_WO1_AT + 64
 STAGED_AT = 54 * KIB
 
+
 UNIT_LIST = [(0, 2, 2 * q, 2) for q in range(4)] + [(i, 1, 4 * h, 4) for i in (2, 3) for h in range(2)]
 
 
@@ -72,6 +73,8 @@ def tile_list_rgg_ownreluP_kernel(
         w4_sc = keep.tile([P, 2 * PASSES, N], U8, name="w4_sc", align_bytes=64)
         ident = keep.tile([P, P], F32, name="ident", align_bytes=64)
 
+        page2 = keep.tile([P, T], F32, name="page2", align_bytes=64)
+        nc.vector.memset(page2[:].bitcast(I32), 0)
         for q in range(QUADS):
             nc.gpsimd.memset(table_sc[32 * q : 32 * q + PARKED, :].bitcast(I32), 0)
         nc.gpsimd.memset(w4_sc[:].bitcast(I32), 0)
@@ -84,14 +87,9 @@ def tile_list_rgg_ownreluP_kernel(
             )
         nc.sync.dma_start(table[:], tab_words[0].rearrange("p t b -> p (t b)").bitcast(I32))
 
-        def load_first_pass(weight, raw):
-            nc.sync.dma_start(raw[:], weight[0:512, :].rearrange("(p j) n -> p j n", j=PACK))
+        def load_pass(weight, a, raw, first, last):
+            nc.sync.dma_start(raw[:], weight[512 * a : 512 * (a + 1), first:last].rearrange("(p j) n -> p j n", j=PACK))
             return raw
-
-        def load_second_pass(weight, halves):
-            for c, raw in enumerate(halves):
-                nc.sync.dma_start(raw[:], weight[512:1024, PAIR * c : PAIR * (c + 1)].rearrange("(p j) n -> p j n", j=PACK))
-            return halves
 
         def load_words(w):
             nc.sync.dma_start(
@@ -105,19 +103,15 @@ def tile_list_rgg_ownreluP_kernel(
                 w4_sc[0:P:8, PASSES * w : PASSES * (w + 1), :].bitcast(I32), scales.rearrange("a s n -> s a n").bitcast(I32)
             )
         load_words(WB)
-        raw_wa0 = load_first_pass(wa, keep.tile([P, PACK, N], F32, name="raw_wa0", align_bytes=64))
-        raw_wa1 = load_second_pass(
-            wa, [keep.tile([P, PACK, PAIR], F32, name="raw_wa1_%d" % c, align_bytes=64) for c in range(2)]
-        )
+        raw_wa = [load_pass(wa, 0, keep.tile([P, PACK, N], F32, name="raw_wa0", align_bytes=64), 0, N)]
 
-        warm = keep.tile([P, 2], F32, name="warm")
-        nc.vector.memset(warm[:, 0:1], 0.0)
-        nc.scalar.activation(warm[:, 1:2], warm[:, 0:1], ACT.Sigmoid)
-
-        for h in range(2):
-            nc.gpsimd.memset(picked_sc[h][96:P].bitcast(I32), 0)
+        nc.gpsimd.memset(picked_sc[0][96:P].bitcast(I32), 0)
         pages = [keep.tile([P, T], F32, name="page0", align_bytes=64)]
         nc.gpsimd.memset(pages[0][:].bitcast(I32), 0)
+        warm = keep.tile([P, 2], F32, name="warm", tag="raw_wa1", align_bytes=64)
+        nc.gpsimd.memset(warm[:, 0:1], 0.0)
+        nc.scalar.activation(warm[:, 1:2], warm[:, 0:1], ACT.Sigmoid)
+        nc.gpsimd.memset(picked_sc[1][96:P].bitcast(I32), 0)
         make_identity(nc, ident[:])
 
         def half_list(l, h):
@@ -138,18 +132,21 @@ def tile_list_rgg_ownreluP_kernel(
         def part_words(parted, pairs):
             nc.vector.tensor_copy(parted.bitcast(U16), pairs.bitcast(U16).rearrange("p l (s a) -> p l a s", a=PASSES))
 
-        pick_scales(0, keep.tile([P, 2 * HALF], U8, name="rows0", align_bytes=64), nc.scalar)
+        pick_scales(0, keep.tile([P, 2 * HALF], U8, name="rows0", align_bytes=64), nc.sync)
         for r in range(1, 4):
-            nc.scalar.dma_start(w4_sc[r:P:32].bitcast(I32), w4_sc[8 * r : P : 32].bitcast(I32))
+            nc.sync.dma_start(w4_sc[r:P:32].bitcast(I32), w4_sc[8 * r : P : 32].bitcast(I32))
+        raw_wa.append(load_pass(wa, 1, keep.tile([P, PACK, N], F32, name="raw_wa1", tag="raw_wa1", align_bytes=64), 0, N))
         pairs0 = placed.tile([P, 5, HALF], U32, name="pairs0", offset=PAIRS0_AT, align_bytes=64)
         for l in (SRC, DST):
             pick_words(l, 0, pairs0[:, l, :])
         picked[0] = keep.tile([P, 2, PASSES, 2 * HALF], U8, name="picked0", align_bytes=64)
-        part_words(picked[0][:], pairs0[:, 0:2, :])
-        raw_wo0 = load_first_pass(wo, placed.tile([P, PACK, N], F32, name="raw_wo0", offset=RAW_WO0_AT, align_bytes=64))
-        raw_wo1 = load_second_pass(
-            wo, [placed.tile([P, PACK, PAIR], F32, name="raw_wo1_%d" % c, offset=RAW_WO1_AT[c], align_bytes=64) for c in range(2)]
-        )
+        for l in (SRC, DST):
+            part_words(picked[0][:, l : l + 1], pairs0[:, l : l + 1, :])
+        raw_wo0 = load_pass(wo, 0, placed.tile([P, PACK, N], F32, name="raw_wo0", offset=RAW_WO0_AT, align_bytes=64), 0, N)
+        raw_wo1 = []
+        for c in range(2):
+            raw = placed.tile([P, PACK, PAIR], F32, name="raw_wo1_%d" % c, offset=RAW_WO1_AT[c], align_bytes=64)
+            raw_wo1.append(load_pass(wo, 1, raw, PAIR * c, PAIR * (c + 1)))
         pick_scales(1, placed.tile([P, 2 * HALF], U8, name="rows1", offset=ROWS1_AT, align_bytes=64), nc.sync)
         pages.append(placed.tile([P, T], F32, name="page1", offset=PAGE1_AT, align_bytes=64))
         nc.gpsimd.memset(pages[1][:].bitcast(I32), 0)
@@ -171,23 +168,18 @@ def tile_list_rgg_ownreluP_kernel(
 
         wa8 = mx_tiles("wa8", [P, PASSES, N])
         rounded = keep.tile([P, N * PACK], BF16, name="rounded_wa0", tag="rounded_wa0", align_bytes=64)
-        round_columns(rounded[:], raw_wa0[:])
+        round_columns(rounded[:], raw_wa[0][:])
         quantize(wa8, 0, slice(0, N), rounded[:])
         pairs1 = [keep.tile([P, 1, HALF], U32, name="pairs1_src", tag="rounded_wa0", align_bytes=64)]
         pick_words(SRC, 1, pairs1[SRC][:, 0, :])
-        for c in range(2):
-            if c == 0:
-                rounded = keep.tile([P, PAIR * PACK], BF16, name="rounded_wa1_0", align_bytes=64)
-            else:
-                rounded = placed.tile([P, N * PACK], BF16, name="rounded_wa1_1", offset=ROUNDED_WA1_AT, align_bytes=64)
-            round_columns(rounded[:, 0 : PAIR * PACK], raw_wa1[c][:])
-            quantize(wa8, 1, slice(PAIR * c, PAIR * (c + 1)), rounded[:, 0 : PAIR * PACK])
+        rounded = placed.tile([P, N * PACK], BF16, name="rounded_wa1", offset=ROUNDED_WA1_AT, align_bytes=64)
+        round_columns(rounded[:], raw_wa[1][:])
+        quantize(wa8, 1, slice(0, N), rounded[:])
         pairs1.append(placed.tile([P, 1, HALF], U32, name="pairs1_dst", offset=PAIRS1_DST_AT, align_bytes=64))
         pick_words(DST, 1, pairs1[DST][:, 0, :])
         gate = placed.tile([P, J], F32, name="gate", offset=GATE_AT, align_bytes=64)
         nc.sync.dma_start(gate[:], wgo)
-        pages.append(placed.tile([P, T], F32, name="page2", offset=PAGE2_AT, align_bytes=64))
-        nc.gpsimd.memset(pages[2][:].bitcast(I32), 0)
+        pages.append(page2)
         pages.append(pages[0])
 
         wo8_first = mx_tiles("wo8_first", [P, PASSES, PAIR])
@@ -212,7 +204,7 @@ def tile_list_rgg_ownreluP_kernel(
         wo8_second = mx_tiles("wo8_second", [P, PASSES, PAIR])
 
         def round_second_planes():
-            both = keep.tile([P, PASSES, 2, P * PACK], BF16, name="rounded_wo_second", tag="own_first", align_bytes=64)
+            both = keep.tile([P, PASSES, 2, P * PACK], BF16, name="rounded_wo_second", tag="eta3", align_bytes=64)
             nc.scalar.copy(
                 both[:, 0].rearrange("p e (m j) -> p m j e", j=PACK),
                 raw_wo0[:].rearrange("p j (m u e) -> p u m j e", u=2, e=2)[:, 1],
@@ -260,7 +252,10 @@ def tile_list_rgg_ownreluP_kernel(
                     mm(out[:], SRC, block, a, w4[:, v, :].bitcast(FP4X4), w4_sc[:, v, :], a == 0, w == WC and a == PASSES - 1)
             for a in range(PASSES):
                 mm(za[:], DST, block, a, wa8[0][:, a, :].bitcast(FP8X4), wa8[1][:, a, :], False, a == PASSES - 1)
-            eta = ring.tile([P, PACK, P], F32, name="eta")
+            if block == 3:
+                eta = keep.tile([P, PACK, P], F32, name="eta3", tag="eta3", align_bytes=64)
+            else:
+                eta = ring.tile([P, PACK, P], F32, name="eta")
             nc.scalar.activation(eta[:], za[:].rearrange("p (m i) -> p i m", i=PACK), ACT.Sigmoid)
             nc.vector.tensor_tensor(
                 msgs[block // 2][:, block % 2], ms[:].rearrange("p (m i) -> p i m", i=PACK), eta[:], ALU.mult
@@ -268,10 +263,10 @@ def tile_list_rgg_ownreluP_kernel(
 
         held = {}
 
-        def project(unit, banks):
+        def project(unit, bank):
             plane0, planes, block0, blocks = UNIT_LIST[unit]
             codes, scales = wo8_first if plane0 == 0 else wo8_second
-            ow = psum.tile([P, blocks, planes * P], F32, name="ow", tag=banks[0])
+            ow = psum.tile([P, blocks, planes * P], F32, name="ow", tag=bank)
             for a in range(PASSES):
                 for c in range(planes):
                     at = P * (plane0 % 2 + c)
@@ -281,21 +276,19 @@ def tile_list_rgg_ownreluP_kernel(
                             codes[:, a, at : at + P].bitcast(FP8X4), scales[:, a, at : at + P],
                             a == 0 and c == 0 and b == 0, a == PASSES - 1 and c == planes - 1 and b == blocks - 1,
                         )
-            if unit == 0:
-                own = keep.tile([P, 2 * blocks, planes, P], F32, name="own_first", tag="own_first", align_bytes=64)
-            elif unit == 7:
+            if unit == 7:
                 own = placed.tile([P, 8 * blocks, planes, P], F32, name="own_held", offset=STAGED_AT, align_bytes=64)
             else:
-                own = ring.tile([P, blocks, planes, P], F32, name="own")
-            total = psum.tile([P, planes, blocks * P], F32, name="total", tag=banks[1])
+                own = ring.tile([P, blocks, planes, P], F32, name="own", bufs=3)
             steps = [(0, 1), (1, 2)] if unit == 0 else [(0, planes)]
             for first, last in steps:
                 nc.scalar.copy(own[:, 0:blocks, first:last], ow[:].rearrange("p b (m e) -> p b e m", e=planes)[:, :, first:last])
-            held[unit] = (own, total)
+            held[unit] = own
 
-        def turn(unit, first, last):
+        def turn(unit, first, last, bank):
             plane0, planes, block0, blocks = UNIT_LIST[unit]
-            own, total = held[unit]
+            own = held[unit]
+            total = psum.tile([P, planes, blocks * P], F32, name="total", tag=bank)
             edges = slice(P * block0, P * (block0 + blocks))
             for e in range(first, last):
                 for b in range(blocks):
@@ -305,10 +298,6 @@ def tile_list_rgg_ownreluP_kernel(
                             total[:, e, P * b : P * (b + 1)], summand, ident[:], start=s == 0, stop=s == 1, is_transpose=True
                         )
             nc.scalar.activation(results[:, plane0 + first : plane0 + last, edges], total[:, first:last, :], ACT.Relu)
-
-        def whole_unit(unit, banks):
-            project(unit, banks)
-            turn(unit, 0, UNIT_LIST[unit][1])
 
         def place(i, first, last):
             nc.vector.tensor_tensor(
@@ -326,35 +315,41 @@ def tile_list_rgg_ownreluP_kernel(
                 else:
                     nc.scalar.copy(staged[c][:, u, :, e], pages[i][:, cols])
 
-        own_banks, gate_banks = ("ow", "total"), ("za0", "za1")
         for block in range(3):
             gated_message(block)
-        project(0, own_banks)
-        turn(0, 0, 1)
+        project(0, "ow")
+        turn(0, 0, 1, "total")
         place(0, 0, UNIT)
         gated_message(3)
-        turn(0, 1, 2)
+        turn(0, 1, 2, "total")
         place(1, 0, UNIT)
+        project(1, "ow")
+        turn(1, 0, 2, "total")
         round_second_planes()
-        whole_unit(1, own_banks)
         for i in range(2):
             place(i, UNIT, 2 * UNIT)
         gated_message(4)
         gated_message(5)
-        whole_unit(4, own_banks)
+        project(4, "ow")
+        turn(4, 0, 1, "total")
         place(2, 0, HALF)
         gated_message(6)
         gated_message(7)
-        whole_unit(2, own_banks)
+        project(2, "ow")
+        turn(2, 0, 2, "total")
         for i in range(2):
             place(i, 2 * UNIT, 3 * UNIT)
-        whole_unit(6, gate_banks)
-        whole_unit(3, own_banks)
+        project(3, "ms0")
+        project(5, "ms1")
+        turn(3, 0, 2, "za0")
         for i in range(2):
             place(i, 3 * UNIT, J)
-        whole_unit(5, gate_banks)
+        project(6, "ow")
+        project(7, "ms0")
+        turn(5, 0, 1, "total")
         place(2, HALF, J)
-        whole_unit(7, own_banks)
+        turn(6, 0, 1, "za1")
+        turn(7, 0, 1, "za0")
         for c in range(CHUNKS):
             at = STAGED_AT + PACK * 2 * STARTS[c]
             staged.append(placed.tile([P, 2, WIDTHS[c], 2], BF16, name="staged%d" % c, offset=at, align_bytes=64))
@@ -387,4 +382,4 @@ def tile_list_rgg_ownreluP_kernel(
                 weave(c + 1)
             quantize_chunk(c)
         for q in range(QUADS):
-            nc.scalar.dma_start(out_2[0, 4 * q : 4 * q + 4, :].bitcast(I32), y_sc[32 * q : 32 * q + 4, :].bitcast(I32))
+            (nc.scalar, nc.sync)[q % 2].dma_start(out_2[0, 4 * q : 4 * q + 4, :].bitcast(I32), y_sc[32 * q : 32 * q + 4, :].bitcast(I32))

@@ -22,13 +22,11 @@ PACK = 4
 PASSES = K // (P * PACK)
 QUADS = 4
 PARKED = 24
+LIVE = 100
 HALF = J // 2
+QUARTER = J // 4
 PAIR = N // 2
-UNIT = 2 * P
-UNITS = J // UNIT
-EARLY = 2
 SRC, DST = 0, 1
-WA, WO = 0, 1
 WB, WC = 0, 1
 
 WIDTHS = (256, 512, 512, 512, 256)
@@ -42,17 +40,7 @@ PAGE1_AT = PAIRS0_AT + 64 - 8 * KIB
 ROWS1_AT = PAIRS0_AT + 64
 RAW_WO1_AT = (ROWS1_AT + KIB, ROWS1_AT + 5 * KIB)
 RAW_WO0_AT = ROWS1_AT + 9 * KIB
-ROUNDED_WA1_AT = 36 * KIB
-PAGE2_AT = ROUNDED_WA1_AT + 64 - 8 * KIB
-PAIRS1_DST_AT = ROUNDED_WA1_AT + 64
-GATE_AT = PAIRS1_DST_AT + 2 * KIB
-ROUNDED_WO1_AT = 48 * KIB
-PICKED1_AT = ROUNDED_WO1_AT + 64 - 4 * KIB
-MSG1_AT = ROUNDED_WO1_AT + 64
-STAGED_AT = 54 * KIB
-
-
-UNIT_LIST = [(0, 2, 2 * q, 2) for q in range(4)] + [(i, 1, 4 * h, 4) for i in (2, 3) for h in range(2)]
+STAGED_AT = 26 * KIB
 
 
 def tile_list_rgg_ownreluP_kernel(
@@ -73,8 +61,8 @@ def tile_list_rgg_ownreluP_kernel(
         w4_sc = keep.tile([P, 2 * PASSES, N], U8, name="w4_sc", align_bytes=64)
         ident = keep.tile([P, P], F32, name="ident", align_bytes=64)
 
-        page2 = keep.tile([P, T], F32, name="page2", align_bytes=64)
-        nc.vector.memset(page2[:].bitcast(I32), 0)
+        pages = {2: keep.tile([P, T], F32, name="page2", align_bytes=64)}
+        nc.vector.memset(pages[2][:].bitcast(I32), 0)
         for q in range(QUADS):
             nc.gpsimd.memset(table_sc[32 * q : 32 * q + PARKED, :].bitcast(I32), 0)
         nc.gpsimd.memset(w4_sc[:].bitcast(I32), 0)
@@ -103,10 +91,10 @@ def tile_list_rgg_ownreluP_kernel(
                 w4_sc[0:P:8, PASSES * w : PASSES * (w + 1), :].bitcast(I32), scales.rearrange("a s n -> s a n").bitcast(I32)
             )
         load_words(WB)
-        raw_wa = [load_pass(wa, 0, keep.tile([P, PACK, N], F32, name="raw_wa0", align_bytes=64), 0, N)]
+        raw_wa0 = load_pass(wa, 0, keep.tile([P, PACK, N], F32, name="raw_wa0", align_bytes=64), 0, N)
 
         nc.gpsimd.memset(picked_sc[0][96:P].bitcast(I32), 0)
-        pages = [keep.tile([P, T], F32, name="page0", align_bytes=64)]
+        pages[0] = keep.tile([P, T], F32, name="page0", align_bytes=64)
         nc.gpsimd.memset(pages[0][:].bitcast(I32), 0)
         warm = keep.tile([P, 2], F32, name="warm", tag="raw_wa1", align_bytes=64)
         nc.gpsimd.memset(warm[:, 0:1], 0.0)
@@ -114,115 +102,98 @@ def tile_list_rgg_ownreluP_kernel(
         nc.gpsimd.memset(picked_sc[1][96:P].bitcast(I32), 0)
         make_identity(nc, ident[:])
 
-        def half_list(l, h):
-            return lists[l][:, 32 * h : 32 * (h + 1)]
+        def offsets(l, first, last):
+            return lists[l][:, first // 16 : last // 16]
 
-        def pick_scales(h, rows, queue):
+        def pick_scales(h, rows):
             for l in (SRC, DST):
-                nc.vector.tensor_copy(rows[:, HALF * l : HALF * (l + 1)], table_sc[:].indirect(half_list(l, h)))
+                nc.vector.tensor_copy(rows[:, HALF * l : HALF * (l + 1)], table_sc[:].indirect(offsets(l, HALF * h, HALF * (h + 1))))
             for a in range(PASSES):
                 shift = PARKED + 4 * a
-                queue.dma_start(picked_sc[h][0:100, a, :].bitcast(I32), rows[shift : shift + 100, :].bitcast(I32))
+                nc.sync.dma_start(picked_sc[h][0:LIVE, a, :].bitcast(I32), rows[shift : shift + LIVE, :].bitcast(I32))
 
-        picked = {}
+        def pick_words(h, pairs):
+            for l in (SRC, DST):
+                nc.vector.tensor_copy(pairs[:, l, :], table[:].bitcast(U32).indirect(offsets(l, HALF * h, HALF * (h + 1))))
 
-        def pick_words(l, h, pairs):
-            nc.vector.tensor_copy(pairs, table[:].bitcast(U32).indirect(half_list(l, h)))
-
-        def part_words(parted, pairs):
+        def part_passes(parted, pairs):
             nc.vector.tensor_copy(parted.bitcast(U16), pairs.bitcast(U16).rearrange("p l (s a) -> p l a s", a=PASSES))
 
-        pick_scales(0, keep.tile([P, 2 * HALF], U8, name="rows0", align_bytes=64), nc.sync)
+        pick_scales(0, keep.tile([P, 2 * HALF], U8, name="rows0", align_bytes=64))
         for r in range(1, 4):
             nc.sync.dma_start(w4_sc[r:P:32].bitcast(I32), w4_sc[8 * r : P : 32].bitcast(I32))
-        raw_wa.append(load_pass(wa, 1, keep.tile([P, PACK, N], F32, name="raw_wa1", tag="raw_wa1", align_bytes=64), 0, N))
+        raw_wa1 = load_pass(wa, 1, keep.tile([P, PACK, N], F32, name="raw_wa1", tag="raw_wa1", align_bytes=64), 0, N)
         pairs0 = placed.tile([P, 5, HALF], U32, name="pairs0", offset=PAIRS0_AT, align_bytes=64)
+        pick_words(0, pairs0)
+        picked = [keep.tile([P, 2, PASSES, 2 * HALF], U8, name="picked0", align_bytes=64)]
         for l in (SRC, DST):
-            pick_words(l, 0, pairs0[:, l, :])
-        picked[0] = keep.tile([P, 2, PASSES, 2 * HALF], U8, name="picked0", align_bytes=64)
-        for l in (SRC, DST):
-            part_words(picked[0][:, l : l + 1], pairs0[:, l : l + 1, :])
+            part_passes(picked[0][:, l : l + 1], pairs0[:, l : l + 1, :])
         raw_wo0 = load_pass(wo, 0, placed.tile([P, PACK, N], F32, name="raw_wo0", offset=RAW_WO0_AT, align_bytes=64), 0, N)
         raw_wo1 = []
         for c in range(2):
             raw = placed.tile([P, PACK, PAIR], F32, name="raw_wo1_%d" % c, offset=RAW_WO1_AT[c], align_bytes=64)
             raw_wo1.append(load_pass(wo, 1, raw, PAIR * c, PAIR * (c + 1)))
-        pick_scales(1, placed.tile([P, 2 * HALF], U8, name="rows1", offset=ROWS1_AT, align_bytes=64), nc.sync)
-        pages.append(placed.tile([P, T], F32, name="page1", offset=PAGE1_AT, align_bytes=64))
+        pick_scales(1, placed.tile([P, 2 * HALF], U8, name="rows1", offset=ROWS1_AT, align_bytes=64))
+        pages[1] = placed.tile([P, T], F32, name="page1", offset=PAGE1_AT, align_bytes=64)
         nc.gpsimd.memset(pages[1][:].bitcast(I32), 0)
+        pages[3] = pages[0]
 
-        def mx_tiles(name, shape):
+        def mx_tiles(name, width):
             return (
-                keep.tile(shape, U32, name=name + "_codes", align_bytes=64),
-                keep.tile(shape, U8, name=name + "_scales", align_bytes=64),
+                keep.tile([P, PASSES, width], U32, name=name + "_codes", align_bytes=64),
+                keep.tile([P, PASSES, width], U8, name=name + "_scales", align_bytes=64),
             )
 
         def quantize(operand, a, cols, rounded):
             codes, scales = operand
             nc.vector.quantize_mx(out=codes[:, a, cols].bitcast(FP8X4), scales=scales[:, a, cols], in_=rounded)
 
-        def round_columns(rounded, raw):
-            nc.scalar.copy(
-                rounded.rearrange("p (c i j) -> p c j i", i=4, j=PACK), raw.rearrange("p j (c i) -> p c j i", i=4)
-            )
+        wa8 = mx_tiles("wa8", N)
 
-        wa8 = mx_tiles("wa8", [P, PASSES, N])
-        rounded = keep.tile([P, N * PACK], BF16, name="rounded_wa0", tag="rounded_wa0", align_bytes=64)
-        round_columns(rounded[:], raw_wa[0][:])
-        quantize(wa8, 0, slice(0, N), rounded[:])
-        pairs1 = [keep.tile([P, 1, HALF], U32, name="pairs1_src", tag="rounded_wa0", align_bytes=64)]
-        pick_words(SRC, 1, pairs1[SRC][:, 0, :])
-        rounded = placed.tile([P, N * PACK], BF16, name="rounded_wa1", offset=ROUNDED_WA1_AT, align_bytes=64)
-        round_columns(rounded[:], raw_wa[1][:])
-        quantize(wa8, 1, slice(0, N), rounded[:])
-        pairs1.append(placed.tile([P, 1, HALF], U32, name="pairs1_dst", offset=PAIRS1_DST_AT, align_bytes=64))
-        pick_words(DST, 1, pairs1[DST][:, 0, :])
-        gate = placed.tile([P, J], F32, name="gate", offset=GATE_AT, align_bytes=64)
+        def round_wa(a, raw):
+            rounded = keep.tile([P, N * PACK], BF16, name="rounded_wa%d" % a, tag="rounded_wa%d" % a, align_bytes=64)
+            nc.scalar.copy(rounded[:].rearrange("p (c i j) -> p c j i", i=4, j=PACK), raw[:].rearrange("p j (c i) -> p c j i", i=4))
+            quantize(wa8, a, slice(0, N), rounded[:])
+
+        round_wa(0, raw_wa0)
+        pairs1 = keep.tile([P, 2, HALF], U32, name="pairs1", tag="rounded_wa0", align_bytes=64)
+        pick_words(1, pairs1)
+        round_wa(1, raw_wa1)
+        gate = keep.tile([P, J], F32, name="gate", tag="rounded_wa1", align_bytes=64)
         nc.sync.dma_start(gate[:], wgo)
-        pages.append(page2)
-        pages.append(pages[0])
 
-        wo8_first = mx_tiles("wo8_first", [P, PASSES, PAIR])
-        rounded = keep.tile([P, PAIR * PACK], BF16, name="rounded_wo0", align_bytes=64)
-        nc.scalar.copy(
-            rounded[:].rearrange("p (m e j) -> p m j e", e=2, j=PACK),
-            raw_wo0[:].rearrange("p j (m u e) -> p u m j e", u=2, e=2)[:, 0],
-        )
-        quantize(wo8_first, 0, slice(0, PAIR), rounded[:])
-        rounded = placed.tile([P, PAIR * PACK], BF16, name="rounded_wo1", offset=ROUNDED_WO1_AT, align_bytes=64)
+        def pair_columns(raw, u):
+            return raw[:].rearrange("p j (m u e) -> p u m j e", u=2, e=2)[:, u]
+
+        wo8 = [mx_tiles("wo8_pair%d" % u, PAIR) for u in range(2)]
+
+        def round_first_pair(a, cols, raw, slot):
+            rounded = keep.tile([P, (cols.stop - cols.start) * PACK], BF16, name=slot, tag=slot, align_bytes=64)
+            nc.scalar.copy(rounded[:].rearrange("p (m e j) -> p m j e", e=2, j=PACK), pair_columns(raw, 0))
+            quantize(wo8[0], a, cols, rounded[:])
+
+        round_first_pair(0, slice(0, PAIR), raw_wo0, "rounded_wo0")
         for c in range(2):
-            part = rounded[:, P * PACK * c : P * PACK * (c + 1)]
-            nc.scalar.copy(
-                part.rearrange("p (m e j) -> p m j e", e=2, j=PACK),
-                raw_wo1[c][:].rearrange("p j (m u e) -> p u m j e", u=2, e=2)[:, 0],
-            )
-            quantize(wo8_first, 1, slice(P * c, P * (c + 1)), part)
-        picked[1] = placed.tile([P, 2, PASSES, 2 * HALF], U8, name="picked1", offset=PICKED1_AT, align_bytes=64)
-        for l in (SRC, DST):
-            part_words(picked[1][:, l : l + 1], pairs1[l][:])
+            round_first_pair(1, slice(P * c, P * (c + 1)), raw_wo1[c], "rounded_wo1_%d" % c)
+        picked.append(keep.tile([P, 2, PASSES, 2 * HALF], U8, name="picked1", tag="rounded_wo1_1", align_bytes=64))
+        part_passes(picked[1][:], pairs1[:])
 
-        wo8_second = mx_tiles("wo8_second", [P, PASSES, PAIR])
-
-        def round_second_planes():
-            both = keep.tile([P, PASSES, 2, P * PACK], BF16, name="rounded_wo_second", tag="eta3", align_bytes=64)
-            nc.scalar.copy(
-                both[:, 0].rearrange("p e (m j) -> p m j e", j=PACK),
-                raw_wo0[:].rearrange("p j (m u e) -> p u m j e", u=2, e=2)[:, 1],
-            )
+        def round_second_pair():
+            both = keep.tile([P, PASSES, 2, P * PACK], BF16, name="rounded_pair1", tag="eta3", align_bytes=64)
+            nc.scalar.copy(both[:, 0].rearrange("p e (m j) -> p m j e", j=PACK), pair_columns(raw_wo0, 1))
             for c in range(2):
                 nc.scalar.copy(
-                    both[:, 1, :, PAIR * c : PAIR * (c + 1)].rearrange("p e (m j) -> p m j e", j=PACK),
-                    raw_wo1[c][:].rearrange("p j (m u e) -> p u m j e", u=2, e=2)[:, 1],
+                    both[:, 1, :, PAIR * c : PAIR * (c + 1)].rearrange("p e (m j) -> p m j e", j=PACK), pair_columns(raw_wo1[c], 1)
                 )
-            codes, scales = wo8_second
+            codes, scales = wo8[1]
             nc.vector.quantize_mx(
                 out=codes[:].rearrange("p a c -> p (a c)").bitcast(FP8X4),
                 scales=scales[:].rearrange("p a c -> p (a c)"),
                 in_=both[:].rearrange("p a e c -> p (a e c)"),
             )
 
-        def mm(out, l, block, a, rhs, rhs_scale, start, stop):
-            h, b = divmod(block, HALF // P)
+        def mm(out, l, group, a, rhs, rhs_scale, start, stop):
+            h, b = divmod(group, HALF // P)
             nc.tensor.matmul_mx(
                 out=out,
                 lhsT=picked[h][:, l, a, 2 * P * b : 2 * P * (b + 1)].bitcast(FP4X4),
@@ -233,78 +204,112 @@ def tile_list_rgg_ownreluP_kernel(
                 stop=stop,
             )
 
-        msgs = []
-        for q in range(4):
-            if q == 1:
-                msgs.append(placed.tile([P, 2, PACK, P], F32, name="msg1", offset=MSG1_AT, align_bytes=64))
-            else:
-                msgs.append(keep.tile([P, 2, PACK, P], F32, name="msg%d" % q, align_bytes=64))
+        msgs = [keep.tile([P, 2, PACK, P], F32, name="msg%d" % q, align_bytes=64) for q in range(4)]
         results = keep.tile([P, PACK, J], F32, name="results", align_bytes=64)
-        staged = []
         out_rows = out_0.rearrange("(p i) t -> i p t", i=PACK)
+        gate_slots = ("rounded_wo0", "rounded_wo1_0", "rounded_wo1_0", "eta3")
 
-        def gated_message(block):
-            ms = psum.tile([P, N], F32, name="ms", tag="ms%d" % (block % 4))
-            za = psum.tile([P, N], F32, name="za", tag="za%d" % (block % 2))
+        def gated_message(group):
+            ms = psum.tile([P, N], F32, name="ms", tag="ms%d" % (group % 4))
+            za = psum.tile([P, N], F32, name="za", tag="za%d" % (group % 2))
             for out, w in ((ms, WC), (za, WB)):
                 for a in range(PASSES):
                     v = PASSES * w + a
-                    mm(out[:], SRC, block, a, w4[:, v, :].bitcast(FP4X4), w4_sc[:, v, :], a == 0, w == WC and a == PASSES - 1)
+                    mm(out[:], SRC, group, a, w4[:, v, :].bitcast(FP4X4), w4_sc[:, v, :], a == 0, w == WC and a == PASSES - 1)
             for a in range(PASSES):
-                mm(za[:], DST, block, a, wa8[0][:, a, :].bitcast(FP8X4), wa8[1][:, a, :], False, a == PASSES - 1)
-            if block == 3:
-                eta = keep.tile([P, PACK, P], F32, name="eta3", tag="eta3", align_bytes=64)
+                mm(za[:], DST, group, a, wa8[0][:, a, :].bitcast(FP8X4), wa8[1][:, a, :], False, a == PASSES - 1)
+            if group < len(gate_slots):
+                eta = keep.tile([P, PACK, P], F32, name="eta%d" % group, tag=gate_slots[group], align_bytes=64)
             else:
                 eta = ring.tile([P, PACK, P], F32, name="eta")
             nc.scalar.activation(eta[:], za[:].rearrange("p (m i) -> p i m", i=PACK), ACT.Sigmoid)
             nc.vector.tensor_tensor(
-                msgs[block // 2][:, block % 2], ms[:].rearrange("p (m i) -> p i m", i=PACK), eta[:], ALU.mult
+                msgs[group // 2][:, group % 2], ms[:].rearrange("p (m i) -> p i m", i=PACK), eta[:], ALU.mult
             )
 
-        held = {}
-
-        def project(unit, bank):
-            plane0, planes, block0, blocks = UNIT_LIST[unit]
-            codes, scales = wo8_first if plane0 == 0 else wo8_second
-            ow = psum.tile([P, blocks, planes * P], F32, name="ow", tag=bank)
+        def project(plane0, group0, bank, steps, own):
+            planes = steps[-1][1]
+            groups = PACK // planes
+            codes, scales = wo8[plane0 // 2]
+            ow = psum.tile([P, groups, planes * P], F32, name="ow", tag=bank)
             for a in range(PASSES):
                 for c in range(planes):
                     at = P * (plane0 % 2 + c)
-                    for b in range(blocks):
+                    for b in range(groups):
                         mm(
-                            ow[:, b, P * c : P * (c + 1)], DST, block0 + b, a,
+                            ow[:, b, P * c : P * (c + 1)], DST, group0 + b, a,
                             codes[:, a, at : at + P].bitcast(FP8X4), scales[:, a, at : at + P],
-                            a == 0 and c == 0 and b == 0, a == PASSES - 1 and c == planes - 1 and b == blocks - 1,
+                            a == 0 and c == 0 and b == 0, a == PASSES - 1 and c == planes - 1 and b == groups - 1,
                         )
-            if unit == 7:
-                own = placed.tile([P, 8 * blocks, planes, P], F32, name="own_held", offset=STAGED_AT, align_bytes=64)
-            else:
-                own = ring.tile([P, blocks, planes, P], F32, name="own", bufs=3)
-            steps = [(0, 1), (1, 2)] if unit == 0 else [(0, planes)]
             for first, last in steps:
-                nc.scalar.copy(own[:, 0:blocks, first:last], ow[:].rearrange("p b (m e) -> p b e m", e=planes)[:, :, first:last])
-            held[unit] = own
+                nc.scalar.copy(own[:, 0:groups, first:last], ow[:].rearrange("p b (m e) -> p b e m", e=planes)[:, :, first:last])
+            return plane0, group0, groups, own
+
+        def project_pair(q, bank, steps):
+            return project(0, 2 * q, bank, steps, ring.tile([P, 2, 2, P], F32, name="own", bufs=3))
+
+        def project_plane(i, h, bank):
+            return project(i, 4 * h, bank, [(0, 1)], ring.tile([P, 4, 1, P], F32, name="own", bufs=3))
 
         def turn(unit, first, last, bank):
-            plane0, planes, block0, blocks = UNIT_LIST[unit]
-            own = held[unit]
-            total = psum.tile([P, planes, blocks * P], F32, name="total", tag=bank)
-            edges = slice(P * block0, P * (block0 + blocks))
+            plane0, group0, groups, own = unit
+            total = psum.tile([P, PACK // groups, groups * P], F32, name="total", tag=bank)
             for e in range(first, last):
-                for b in range(blocks):
-                    block = block0 + b
-                    for s, summand in enumerate((own[:, b, e], msgs[block // 2][:, block % 2, plane0 + e])):
+                for b in range(groups):
+                    group = group0 + b
+                    for s, summand in enumerate((own[:, b, e], msgs[group // 2][:, group % 2, plane0 + e])):
                         nc.tensor.matmul(
                             total[:, e, P * b : P * (b + 1)], summand, ident[:], start=s == 0, stop=s == 1, is_transpose=True
                         )
+            edges = slice(P * group0, P * (group0 + groups))
             nc.scalar.activation(results[:, plane0 + first : plane0 + last, edges], total[:, first:last, :], ACT.Relu)
 
         def place(i, first, last):
             nc.vector.tensor_tensor(
-                pages[i][:].indirect(lists[DST][:, first // 16 : last // 16]), results[:, i, first:last], gate[:, first:last], ALU.mult
+                pages[i][:].indirect(offsets(DST, first, last)), results[:, i, first:last], gate[:, first:last], ALU.mult
             )
             if last == J:
                 nc.sync.dma_start(out_rows[i], pages[i][:])
+
+        def place_pair(q):
+            for i in range(2):
+                place(i, QUARTER * q, QUARTER * (q + 1))
+
+        for group in range(3):
+            gated_message(group)
+        unit = project_pair(0, "ow", [(0, 1), (1, 2)])
+        turn(unit, 0, 1, "total")
+        place(0, 0, QUARTER)
+        gated_message(3)
+        turn(unit, 1, 2, "total")
+        place(1, 0, QUARTER)
+        turn(project_pair(1, "ow", [(0, 2)]), 0, 2, "total")
+        round_second_pair()
+        place_pair(1)
+        gated_message(4)
+        gated_message(5)
+        turn(project_plane(2, 0, "ow"), 0, 1, "total")
+        place(2, 0, HALF)
+        gated_message(6)
+        gated_message(7)
+        turn(project_pair(2, "ow", [(0, 2)]), 0, 2, "total")
+        place_pair(2)
+        last_pair = project_pair(3, "ms0", [(0, 2)])
+        plane2 = project_plane(2, 1, "ms1")
+        turn(last_pair, 0, 2, "za0")
+        place_pair(3)
+        plane3_first = project_plane(3, 0, "ow")
+        wide_own = placed.tile([P, T * PACK * 2 // (P * 4), 1, P], F32, name="wide_own", offset=STAGED_AT, align_bytes=64)
+        plane3_second = project(3, 4, "ms0", [(0, 1)], wide_own)
+        turn(plane2, 0, 1, "total")
+        place(2, HALF, J)
+        turn(plane3_first, 0, 1, "za1")
+        turn(plane3_second, 0, 1, "za0")
+
+        staged = [
+            placed.tile([P, 2, WIDTHS[c], 2], BF16, name="staged%d" % c, offset=STAGED_AT + PACK * 2 * STARTS[c], align_bytes=64)
+            for c in range(CHUNKS)
+        ]
 
         def round_plane(i):
             u, e = divmod(i, 2)
@@ -315,44 +320,6 @@ def tile_list_rgg_ownreluP_kernel(
                 else:
                     nc.scalar.copy(staged[c][:, u, :, e], pages[i][:, cols])
 
-        for block in range(3):
-            gated_message(block)
-        project(0, "ow")
-        turn(0, 0, 1, "total")
-        place(0, 0, UNIT)
-        gated_message(3)
-        turn(0, 1, 2, "total")
-        place(1, 0, UNIT)
-        project(1, "ow")
-        turn(1, 0, 2, "total")
-        round_second_planes()
-        for i in range(2):
-            place(i, UNIT, 2 * UNIT)
-        gated_message(4)
-        gated_message(5)
-        project(4, "ow")
-        turn(4, 0, 1, "total")
-        place(2, 0, HALF)
-        gated_message(6)
-        gated_message(7)
-        project(2, "ow")
-        turn(2, 0, 2, "total")
-        for i in range(2):
-            place(i, 2 * UNIT, 3 * UNIT)
-        project(3, "ms0")
-        project(5, "ms1")
-        turn(3, 0, 2, "za0")
-        for i in range(2):
-            place(i, 3 * UNIT, J)
-        project(6, "ow")
-        project(7, "ms0")
-        turn(5, 0, 1, "total")
-        place(2, HALF, J)
-        turn(6, 0, 1, "za1")
-        turn(7, 0, 1, "za0")
-        for c in range(CHUNKS):
-            at = STAGED_AT + PACK * 2 * STARTS[c]
-            staged.append(placed.tile([P, 2, WIDTHS[c], 2], BF16, name="staged%d" % c, offset=at, align_bytes=64))
         round_plane(0)
         place(3, 0, J)
         for i in range(1, PACK):
@@ -382,4 +349,5 @@ def tile_list_rgg_ownreluP_kernel(
                 weave(c + 1)
             quantize_chunk(c)
         for q in range(QUADS):
-            (nc.scalar, nc.sync)[q % 2].dma_start(out_2[0, 4 * q : 4 * q + 4, :].bitcast(I32), y_sc[32 * q : 32 * q + 4, :].bitcast(I32))
+            queue = (nc.scalar, nc.sync)[q % 2]
+            queue.dma_start(out_2[0, 4 * q : 4 * q + 4, :].bitcast(I32), y_sc[32 * q : 32 * q + 4, :].bitcast(I32))

@@ -32,7 +32,7 @@ WB, WC = 0, 1
 WIDTHS = (256, 512, 512, 512, 256)
 STARTS = [sum(WIDTHS[:c]) for c in range(len(WIDTHS))]
 CHUNKS = len(WIDTHS)
-VECTOR_CHUNKS = 3
+SCALAR_CHUNK = 3
 
 KIB = 1024
 PAIRS0_AT = 8 * KIB
@@ -40,6 +40,9 @@ PAGE1_AT = PAIRS0_AT + 64 - 8 * KIB
 ROWS1_AT = PAIRS0_AT + 64
 RAW_WO1_AT = (ROWS1_AT + KIB, ROWS1_AT + 5 * KIB)
 RAW_WO0_AT = ROWS1_AT + 9 * KIB
+ROUNDED_WA0_AT = 50 * KIB
+PAGE2_AT = ROUNDED_WA0_AT + 64 - 8 * KIB
+PAIRS1_AT = ROUNDED_WA0_AT + 64
 STAGED_AT = 26 * KIB
 
 
@@ -61,8 +64,7 @@ def tile_list_rgg_ownreluP_kernel(
         w4_sc = keep.tile([P, 2 * PASSES, N], U8, name="w4_sc", align_bytes=64)
         ident = keep.tile([P, P], F32, name="ident", align_bytes=64)
 
-        pages = {2: keep.tile([P, T], F32, name="page2", align_bytes=64)}
-        nc.vector.memset(pages[2][:].bitcast(I32), 0)
+        pages = {}
         for q in range(QUADS):
             nc.gpsimd.memset(table_sc[32 * q : 32 * q + PARKED, :].bitcast(I32), 0)
         nc.gpsimd.memset(w4_sc[:].bitcast(I32), 0)
@@ -94,13 +96,13 @@ def tile_list_rgg_ownreluP_kernel(
         raw_wa0 = load_pass(wa, 0, keep.tile([P, PACK, N], F32, name="raw_wa0", align_bytes=64), 0, N)
 
         nc.gpsimd.memset(picked_sc[0][96:P].bitcast(I32), 0)
-        pages[0] = keep.tile([P, T], F32, name="page0", align_bytes=64)
-        nc.gpsimd.memset(pages[0][:].bitcast(I32), 0)
+        make_identity(nc, ident[:])
         warm = keep.tile([P, 2], F32, name="warm", tag="raw_wa1", align_bytes=64)
         nc.gpsimd.memset(warm[:, 0:1], 0.0)
         nc.scalar.activation(warm[:, 1:2], warm[:, 0:1], ACT.Sigmoid)
+        pages[0] = keep.tile([P, T], F32, name="page0", align_bytes=64)
+        nc.gpsimd.memset(pages[0][:].bitcast(I32), 0)
         nc.gpsimd.memset(picked_sc[1][96:P].bitcast(I32), 0)
-        make_identity(nc, ident[:])
 
         def offsets(l, first, last):
             return lists[l][:, first // 16 : last // 16]
@@ -150,15 +152,16 @@ def tile_list_rgg_ownreluP_kernel(
 
         wa8 = mx_tiles("wa8", N)
 
-        def round_wa(a, raw):
-            rounded = keep.tile([P, N * PACK], BF16, name="rounded_wa%d" % a, tag="rounded_wa%d" % a, align_bytes=64)
+        def round_wa(a, raw, rounded):
             nc.scalar.copy(rounded[:].rearrange("p (c i j) -> p c j i", i=4, j=PACK), raw[:].rearrange("p j (c i) -> p c j i", i=4))
             quantize(wa8, a, slice(0, N), rounded[:])
 
-        round_wa(0, raw_wa0)
-        pairs1 = keep.tile([P, 2, HALF], U32, name="pairs1", tag="rounded_wa0", align_bytes=64)
+        round_wa(0, raw_wa0, placed.tile([P, N * PACK], BF16, name="rounded_wa0", offset=ROUNDED_WA0_AT, align_bytes=64))
+        pairs1 = placed.tile([P, 2, HALF], U32, name="pairs1", offset=PAIRS1_AT, align_bytes=64)
         pick_words(1, pairs1)
-        round_wa(1, raw_wa1)
+        pages[2] = placed.tile([P, T], F32, name="page2", offset=PAGE2_AT, align_bytes=64)
+        nc.gpsimd.memset(pages[2][:].bitcast(I32), 0)
+        round_wa(1, raw_wa1, keep.tile([P, N * PACK], BF16, name="rounded_wa1", tag="rounded_wa1", align_bytes=64))
         gate = keep.tile([P, J], F32, name="gate", tag="rounded_wa1", align_bytes=64)
         nc.sync.dma_start(gate[:], wgo)
 
@@ -333,7 +336,7 @@ def tile_list_rgg_ownreluP_kernel(
         def weave(c):
             dst = woven[c][:].bitcast(U32).rearrange("p (g s u) -> p g u s", s=4, u=2)
             src = staged[c][:].rearrange("p u t e -> p u (t e)").bitcast(U32).rearrange("p u (g s) -> p g u s", s=4)
-            if c >= VECTOR_CHUNKS:
+            if c == SCALAR_CHUNK:
                 nc.scalar.copy(dst, src)
             else:
                 nc.vector.tensor_copy(dst.bitcast(I32), src.bitcast(I32))

@@ -38,8 +38,6 @@ KIB = 1024
 PAIRS0_AT = 8 * KIB
 PAGE1_AT = PAIRS0_AT + 64 - 8 * KIB
 ROWS1_AT = PAIRS0_AT + 64
-RAW_WO1_AT = (ROWS1_AT + KIB, ROWS1_AT + 5 * KIB)
-RAW_WO0_AT = ROWS1_AT + 9 * KIB
 ROUNDED_WA0_AT = 50 * KIB
 PAGE2_AT = ROUNDED_WA0_AT + 64 - 8 * KIB
 PAIRS1_AT = ROUNDED_WA0_AT + 64
@@ -81,25 +79,23 @@ def tile_list_rgg_ownreluP_kernel(
             nc.sync.dma_start(raw[:], weight[512 * a : 512 * (a + 1), first:last].rearrange("(p j) n -> p j n", j=PACK))
             return raw
 
-        def load_words(w):
-            nc.sync.dma_start(
-                w4[:, PASSES * w : PASSES * (w + 1), :].bitcast(I32),
-                (wb_words, wc_words)[w].rearrange("a p c -> p a c").bitcast(I32),
-            )
+        def load_words(w, a):
+            nc.sync.dma_start(w4[:, PASSES * w + a, :].bitcast(I32), (wb_words, wc_words)[w][a].bitcast(I32))
 
-        load_words(WC)
+        load_words(WC, 0)
         for w, scales in enumerate((wb_scales, wc_scales)):
             nc.sync.dma_start(
                 w4_sc[0:P:8, PASSES * w : PASSES * (w + 1), :].bitcast(I32), scales.rearrange("a s n -> s a n").bitcast(I32)
             )
-        load_words(WB)
+        load_words(WC, 1)
+        for a in range(PASSES):
+            load_words(WB, a)
         raw_wa0 = load_pass(wa, 0, keep.tile([P, PACK, N], F32, name="raw_wa0", align_bytes=64), 0, N)
 
         nc.gpsimd.memset(picked_sc[0][96:P].bitcast(I32), 0)
         make_identity(nc, ident[:])
-        warm = keep.tile([P, 2], F32, name="warm", tag="raw_wa1", align_bytes=64)
-        nc.gpsimd.memset(warm[:, 0:1], 0.0)
-        nc.scalar.activation(warm[:, 1:2], warm[:, 0:1], ACT.Sigmoid)
+        warm = keep.tile([P, 1], F32, name="warm", align_bytes=64)
+        nc.scalar.activation(warm[:], ident[:, 0:1], ACT.Sigmoid)
         pages[0] = keep.tile([P, T], F32, name="page0", align_bytes=64)
         nc.gpsimd.memset(pages[0][:].bitcast(I32), 0)
         nc.gpsimd.memset(picked_sc[1][96:P].bitcast(I32), 0)
@@ -124,16 +120,16 @@ def tile_list_rgg_ownreluP_kernel(
         pick_scales(0, keep.tile([P, 2 * HALF], U8, name="rows0", align_bytes=64))
         for r in range(1, 4):
             nc.sync.dma_start(w4_sc[r:P:32].bitcast(I32), w4_sc[8 * r : P : 32].bitcast(I32))
-        raw_wa1 = load_pass(wa, 1, keep.tile([P, PACK, N], F32, name="raw_wa1", tag="raw_wa1", align_bytes=64), 0, N)
-        pairs0 = placed.tile([P, 5, HALF], U32, name="pairs0", offset=PAIRS0_AT, align_bytes=64)
+        raw_wa1 = load_pass(wa, 1, keep.tile([P, PACK, N], F32, name="raw_wa1", align_bytes=64), 0, N)
+        pairs0 = placed.tile([P, 2, HALF], U32, name="pairs0", offset=PAIRS0_AT, align_bytes=64)
         pick_words(0, pairs0)
         picked = [keep.tile([P, 2, PASSES, 2 * HALF], U8, name="picked0", align_bytes=64)]
         for l in (SRC, DST):
             part_passes(picked[0][:, l : l + 1], pairs0[:, l : l + 1, :])
-        raw_wo0 = load_pass(wo, 0, placed.tile([P, PACK, N], F32, name="raw_wo0", offset=RAW_WO0_AT, align_bytes=64), 0, N)
+        raw_wo0 = load_pass(wo, 0, keep.tile([P, PACK, N], F32, name="raw_wo0", align_bytes=64), 0, N)
         raw_wo1 = []
         for c in range(2):
-            raw = placed.tile([P, PACK, PAIR], F32, name="raw_wo1_%d" % c, offset=RAW_WO1_AT[c], align_bytes=64)
+            raw = keep.tile([P, PACK, PAIR], F32, name="raw_wo1_%d" % c, align_bytes=64)
             raw_wo1.append(load_pass(wo, 1, raw, PAIR * c, PAIR * (c + 1)))
         pick_scales(1, placed.tile([P, 2 * HALF], U8, name="rows1", offset=ROWS1_AT, align_bytes=64))
         pages[1] = placed.tile([P, T], F32, name="page1", offset=PAGE1_AT, align_bytes=64)

@@ -28,6 +28,7 @@ QUARTER = J // 4
 PAIR = N // 2
 SRC, DST = 0, 1
 WB, WC = 0, 1
+EARLY_GROUPS = 4
 
 WIDTHS = (256, 512, 512, 512, 256)
 STARTS = [sum(WIDTHS[:c]) for c in range(len(WIDTHS))]
@@ -35,13 +36,13 @@ CHUNKS = len(WIDTHS)
 SCALAR_CHUNK = 3
 
 KIB = 1024
-PAIRS0_AT = 8 * KIB
-PAGE1_AT = PAIRS0_AT + 64 - 8 * KIB
-ROWS1_AT = PAIRS0_AT + 64
-ROUNDED_WA0_AT = 50 * KIB
-PAGE2_AT = ROUNDED_WA0_AT + 64 - 8 * KIB
-PAIRS1_AT = ROUNDED_WA0_AT + 64
-STAGED_AT = 26 * KIB
+PAIRS_S0_AT = 8 * KIB
+PAGE1_AT = PAIRS_S0_AT + 64 - 8 * KIB
+STAGED_AT = 12 * KIB
+ETA1_AT = 52 * KIB
+OWN_FIRST_AT = 64 * KIB
+WO0_AT = 70 * KIB
+TABLE_SC_AT = 40 * KIB
 
 
 def tile_list_rgg_ownreluP_kernel(
@@ -54,93 +55,110 @@ def tile_list_rgg_ownreluP_kernel(
         psum = ctx.enter_context(tc.psum_pool(name="psum", bufs=1))
         placed = ctx.enter_context(tc.tile_pool(name="placed", bufs=1))
 
-        lists = [keep.tile([P, J // 16], U16, name="src_list"), keep.tile([P, J // 16], U16, name="dst_list")]
-        table = keep.tile([P, T], I32, name="table", align_bytes=64)
-        table_sc = keep.tile([P, T], U8, name="table_sc", align_bytes=64)
-        picked_sc = [keep.tile([P, PASSES, 2 * HALF], U8, name="picked_sc%d" % h, align_bytes=64) for h in range(2)]
-        w4 = keep.tile([P, 2 * PASSES, 2 * N], U8, name="w4", align_bytes=64)
-        w4_sc = keep.tile([P, 2 * PASSES, N], U8, name="w4_sc", align_bytes=64)
-        ident = keep.tile([P, P], F32, name="ident", align_bytes=64)
+        def tile(shape, dtype, name, slot=None):
+            return keep.tile(shape, dtype, name=name, tag=slot or name, align_bytes=64)
 
-        pages = {}
+        lists = [keep.tile([P, J // 16], U16, name="src_list"), keep.tile([P, J // 16], U16, name="dst_list")]
+        table = tile([P, T], I32, "table")
+        table_sc = placed.tile([P, T], U8, name="table_sc", offset=TABLE_SC_AT, align_bytes=64)
+        picked_sc = [tile([P, PASSES, width], U8, "picked_sc%d" % width) for width in (HALF, HALF + J)]
+        w4 = tile([P, 2 * PASSES, 2 * N], U8, "w4")
+        w4_sc = tile([P, 2 * PASSES, N], U8, "w4_sc")
+        ident = tile([P, P], F32, "ident")
+
+        pages = {2: tile([P, T], F32, "page2")}
+        nc.vector.memset(pages[2][:].bitcast(I32), 0)
+        warm = tile([P, 2], F32, "warm")
+        nc.gpsimd.memset(warm[:, 0:1], 0.0)
+        nc.scalar.activation(warm[:, 1:2], warm[:, 0:1], ACT.Sigmoid)
         for q in range(QUADS):
             nc.gpsimd.memset(table_sc[32 * q : 32 * q + PARKED, :].bitcast(I32), 0)
         nc.gpsimd.memset(w4_sc[:].bitcast(I32), 0)
 
         nc.sync.dma_start(lists[SRC][:], offs)
-        nc.sync.dma_start(lists[DST][:], offs2)
         for q in range(QUADS):
             nc.sync.dma_start(
                 table_sc[32 * q + PARKED : 32 * (q + 1), :].bitcast(I32), tab_scales[:, 4 * q : 4 * q + 4, :].bitcast(I32)
             )
         nc.sync.dma_start(table[:], tab_words[0].rearrange("p t b -> p (t b)").bitcast(I32))
 
-        def load_pass(weight, a, raw, first, last):
+        def load_pass(weight, a, name, first, last, at=None):
+            if at is None:
+                raw = tile([P, PACK, last - first], F32, name)
+            else:
+                raw = placed.tile([P, PACK, last - first], F32, name=name, offset=at, align_bytes=64)
             nc.sync.dma_start(raw[:], weight[512 * a : 512 * (a + 1), first:last].rearrange("(p j) n -> p j n", j=PACK))
             return raw
 
-        def load_words(w, a):
-            nc.sync.dma_start(w4[:, PASSES * w + a, :].bitcast(I32), (wb_words, wc_words)[w][a].bitcast(I32))
+        def load_words(w):
+            words = (wb_words, wc_words)[w].rearrange("a p n -> p a n")
+            nc.sync.dma_start(w4[:, PASSES * w : PASSES * (w + 1), :].bitcast(I32), words.bitcast(I32))
 
-        load_words(WC, 0)
+        load_words(WC)
         for w, scales in enumerate((wb_scales, wc_scales)):
             nc.sync.dma_start(
                 w4_sc[0:P:8, PASSES * w : PASSES * (w + 1), :].bitcast(I32), scales.rearrange("a s n -> s a n").bitcast(I32)
             )
-        load_words(WC, 1)
-        for a in range(PASSES):
-            load_words(WB, a)
-        raw_wa0 = load_pass(wa, 0, keep.tile([P, PACK, N], F32, name="raw_wa0", align_bytes=64), 0, N)
+        load_words(WB)
+        nc.sync.dma_start(lists[DST][:], offs2)
+        raw_wa0 = load_pass(wa, 0, "raw_wa0", 0, N)
 
-        nc.gpsimd.memset(picked_sc[0][96:P].bitcast(I32), 0)
+        nc.gpsimd.memset(picked_sc[SRC][96:P].bitcast(I32), 0)
         make_identity(nc, ident[:])
-        warm = keep.tile([P, 1], F32, name="warm", align_bytes=64)
-        nc.scalar.activation(warm[:], ident[:, 0:1], ACT.Sigmoid)
-        pages[0] = keep.tile([P, T], F32, name="page0", align_bytes=64)
+        pages[0] = tile([P, T], F32, "page0")
         nc.gpsimd.memset(pages[0][:].bitcast(I32), 0)
-        nc.gpsimd.memset(picked_sc[1][96:P].bitcast(I32), 0)
+        nc.gpsimd.memset(picked_sc[DST][96:P].bitcast(I32), 0)
 
         def offsets(l, first, last):
             return lists[l][:, first // 16 : last // 16]
 
-        def pick_scales(h, rows):
-            for l in (SRC, DST):
-                nc.vector.tensor_copy(rows[:, HALF * l : HALF * (l + 1)], table_sc[:].indirect(offsets(l, HALF * h, HALF * (h + 1))))
+        def pick_scales(rows, l, first, last):
+            nc.vector.tensor_copy(rows, table_sc[:].indirect(offsets(l, first, last)))
+
+        def shift_scales(batch, rows):
             for a in range(PASSES):
                 shift = PARKED + 4 * a
-                nc.sync.dma_start(picked_sc[h][0:LIVE, a, :].bitcast(I32), rows[shift : shift + LIVE, :].bitcast(I32))
+                nc.sync.dma_start(picked_sc[batch][0:LIVE, a, :].bitcast(I32), rows[shift : shift + LIVE, :].bitcast(I32))
 
-        def pick_words(h, pairs):
-            for l in (SRC, DST):
-                nc.vector.tensor_copy(pairs[:, l, :], table[:].bitcast(U32).indirect(offsets(l, HALF * h, HALF * (h + 1))))
+        def scale_columns(l, group, a):
+            if l == SRC and group < HALF // P:
+                return picked_sc[0][:, a, P * group : P * (group + 1)]
+            at = HALF * l + P * group - (HALF if l == SRC else 0)
+            return picked_sc[1][:, a, at : at + P]
 
-        def part_passes(parted, pairs):
-            nc.vector.tensor_copy(parted.bitcast(U16), pairs.bitcast(U16).rearrange("p l (s a) -> p l a s", a=PASSES))
+        def pick_words(l, h, pairs):
+            nc.vector.tensor_copy(pairs[:, 0:HALF], table[:].bitcast(U32).indirect(offsets(l, HALF * h, HALF * (h + 1))))
+            return pairs
 
-        pick_scales(0, keep.tile([P, 2 * HALF], U8, name="rows0", align_bytes=64))
+        picked = {}
+
+        def part_passes(l, h, pairs, parted=None):
+            picked[l, h] = tile([P, PASSES, 2 * HALF], U8, "picked%d%d" % (l, h)) if parted is None else parted
+            nc.vector.tensor_copy(
+                picked[l, h][:].bitcast(U16), pairs[:, 0:HALF].bitcast(U16).rearrange("p (s a) -> p a s", a=PASSES)
+            )
+
+        rows_first = tile([P, HALF], U8, "rows_first")
+        pick_scales(rows_first[:], SRC, 0, HALF)
+        shift_scales(0, rows_first)
+        rows_rest = tile([P, HALF + J], U8, "rows_rest")
+        pick_scales(rows_rest[:, 0:HALF], SRC, HALF, J)
         for r in range(1, 4):
             nc.sync.dma_start(w4_sc[r:P:32].bitcast(I32), w4_sc[8 * r : P : 32].bitcast(I32))
-        raw_wa1 = load_pass(wa, 1, keep.tile([P, PACK, N], F32, name="raw_wa1", align_bytes=64), 0, N)
-        pairs0 = placed.tile([P, 2, HALF], U32, name="pairs0", offset=PAIRS0_AT, align_bytes=64)
-        pick_words(0, pairs0)
-        picked = [keep.tile([P, 2, PASSES, 2 * HALF], U8, name="picked0", align_bytes=64)]
-        for l in (SRC, DST):
-            part_passes(picked[0][:, l : l + 1], pairs0[:, l : l + 1, :])
-        raw_wo0 = load_pass(wo, 0, keep.tile([P, PACK, N], F32, name="raw_wo0", align_bytes=64), 0, N)
-        raw_wo1 = []
-        for c in range(2):
-            raw = keep.tile([P, PACK, PAIR], F32, name="raw_wo1_%d" % c, align_bytes=64)
-            raw_wo1.append(load_pass(wo, 1, raw, PAIR * c, PAIR * (c + 1)))
-        pick_scales(1, placed.tile([P, 2 * HALF], U8, name="rows1", offset=ROWS1_AT, align_bytes=64))
+        raw_wa1 = load_pass(wa, 1, "raw_wa1", 0, N)
+        pairs_s0 = placed.tile([P, HALF], U32, name="pairs_s0", offset=PAIRS_S0_AT, align_bytes=64)
+        part_passes(SRC, 0, pick_words(SRC, 0, pairs_s0))
+        raw_wo0 = load_pass(wo, 0, "raw_wo0", 0, N)
+        pick_scales(rows_rest[:, HALF:], DST, 0, J)
+        shift_scales(1, rows_rest)
+        raw_wo1 = [load_pass(wo, 1, "raw_wo1_%d" % c, PAIR * c, PAIR * (c + 1), TABLE_SC_AT + 64 + 4 * KIB * (c - 1)) for c in range(2)]
         pages[1] = placed.tile([P, T], F32, name="page1", offset=PAGE1_AT, align_bytes=64)
         nc.gpsimd.memset(pages[1][:].bitcast(I32), 0)
         pages[3] = pages[0]
+        pairs_d0 = pick_words(DST, 0, tile([P, HALF], U32, "pairs_d0"))
 
         def mx_tiles(name, width):
-            return (
-                keep.tile([P, PASSES, width], U32, name=name + "_codes", align_bytes=64),
-                keep.tile([P, PASSES, width], U8, name=name + "_scales", align_bytes=64),
-            )
+            return tile([P, PASSES, width], U32, name + "_codes"), tile([P, PASSES, width], U8, name + "_scales")
 
         def quantize(operand, a, cols, rounded):
             codes, scales = operand
@@ -148,17 +166,16 @@ def tile_list_rgg_ownreluP_kernel(
 
         wa8 = mx_tiles("wa8", N)
 
-        def round_wa(a, raw, rounded):
+        def round_wa(a, raw):
+            rounded = tile([P, N * PACK], BF16, "rounded_wa%d" % a)
             nc.scalar.copy(rounded[:].rearrange("p (c i j) -> p c j i", i=4, j=PACK), raw[:].rearrange("p j (c i) -> p c j i", i=4))
             quantize(wa8, a, slice(0, N), rounded[:])
 
-        round_wa(0, raw_wa0, placed.tile([P, N * PACK], BF16, name="rounded_wa0", offset=ROUNDED_WA0_AT, align_bytes=64))
-        pairs1 = placed.tile([P, 2, HALF], U32, name="pairs1", offset=PAIRS1_AT, align_bytes=64)
-        pick_words(1, pairs1)
-        pages[2] = placed.tile([P, T], F32, name="page2", offset=PAGE2_AT, align_bytes=64)
-        nc.gpsimd.memset(pages[2][:].bitcast(I32), 0)
-        round_wa(1, raw_wa1, keep.tile([P, N * PACK], BF16, name="rounded_wa1", tag="rounded_wa1", align_bytes=64))
-        gate = keep.tile([P, J], F32, name="gate", tag="rounded_wa1", align_bytes=64)
+        round_wa(0, raw_wa0)
+        part_passes(DST, 0, pairs_d0)
+        pairs_s1 = pick_words(SRC, 1, tile([P, HALF], U32, "pairs_s1", "rounded_wa0"))
+        round_wa(1, raw_wa1)
+        gate = tile([P, J], F32, "gate", "rounded_wa1")
         nc.sync.dma_start(gate[:], wgo)
 
         def pair_columns(raw, u):
@@ -166,19 +183,11 @@ def tile_list_rgg_ownreluP_kernel(
 
         wo8 = [mx_tiles("wo8_pair%d" % u, PAIR) for u in range(2)]
 
-        def round_first_pair(a, cols, raw, slot):
-            rounded = keep.tile([P, (cols.stop - cols.start) * PACK], BF16, name=slot, tag=slot, align_bytes=64)
+        def round_first_pair(a, cols, raw, rounded):
             nc.scalar.copy(rounded[:].rearrange("p (m e j) -> p m j e", e=2, j=PACK), pair_columns(raw, 0))
             quantize(wo8[0], a, cols, rounded[:])
 
-        round_first_pair(0, slice(0, PAIR), raw_wo0, "rounded_wo0")
-        for c in range(2):
-            round_first_pair(1, slice(P * c, P * (c + 1)), raw_wo1[c], "rounded_wo1_%d" % c)
-        picked.append(keep.tile([P, 2, PASSES, 2 * HALF], U8, name="picked1", tag="rounded_wo1_1", align_bytes=64))
-        part_passes(picked[1][:], pairs1[:])
-
-        def round_second_pair():
-            both = keep.tile([P, PASSES, 2, P * PACK], BF16, name="rounded_pair1", tag="eta3", align_bytes=64)
+        def round_second_pair(both):
             nc.scalar.copy(both[:, 0].rearrange("p e (m j) -> p m j e", j=PACK), pair_columns(raw_wo0, 1))
             for c in range(2):
                 nc.scalar.copy(
@@ -195,115 +204,153 @@ def tile_list_rgg_ownreluP_kernel(
             h, b = divmod(group, HALF // P)
             nc.tensor.matmul_mx(
                 out=out,
-                lhsT=picked[h][:, l, a, 2 * P * b : 2 * P * (b + 1)].bitcast(FP4X4),
-                lhsT_scale=picked_sc[h][:, a, HALF * l + P * b : HALF * l + P * (b + 1)],
+                lhsT=picked[l, h][:, a, 2 * P * b : 2 * P * (b + 1)].bitcast(FP4X4),
+                lhsT_scale=scale_columns(l, group, a),
                 rhs=rhs,
                 rhs_scale=rhs_scale,
                 start=start,
                 stop=stop,
             )
 
-        msgs = [keep.tile([P, 2, PACK, P], F32, name="msg%d" % q, align_bytes=64) for q in range(4)]
-        results = keep.tile([P, PACK, J], F32, name="results", align_bytes=64)
-        out_rows = out_0.rearrange("(p i) t -> i p t", i=PACK)
-        gate_slots = ("rounded_wo0", "rounded_wo1_0", "rounded_wo1_0", "eta3")
+        def bank(shape, name, b):
+            return psum.tile(shape, F32, name=name, tag="bank%d" % b)
 
-        def gated_message(group):
-            ms = psum.tile([P, N], F32, name="ms", tag="ms%d" % (group % 4))
-            za = psum.tile([P, N], F32, name="za", tag="za%d" % (group % 2))
+        msgs = {q: tile([P, 2, PACK, P], F32, "msg%d" % q) for q in (0, 2, 3)}
+        results = tile([P, PACK, J], F32, "results")
+        out_rows = out_0.rearrange("(p i) t -> i p t", i=PACK)
+
+        def source_passes(group, ms_bank, za_bank):
+            ms, za = bank([P, N], "ms", ms_bank), bank([P, N], "za", za_bank)
             for out, w in ((ms, WC), (za, WB)):
                 for a in range(PASSES):
                     v = PASSES * w + a
                     mm(out[:], SRC, group, a, w4[:, v, :].bitcast(FP4X4), w4_sc[:, v, :], a == 0, w == WC and a == PASSES - 1)
-            for a in range(PASSES):
-                mm(za[:], DST, group, a, wa8[0][:, a, :].bitcast(FP8X4), wa8[1][:, a, :], False, a == PASSES - 1)
-            if group < len(gate_slots):
-                eta = keep.tile([P, PACK, P], F32, name="eta%d" % group, tag=gate_slots[group], align_bytes=64)
-            else:
-                eta = ring.tile([P, PACK, P], F32, name="eta")
+            return group, ms, za
+
+        def target_pass(sums, a):
+            group, ms, za = sums
+            mm(za[:], DST, group, a, wa8[0][:, a, :].bitcast(FP8X4), wa8[1][:, a, :], False, a == PASSES - 1)
+
+        def message(sums, eta=None):
+            group, ms, za = sums
+            if eta is None:
+                eta = tile([P, PACK, P], F32, "eta%d" % group)
             nc.scalar.activation(eta[:], za[:].rearrange("p (m i) -> p i m", i=PACK), ACT.Sigmoid)
-            nc.vector.tensor_tensor(
-                msgs[group // 2][:, group % 2], ms[:].rearrange("p (m i) -> p i m", i=PACK), eta[:], ALU.mult
-            )
+            by_plane = ms[:].rearrange("p (m i) -> p i m", i=PACK)
+            if group < EARLY_GROUPS:
+                nc.vector.tensor_tensor(msgs[group // 2][:, group % 2], by_plane, eta[:], ALU.mult)
+            else:
+                plain = ring.tile([P, PACK, P], F32, name="plain")
+                nc.scalar.copy(plain[:], by_plane)
+                nc.gpsimd.tensor_tensor(msgs[group // 2][:, group % 2], plain[:], eta[:], ALU.mult)
 
-        def project(plane0, group0, bank, steps, own):
-            planes = steps[-1][1]
-            groups = PACK // planes
-            codes, scales = wo8[plane0 // 2]
-            ow = psum.tile([P, groups, planes * P], F32, name="ow", tag=bank)
+        def gate_sums(group, ms_bank, za_bank):
+            sums = source_passes(group, ms_bank, za_bank)
             for a in range(PASSES):
-                for c in range(planes):
-                    at = P * (plane0 % 2 + c)
-                    for b in range(groups):
-                        mm(
-                            ow[:, b, P * c : P * (c + 1)], DST, group0 + b, a,
-                            codes[:, a, at : at + P].bitcast(FP8X4), scales[:, a, at : at + P],
-                            a == 0 and c == 0 and b == 0, a == PASSES - 1 and c == planes - 1 and b == groups - 1,
-                        )
-            for first, last in steps:
-                nc.scalar.copy(own[:, 0:groups, first:last], ow[:].rearrange("p b (m e) -> p b e m", e=planes)[:, :, first:last])
-            return plane0, group0, groups, own
+                target_pass(sums, a)
+            return sums
 
-        def project_pair(q, bank, steps):
-            return project(0, 2 * q, bank, steps, ring.tile([P, 2, 2, P], F32, name="own", bufs=3))
+        def late_message(group, ms_bank, za_bank):
+            message(gate_sums(group, ms_bank, za_bank))
 
-        def project_plane(i, h, bank):
-            return project(i, 4 * h, bank, [(0, 1)], ring.tile([P, 4, 1, P], F32, name="own", bufs=3))
+        def at(shape, dtype, name, offset):
+            return placed.tile(shape, dtype, name=name, offset=offset, align_bytes=64)
 
-        def turn(unit, first, last, bank):
+        def project_pair(q, b, parts=None):
+            codes, scales = wo8[0]
+            ow = bank([P, 2, PAIR], "ow", b)
+            for a in range(PASSES):
+                for g in range(2):
+                    mm(ow[:, g, :], DST, 2 * q + g, a, codes[:, a, :].bitcast(FP8X4), scales[:, a, :], a == 0 and g == 0, a == PASSES - 1 and g == 1)
+            by_plane = ow[:].rearrange("p g (m e) -> p g e m", e=2)
+            if parts is None:
+                own = ring.tile([P, 2, 2, P], F32, name="own", bufs=3)
+                nc.scalar.copy(own[:], by_plane)
+                return 0, 2 * q, 2, [own[:, :, e] for e in range(2)]
+            for e in range(2):
+                nc.scalar.copy(parts[e][:], by_plane[:, :, e])
+            return 0, 2 * q, 2, parts
+
+        def project_plane(i, h, b, own=None):
+            codes, scales = wo8[1]
+            ow = bank([P, 4, P], "ow", b)
+            if own is None:
+                own = ring.tile([P, 4, 1, P], F32, name="own", bufs=3)
+            cols = slice(P * (i % 2), P * (i % 2 + 1))
+            for a in range(PASSES):
+                for g in range(4):
+                    mm(ow[:, g, :], DST, 4 * h + g, a, codes[:, a, cols].bitcast(FP8X4), scales[:, a, cols], a == 0 and g == 0, a == PASSES - 1 and g == 3)
+            nc.scalar.copy(own[:, 0:4, 0], ow[:])
+            return i, 4 * h, 4, [own[:, :, 0]]
+
+        def turn(unit, first, last, b):
             plane0, group0, groups, own = unit
-            total = psum.tile([P, PACK // groups, groups * P], F32, name="total", tag=bank)
+            total = bank([P, PACK // groups, groups * P], "total", b)
             for e in range(first, last):
-                for b in range(groups):
-                    group = group0 + b
-                    for s, summand in enumerate((own[:, b, e], msgs[group // 2][:, group % 2, plane0 + e])):
+                for g in range(groups):
+                    group = group0 + g
+                    for s, summand in enumerate((own[e][:, g], msgs[group // 2][:, group % 2, plane0 + e])):
                         nc.tensor.matmul(
-                            total[:, e, P * b : P * (b + 1)], summand, ident[:], start=s == 0, stop=s == 1, is_transpose=True
+                            total[:, e, P * g : P * (g + 1)], summand, ident[:], start=s == 0, stop=s == 1, is_transpose=True
                         )
             edges = slice(P * group0, P * (group0 + groups))
             nc.scalar.activation(results[:, plane0 + first : plane0 + last, edges], total[:, first:last, :], ACT.Relu)
 
-        def place(i, first, last):
-            nc.vector.tensor_tensor(
-                pages[i][:].indirect(offsets(DST, first, last)), results[:, i, first:last], gate[:, first:last], ALU.mult
-            )
+        def place(i, first, last, weighted=None):
+            window = pages[i][:].indirect(offsets(DST, first, last))
+            if weighted is None:
+                nc.vector.tensor_tensor(window, results[:, i, first:last], gate[:, first:last], ALU.mult)
+            else:
+                nc.gpsimd.tensor_tensor(weighted[:], results[:, i, first:last], gate[:, first:last], ALU.mult)
+                nc.vector.tensor_copy(window, weighted[:])
             if last == J:
                 nc.sync.dma_start(out_rows[i], pages[i][:])
 
-        def place_pair(q):
-            for i in range(2):
-                place(i, QUARTER * q, QUARTER * (q + 1))
+        def weigh(i, first, last):
+            place(i, first, last, tile([P, last - first], F32, "weighted%d_%d" % (i, first)))
 
-        for group in range(3):
-            gated_message(group)
-        unit = project_pair(0, "ow", [(0, 1), (1, 2)])
-        turn(unit, 0, 1, "total")
-        place(0, 0, QUARTER)
-        gated_message(3)
-        turn(unit, 1, 2, "total")
-        place(1, 0, QUARTER)
-        turn(project_pair(1, "ow", [(0, 2)]), 0, 2, "total")
-        round_second_pair()
-        place_pair(1)
-        gated_message(4)
-        gated_message(5)
-        turn(project_plane(2, 0, "ow"), 0, 1, "total")
-        place(2, 0, HALF)
-        gated_message(6)
-        gated_message(7)
-        turn(project_pair(2, "ow", [(0, 2)]), 0, 2, "total")
-        place_pair(2)
-        last_pair = project_pair(3, "ms0", [(0, 2)])
-        plane2 = project_plane(2, 1, "ms1")
-        turn(last_pair, 0, 2, "za0")
-        place_pair(3)
-        plane3_first = project_plane(3, 0, "ow")
+        sums = [gate_sums(g, g, 4 + g) for g in range(2)]
+        round_first_pair(0, slice(0, PAIR), raw_wo0, at([P, PAIR * PACK], BF16, "rounded_wo0", WO0_AT))
+        part_passes(SRC, 1, pairs_s1, at([P, PASSES, 2 * HALF], U8, "picked_s1", WO0_AT + 64 - 2 * KIB))
+        message(sums[0], at([P, PACK, P], F32, "eta0", WO0_AT + 64))
+        round_first_pair(1, slice(0, P), raw_wo1[0], tile([P, P * PACK], BF16, "rounded_wo1_0"))
+        message(sums[1], at([P, PACK, P], F32, "eta1", ETA1_AT))
+        round_first_pair(1, slice(P, 2 * P), raw_wo1[1], at([P, 2 * P * PACK], BF16, "rounded_wo1_1", ETA1_AT + 2 * KIB)[:, 0 : P * PACK])
+        pairs_d1 = pick_words(DST, 1, at([P, HALF], U32, "pairs_d1", ETA1_AT + 3 * KIB // 2))
+        unit = project_pair(0, 6, [at([P, 2, P], F32, "own_first0", OWN_FIRST_AT), at([P, 2, P], F32, "own_first1", OWN_FIRST_AT - KIB)])
+        turn(unit, 0, 1, 7)
+        part_passes(DST, 1, pairs_d1, at([P, PASSES, 2 * HALF], U8, "picked_d1", OWN_FIRST_AT + 64))
+        msgs[1] = at([P, 2, PACK, P], F32, "msg1", ETA1_AT + 3 * KIB // 2 + 64 - 4 * KIB)
+        message(gate_sums(2, 2, 4), at([P, PACK, P], F32, "eta2", ETA1_AT + 7 * KIB // 2))
+        message(gate_sums(3, 3, 5))
+        place(0, 0, QUARTER, at([P, QUARTER], F32, "weighted_first", ETA1_AT + 2 * KIB))
+        round_second_pair(at([P, PASSES, 2, P * PACK], BF16, "rounded_pair1", OWN_FIRST_AT + 64 - 5 * KIB))
+        turn(unit, 1, 2, 0)
+        weigh(1, 0, QUARTER)
+        turn(project_pair(1, 1), 0, 2, 2)
+        for i in range(2):
+            weigh(i, QUARTER, HALF)
+        late_message(4, 7, 6)
+        plane2 = project_plane(2, 0, 3)
+        late_message(5, 0, 4)
+        turn(plane2, 0, 1, 5)
+        weigh(2, 0, HALF)
+        late_message(6, 7, 6)
+        turn(project_pair(2, 3), 0, 2, 2)
+        late_message(7, 0, 4)
+        weigh(0, HALF, 3 * QUARTER)
+        place(1, HALF, 3 * QUARTER)
+        turn(project_pair(3, 3), 0, 2, 5)
+        for i in range(2):
+            place(i, 3 * QUARTER, J)
+        plane2 = project_plane(2, 1, 0)
+        plane3_first = project_plane(3, 0, 4)
         wide_own = placed.tile([P, T * PACK * 2 // (P * 4), 1, P], F32, name="wide_own", offset=STAGED_AT, align_bytes=64)
-        plane3_second = project(3, 4, "ms0", [(0, 1)], wide_own)
-        turn(plane2, 0, 1, "total")
+        plane3_second = project_plane(3, 1, 3, wide_own)
+        turn(plane2, 0, 1, 1)
         place(2, HALF, J)
-        turn(plane3_first, 0, 1, "za1")
-        turn(plane3_second, 0, 1, "za0")
+        turn(plane3_first, 0, 1, 7)
+        turn(plane3_second, 0, 1, 6)
 
         staged = [
             placed.tile([P, 2, WIDTHS[c], 2], BF16, name="staged%d" % c, offset=STAGED_AT + PACK * 2 * STARTS[c], align_bytes=64)
@@ -324,10 +371,10 @@ def tile_list_rgg_ownreluP_kernel(
         for i in range(1, PACK):
             round_plane(i)
 
-        y_sc = keep.tile([P, T], U8, name="y_sc", align_bytes=64)
+        y_sc = tile([P, T], U8, "y_sc")
         words_out = out_1[0].rearrange("p t b -> p (t b)").bitcast(I32)
-        woven = [keep.tile([P, WIDTHS[c] * PACK], BF16, name="woven%d" % c, align_bytes=64) for c in range(CHUNKS)]
-        y_codes = [keep.tile([P, WIDTHS[c]], I32, name="y_codes%d" % c, align_bytes=64) for c in range(CHUNKS)]
+        woven = [tile([P, WIDTHS[c] * PACK], BF16, "woven%d" % c) for c in range(CHUNKS)]
+        y_codes = [tile([P, WIDTHS[c]], I32, "y_codes%d" % c) for c in range(CHUNKS)]
 
         def weave(c):
             dst = woven[c][:].bitcast(U32).rearrange("p (g s u) -> p g u s", s=4, u=2)

@@ -36,13 +36,11 @@ CHUNKS = len(WIDTHS)
 SCALAR_CHUNK = 3
 
 KIB = 1024
-PAIRS_S0_AT = 8 * KIB
-PAGE1_AT = PAIRS_S0_AT + 64 - 8 * KIB
-STAGED_AT = 12 * KIB
-ETA1_AT = 52 * KIB
-OWN_FIRST_AT = 64 * KIB
-WO0_AT = 70 * KIB
-TABLE_SC_AT = 40 * KIB
+PAIRS0_AT = 8 * KIB
+STAGED_AT = 13 * KIB
+ROUNDED_WA0_AT = 38 * KIB
+LAST_WO_AT = 47 * KIB
+OWN_FIRST_AT = 54 * KIB
 
 
 def tile_list_rgg_ownreluP_kernel(
@@ -58,104 +56,88 @@ def tile_list_rgg_ownreluP_kernel(
         def tile(shape, dtype, name, slot=None):
             return keep.tile(shape, dtype, name=name, tag=slot or name, align_bytes=64)
 
+        def at(shape, dtype, name, offset):
+            return placed.tile(shape, dtype, name=name, offset=offset, align_bytes=64)
+
         lists = [keep.tile([P, J // 16], U16, name="src_list"), keep.tile([P, J // 16], U16, name="dst_list")]
         table = tile([P, T], I32, "table")
-        table_sc = placed.tile([P, T], U8, name="table_sc", offset=TABLE_SC_AT, align_bytes=64)
-        picked_sc = [tile([P, PASSES, width], U8, "picked_sc%d" % width) for width in (HALF, HALF + J)]
+        table_sc = tile([P, T], U8, "table_sc")
+        picked_sc = [tile([P, PASSES, 2 * HALF], U8, "picked_sc%d" % h) for h in range(2)]
         w4 = tile([P, 2 * PASSES, 2 * N], U8, "w4")
         w4_sc = tile([P, 2 * PASSES, N], U8, "w4_sc")
         ident = tile([P, P], F32, "ident")
 
-        pages = {2: tile([P, T], F32, "page2")}
-        nc.vector.memset(pages[2][:].bitcast(I32), 0)
-        warm = tile([P, 2], F32, "warm")
-        nc.gpsimd.memset(warm[:, 0:1], 0.0)
-        nc.scalar.activation(warm[:, 1:2], warm[:, 0:1], ACT.Sigmoid)
+        pages = {}
         for q in range(QUADS):
             nc.gpsimd.memset(table_sc[32 * q : 32 * q + PARKED, :].bitcast(I32), 0)
         nc.gpsimd.memset(w4_sc[:].bitcast(I32), 0)
 
         nc.sync.dma_start(lists[SRC][:], offs)
+        nc.sync.dma_start(lists[DST][:], offs2)
         for q in range(QUADS):
             nc.sync.dma_start(
                 table_sc[32 * q + PARKED : 32 * (q + 1), :].bitcast(I32), tab_scales[:, 4 * q : 4 * q + 4, :].bitcast(I32)
             )
         nc.sync.dma_start(table[:], tab_words[0].rearrange("p t b -> p (t b)").bitcast(I32))
 
-        def load_pass(weight, a, name, first, last, at=None):
-            if at is None:
-                raw = tile([P, PACK, last - first], F32, name)
-            else:
-                raw = placed.tile([P, PACK, last - first], F32, name=name, offset=at, align_bytes=64)
+        def load_pass(weight, a, name, first, last):
+            raw = tile([P, PACK, last - first], F32, name)
             nc.sync.dma_start(raw[:], weight[512 * a : 512 * (a + 1), first:last].rearrange("(p j) n -> p j n", j=PACK))
             return raw
 
-        def load_words(w):
-            words = (wb_words, wc_words)[w].rearrange("a p n -> p a n")
-            nc.sync.dma_start(w4[:, PASSES * w : PASSES * (w + 1), :].bitcast(I32), words.bitcast(I32))
+        def load_words(w, a):
+            nc.sync.dma_start(w4[:, PASSES * w + a, :].bitcast(I32), (wb_words, wc_words)[w][a].bitcast(I32))
 
-        load_words(WC)
+        load_words(WC, 0)
         for w, scales in enumerate((wb_scales, wc_scales)):
             nc.sync.dma_start(
                 w4_sc[0:P:8, PASSES * w : PASSES * (w + 1), :].bitcast(I32), scales.rearrange("a s n -> s a n").bitcast(I32)
             )
-        load_words(WB)
-        nc.sync.dma_start(lists[DST][:], offs2)
+        load_words(WC, 1)
+        for a in range(PASSES):
+            load_words(WB, a)
         raw_wa0 = load_pass(wa, 0, "raw_wa0", 0, N)
 
-        nc.gpsimd.memset(picked_sc[SRC][96:P].bitcast(I32), 0)
+        nc.gpsimd.memset(picked_sc[0][96:P].bitcast(I32), 0)
         make_identity(nc, ident[:])
+        warm = tile([P, 1], F32, "warm")
+        nc.scalar.activation(warm[:], ident[:, 0:1], ACT.Sigmoid)
         pages[0] = tile([P, T], F32, "page0")
         nc.gpsimd.memset(pages[0][:].bitcast(I32), 0)
-        nc.gpsimd.memset(picked_sc[DST][96:P].bitcast(I32), 0)
+        nc.gpsimd.memset(picked_sc[1][96:P].bitcast(I32), 0)
 
         def offsets(l, first, last):
             return lists[l][:, first // 16 : last // 16]
 
-        def pick_scales(rows, l, first, last):
-            nc.vector.tensor_copy(rows, table_sc[:].indirect(offsets(l, first, last)))
-
-        def shift_scales(batch, rows):
+        def pick_scales(h, rows):
+            for l in (SRC, DST):
+                nc.vector.tensor_copy(rows[:, HALF * l : HALF * (l + 1)], table_sc[:].indirect(offsets(l, HALF * h, HALF * (h + 1))))
             for a in range(PASSES):
                 shift = PARKED + 4 * a
-                nc.sync.dma_start(picked_sc[batch][0:LIVE, a, :].bitcast(I32), rows[shift : shift + LIVE, :].bitcast(I32))
+                nc.sync.dma_start(picked_sc[h][0:LIVE, a, :].bitcast(I32), rows[shift : shift + LIVE, :].bitcast(I32))
 
-        def scale_columns(l, group, a):
-            if l == SRC and group < HALF // P:
-                return picked_sc[0][:, a, P * group : P * (group + 1)]
-            at = HALF * l + P * group - (HALF if l == SRC else 0)
-            return picked_sc[1][:, a, at : at + P]
+        def pick_words(h, pairs):
+            for l in (SRC, DST):
+                nc.vector.tensor_copy(pairs[:, l, :], table[:].bitcast(U32).indirect(offsets(l, HALF * h, HALF * (h + 1))))
 
-        def pick_words(l, h, pairs):
-            nc.vector.tensor_copy(pairs[:, 0:HALF], table[:].bitcast(U32).indirect(offsets(l, HALF * h, HALF * (h + 1))))
-            return pairs
+        def part_passes(parted, pairs):
+            nc.vector.tensor_copy(parted.bitcast(U16), pairs.bitcast(U16).rearrange("p l (s a) -> p l a s", a=PASSES))
 
-        picked = {}
-
-        def part_passes(l, h, pairs, parted=None):
-            picked[l, h] = tile([P, PASSES, 2 * HALF], U8, "picked%d%d" % (l, h)) if parted is None else parted
-            nc.vector.tensor_copy(
-                picked[l, h][:].bitcast(U16), pairs[:, 0:HALF].bitcast(U16).rearrange("p (s a) -> p a s", a=PASSES)
-            )
-
-        rows_first = tile([P, HALF], U8, "rows_first")
-        pick_scales(rows_first[:], SRC, 0, HALF)
-        shift_scales(0, rows_first)
-        rows_rest = tile([P, HALF + J], U8, "rows_rest")
-        pick_scales(rows_rest[:, 0:HALF], SRC, HALF, J)
+        pick_scales(0, tile([P, 2 * HALF], U8, "rows0"))
         for r in range(1, 4):
             nc.sync.dma_start(w4_sc[r:P:32].bitcast(I32), w4_sc[8 * r : P : 32].bitcast(I32))
         raw_wa1 = load_pass(wa, 1, "raw_wa1", 0, N)
-        pairs_s0 = placed.tile([P, HALF], U32, name="pairs_s0", offset=PAIRS_S0_AT, align_bytes=64)
-        part_passes(SRC, 0, pick_words(SRC, 0, pairs_s0))
+        pairs0 = at([P, 2, HALF], U32, "pairs0", PAIRS0_AT)
+        pick_words(0, pairs0)
+        picked = [tile([P, 2, PASSES, 2 * HALF], U8, "picked0")]
+        for l in (SRC, DST):
+            part_passes(picked[0][:, l : l + 1], pairs0[:, l : l + 1, :])
         raw_wo0 = load_pass(wo, 0, "raw_wo0", 0, N)
-        pick_scales(rows_rest[:, HALF:], DST, 0, J)
-        shift_scales(1, rows_rest)
-        raw_wo1 = [load_pass(wo, 1, "raw_wo1_%d" % c, PAIR * c, PAIR * (c + 1), TABLE_SC_AT + 64 + 4 * KIB * (c - 1)) for c in range(2)]
-        pages[1] = placed.tile([P, T], F32, name="page1", offset=PAGE1_AT, align_bytes=64)
+        raw_wo1 = [load_pass(wo, 1, "raw_wo1_%d" % c, PAIR * c, PAIR * (c + 1)) for c in range(2)]
+        pick_scales(1, at([P, 2 * HALF], U8, "rows1", PAIRS0_AT + 64))
+        pages[1] = at([P, T], F32, "page1", PAIRS0_AT + 64 - 8 * KIB)
         nc.gpsimd.memset(pages[1][:].bitcast(I32), 0)
         pages[3] = pages[0]
-        pairs_d0 = pick_words(DST, 0, tile([P, HALF], U32, "pairs_d0"))
 
         def mx_tiles(name, width):
             return tile([P, PASSES, width], U32, name + "_codes"), tile([P, PASSES, width], U8, name + "_scales")
@@ -166,15 +148,16 @@ def tile_list_rgg_ownreluP_kernel(
 
         wa8 = mx_tiles("wa8", N)
 
-        def round_wa(a, raw):
-            rounded = tile([P, N * PACK], BF16, "rounded_wa%d" % a)
+        def round_wa(a, raw, rounded):
             nc.scalar.copy(rounded[:].rearrange("p (c i j) -> p c j i", i=4, j=PACK), raw[:].rearrange("p j (c i) -> p c j i", i=4))
             quantize(wa8, a, slice(0, N), rounded[:])
 
-        round_wa(0, raw_wa0)
-        part_passes(DST, 0, pairs_d0)
-        pairs_s1 = pick_words(SRC, 1, tile([P, HALF], U32, "pairs_s1", "rounded_wa0"))
-        round_wa(1, raw_wa1)
+        round_wa(0, raw_wa0, at([P, N * PACK], BF16, "rounded_wa0", ROUNDED_WA0_AT))
+        pairs1 = at([P, 2, HALF], U32, "pairs1", ROUNDED_WA0_AT + 64)
+        pick_words(1, pairs1)
+        pages[2] = at([P, T], F32, "page2", ROUNDED_WA0_AT + 64 - 8 * KIB)
+        nc.gpsimd.memset(pages[2][:].bitcast(I32), 0)
+        round_wa(1, raw_wa1, tile([P, N * PACK], BF16, "rounded_wa1"))
         gate = tile([P, J], F32, "gate", "rounded_wa1")
         nc.sync.dma_start(gate[:], wgo)
 
@@ -187,25 +170,12 @@ def tile_list_rgg_ownreluP_kernel(
             nc.scalar.copy(rounded[:].rearrange("p (m e j) -> p m j e", e=2, j=PACK), pair_columns(raw, 0))
             quantize(wo8[0], a, cols, rounded[:])
 
-        def round_second_pair(both):
-            nc.scalar.copy(both[:, 0].rearrange("p e (m j) -> p m j e", j=PACK), pair_columns(raw_wo0, 1))
-            for c in range(2):
-                nc.scalar.copy(
-                    both[:, 1, :, PAIR * c : PAIR * (c + 1)].rearrange("p e (m j) -> p m j e", j=PACK), pair_columns(raw_wo1[c], 1)
-                )
-            codes, scales = wo8[1]
-            nc.vector.quantize_mx(
-                out=codes[:].rearrange("p a c -> p (a c)").bitcast(FP8X4),
-                scales=scales[:].rearrange("p a c -> p (a c)"),
-                in_=both[:].rearrange("p a e c -> p (a e c)"),
-            )
-
         def mm(out, l, group, a, rhs, rhs_scale, start, stop):
             h, b = divmod(group, HALF // P)
             nc.tensor.matmul_mx(
                 out=out,
-                lhsT=picked[l, h][:, a, 2 * P * b : 2 * P * (b + 1)].bitcast(FP4X4),
-                lhsT_scale=scale_columns(l, group, a),
+                lhsT=picked[h][:, l, a, 2 * P * b : 2 * P * (b + 1)].bitcast(FP4X4),
+                lhsT_scale=picked_sc[h][:, a, HALF * l + P * b : HALF * l + P * (b + 1)],
                 rhs=rhs,
                 rhs_scale=rhs_scale,
                 start=start,
@@ -215,7 +185,7 @@ def tile_list_rgg_ownreluP_kernel(
         def bank(shape, name, b):
             return psum.tile(shape, F32, name=name, tag="bank%d" % b)
 
-        msgs = {q: tile([P, 2, PACK, P], F32, "msg%d" % q) for q in (0, 2, 3)}
+        msgs = {q: tile([P, 2, PACK, P], F32, "msg%d" % q) for q in range(4)}
         results = tile([P, PACK, J], F32, "results")
         out_rows = out_0.rearrange("(p i) t -> i p t", i=PACK)
 
@@ -231,7 +201,7 @@ def tile_list_rgg_ownreluP_kernel(
             group, ms, za = sums
             mm(za[:], DST, group, a, wa8[0][:, a, :].bitcast(FP8X4), wa8[1][:, a, :], False, a == PASSES - 1)
 
-        def message(sums, eta=None):
+        def message(sums, eta=None, plain=None):
             group, ms, za = sums
             if eta is None:
                 eta = tile([P, PACK, P], F32, "eta%d" % group)
@@ -240,7 +210,8 @@ def tile_list_rgg_ownreluP_kernel(
             if group < EARLY_GROUPS:
                 nc.vector.tensor_tensor(msgs[group // 2][:, group % 2], by_plane, eta[:], ALU.mult)
             else:
-                plain = ring.tile([P, PACK, P], F32, name="plain")
+                if plain is None:
+                    plain = ring.tile([P, PACK, P], F32, name="plain")
                 nc.scalar.copy(plain[:], by_plane)
                 nc.gpsimd.tensor_tensor(msgs[group // 2][:, group % 2], plain[:], eta[:], ALU.mult)
 
@@ -252,9 +223,6 @@ def tile_list_rgg_ownreluP_kernel(
 
         def late_message(group, ms_bank, za_bank):
             message(gate_sums(group, ms_bank, za_bank))
-
-        def at(shape, dtype, name, offset):
-            return placed.tile(shape, dtype, name=name, offset=offset, align_bytes=64)
 
         def project_pair(q, b, parts=None):
             codes, scales = wo8[0]
@@ -310,47 +278,53 @@ def tile_list_rgg_ownreluP_kernel(
             place(i, first, last, tile([P, last - first], F32, "weighted%d_%d" % (i, first)))
 
         sums = [gate_sums(g, g, 4 + g) for g in range(2)]
-        round_first_pair(0, slice(0, PAIR), raw_wo0, at([P, PAIR * PACK], BF16, "rounded_wo0", WO0_AT))
-        part_passes(SRC, 1, pairs_s1, at([P, PASSES, 2 * HALF], U8, "picked_s1", WO0_AT + 64 - 2 * KIB))
-        message(sums[0], at([P, PACK, P], F32, "eta0", WO0_AT + 64))
+        round_first_pair(0, slice(0, PAIR), raw_wo0, tile([P, PAIR * PACK], BF16, "rounded_wo0"))
         round_first_pair(1, slice(0, P), raw_wo1[0], tile([P, P * PACK], BF16, "rounded_wo1_0"))
-        message(sums[1], at([P, PACK, P], F32, "eta1", ETA1_AT))
-        round_first_pair(1, slice(P, 2 * P), raw_wo1[1], at([P, 2 * P * PACK], BF16, "rounded_wo1_1", ETA1_AT + 2 * KIB)[:, 0 : P * PACK])
-        pairs_d1 = pick_words(DST, 1, at([P, HALF], U32, "pairs_d1", ETA1_AT + 3 * KIB // 2))
-        unit = project_pair(0, 6, [at([P, 2, P], F32, "own_first0", OWN_FIRST_AT), at([P, 2, P], F32, "own_first1", OWN_FIRST_AT - KIB)])
-        turn(unit, 0, 1, 7)
-        part_passes(DST, 1, pairs_d1, at([P, PASSES, 2 * HALF], U8, "picked_d1", OWN_FIRST_AT + 64))
-        msgs[1] = at([P, 2, PACK, P], F32, "msg1", ETA1_AT + 3 * KIB // 2 + 64 - 4 * KIB)
-        message(gate_sums(2, 2, 4), at([P, PACK, P], F32, "eta2", ETA1_AT + 7 * KIB // 2))
+        round_first_pair(1, slice(P, 2 * P), raw_wo1[1], at([P, 2 * P * PACK], BF16, "rounded_wo1_1", LAST_WO_AT)[:, 0 : P * PACK])
+        picked.append(at([P, 2, PASSES, 2 * HALF], U8, "picked1", LAST_WO_AT + 2 * KIB - 64))
+        message(sums[0], tile([P, PACK, P], F32, "eta0", "rounded_wo0"))
+        message(sums[1], tile([P, PACK, P], F32, "eta1", "rounded_wo1_0"))
+        part_passes(picked[1][:], pairs1[:])
+        both = at([P, PASSES, 2, P * PACK], BF16, "rounded_pair1", LAST_WO_AT + 64 - 4 * KIB)
+        nc.scalar.copy(both[:, 0].rearrange("p e (m j) -> p m j e", j=PACK), pair_columns(raw_wo0, 1))
+        for c in range(2):
+            nc.scalar.copy(both[:, 1, :, PAIR * c : PAIR * (c + 1)].rearrange("p e (m j) -> p m j e", j=PACK), pair_columns(raw_wo1[c], 1))
+        nc.vector.quantize_mx(
+            out=wo8[1][0][:].rearrange("p a c -> p (a c)").bitcast(FP8X4),
+            scales=wo8[1][1][:].rearrange("p a c -> p (a c)"),
+            in_=both[:].rearrange("p a e c -> p (a e c)"),
+        )
+        unit = project_pair(0, 6, [tile([P, 2, P], F32, "own_first0"), at([P, 2, P], F32, "own_first1", OWN_FIRST_AT)])
+        turn(unit, 0, 1, 1)
+        message(gate_sums(2, 2, 4))
         message(gate_sums(3, 3, 5))
-        place(0, 0, QUARTER, at([P, QUARTER], F32, "weighted_first", ETA1_AT + 2 * KIB))
-        round_second_pair(at([P, PASSES, 2, P * PACK], BF16, "rounded_pair1", OWN_FIRST_AT + 64 - 5 * KIB))
+        place(0, 0, QUARTER, at([P, QUARTER], F32, "weighted_first", LAST_WO_AT - KIB))
         turn(unit, 1, 2, 0)
         weigh(1, 0, QUARTER)
-        turn(project_pair(1, 1), 0, 2, 2)
+        turn(project_pair(1, 6), 0, 2, 2)
         for i in range(2):
             weigh(i, QUARTER, HALF)
-        late_message(4, 7, 6)
+        message(gate_sums(4, 7, 4), None, at([P, PACK, P], F32, "plain4", OWN_FIRST_AT + 64))
         plane2 = project_plane(2, 0, 3)
-        late_message(5, 0, 4)
-        turn(plane2, 0, 1, 5)
+        late_message(5, 1, 5)
+        turn(plane2, 0, 1, 0)
         weigh(2, 0, HALF)
-        late_message(6, 7, 6)
-        turn(project_pair(2, 3), 0, 2, 2)
-        late_message(7, 0, 4)
-        weigh(0, HALF, 3 * QUARTER)
-        place(1, HALF, 3 * QUARTER)
-        turn(project_pair(3, 3), 0, 2, 5)
+        late_message(6, 7, 4)
+        turn(project_pair(2, 3), 0, 2, 6)
+        late_message(7, 1, 5)
+        for i in range(2):
+            weigh(i, HALF, 3 * QUARTER)
+        turn(project_pair(3, 3), 0, 2, 2)
         for i in range(2):
             place(i, 3 * QUARTER, J)
-        plane2 = project_plane(2, 1, 0)
-        plane3_first = project_plane(3, 0, 4)
-        wide_own = placed.tile([P, T * PACK * 2 // (P * 4), 1, P], F32, name="wide_own", offset=STAGED_AT, align_bytes=64)
+        plane2 = project_plane(2, 1, 1)
+        plane3_first = project_plane(3, 0, 5)
+        wide_own = at([P, T * PACK * 2 // (P * 4), 1, P], F32, "wide_own", STAGED_AT)
         plane3_second = project_plane(3, 1, 3, wide_own)
-        turn(plane2, 0, 1, 1)
+        turn(plane2, 0, 1, 0)
         place(2, HALF, J)
         turn(plane3_first, 0, 1, 7)
-        turn(plane3_second, 0, 1, 6)
+        turn(plane3_second, 0, 1, 4)
 
         staged = [
             placed.tile([P, 2, WIDTHS[c], 2], BF16, name="staged%d" % c, offset=STAGED_AT + PACK * 2 * STARTS[c], align_bytes=64)

@@ -39,8 +39,8 @@ KIB = 1024
 PAIRS0_AT = 8 * KIB
 STAGED_AT = 13 * KIB
 ROUNDED_WA0_AT = 38 * KIB
-LAST_WO_AT = 47 * KIB
-OWN_FIRST_AT = 54 * KIB
+LAST_WO_AT = 51 * KIB
+OWN_FIRST_AT = 58 * KIB
 
 
 def tile_list_rgg_ownreluP_kernel(
@@ -185,7 +185,7 @@ def tile_list_rgg_ownreluP_kernel(
         def bank(shape, name, b):
             return psum.tile(shape, F32, name=name, tag="bank%d" % b)
 
-        msgs = {q: tile([P, 2, PACK, P], F32, "msg%d" % q) for q in range(4)}
+        msgs = {q: tile([P, 2, PACK, P], F32, "msg%d" % q) for q in (0, 2, 3)}
         results = tile([P, PACK, J], F32, "results")
         out_rows = out_0.rearrange("(p i) t -> i p t", i=PACK)
 
@@ -223,6 +223,16 @@ def tile_list_rgg_ownreluP_kernel(
 
         def late_message(group, ms_bank, za_bank):
             message(gate_sums(group, ms_bank, za_bank))
+
+        def last_message(group, ms_bank, za_bank):
+            group, ms, za = gate_sums(group, ms_bank, za_bank)
+            eta = tile([P, PACK, P], F32, "eta%d" % group)
+            plain = ring.tile([P, PACK, P], F32, name="plain")
+            for u in range(2):
+                planes = slice(2 * u, 2 * u + 2)
+                nc.scalar.copy(plain[:, planes], ms[:].rearrange("p (m i) -> p i m", i=PACK)[:, planes])
+                nc.scalar.activation(eta[:, planes], za[:].rearrange("p (m i) -> p i m", i=PACK)[:, planes], ACT.Sigmoid)
+                nc.gpsimd.tensor_tensor(msgs[group // 2][:, group % 2, planes], plain[:, planes], eta[:, planes], ALU.mult)
 
         def project_pair(q, b, parts=None):
             codes, scales = wo8[0]
@@ -284,16 +294,18 @@ def tile_list_rgg_ownreluP_kernel(
         picked.append(at([P, 2, PASSES, 2 * HALF], U8, "picked1", LAST_WO_AT + 2 * KIB - 64))
         message(sums[0], tile([P, PACK, P], F32, "eta0", "rounded_wo0"))
         message(sums[1], tile([P, PACK, P], F32, "eta1", "rounded_wo1_0"))
-        part_passes(picked[1][:], pairs1[:])
         both = at([P, PASSES, 2, P * PACK], BF16, "rounded_pair1", LAST_WO_AT + 64 - 4 * KIB)
-        nc.scalar.copy(both[:, 0].rearrange("p e (m j) -> p m j e", j=PACK), pair_columns(raw_wo0, 1))
+        part_passes(picked[1][:, SRC : SRC + 1], pairs1[:, SRC : SRC + 1, :])
         for c in range(2):
-            nc.scalar.copy(both[:, 1, :, PAIR * c : PAIR * (c + 1)].rearrange("p e (m j) -> p m j e", j=PACK), pair_columns(raw_wo1[c], 1))
+            nc.vector.tensor_copy(both[:, 1, :, PAIR * c : PAIR * (c + 1)].rearrange("p e (m j) -> p m j e", j=PACK), pair_columns(raw_wo1[c], 1))
+        part_passes(picked[1][:, DST : DST + 1], pairs1[:, DST : DST + 1, :])
+        nc.scalar.copy(both[:, 0].rearrange("p e (m j) -> p m j e", j=PACK), pair_columns(raw_wo0, 1))
         nc.vector.quantize_mx(
             out=wo8[1][0][:].rearrange("p a c -> p (a c)").bitcast(FP8X4),
             scales=wo8[1][1][:].rearrange("p a c -> p (a c)"),
             in_=both[:].rearrange("p a e c -> p (a e c)"),
         )
+        msgs[1] = at([P, 2, PACK, P], F32, "msg1", LAST_WO_AT + 128 - 8 * KIB)
         unit = project_pair(0, 6, [tile([P, 2, P], F32, "own_first0"), at([P, 2, P], F32, "own_first1", OWN_FIRST_AT)])
         turn(unit, 0, 1, 1)
         message(gate_sums(2, 2, 4))
@@ -311,12 +323,14 @@ def tile_list_rgg_ownreluP_kernel(
         weigh(2, 0, HALF)
         late_message(6, 7, 4)
         turn(project_pair(2, 3), 0, 2, 6)
-        late_message(7, 1, 5)
+        last_message(7, 1, 5)
         for i in range(2):
             weigh(i, HALF, 3 * QUARTER)
-        turn(project_pair(3, 3), 0, 2, 2)
-        for i in range(2):
-            place(i, 3 * QUARTER, J)
+        unit = project_pair(3, 3)
+        turn(unit, 0, 1, 2)
+        place(0, 3 * QUARTER, J)
+        turn(unit, 1, 2, 6)
+        place(1, 3 * QUARTER, J)
         plane2 = project_plane(2, 1, 1)
         plane3_first = project_plane(3, 0, 5)
         wide_own = at([P, T * PACK * 2 // (P * 4), 1, P], F32, "wide_own", STAGED_AT)

from contextlib import ExitStack

import concourse.mybir as mybir
from concourse.masks import make_identity

K, N, T, J = 1024, 512, 2048, 1024
FLOPS = 4 * 2 * K * N * J

F32 = mybir.dt.float32
BF16 = mybir.dt.bfloat16
I32 = mybir.dt.int32
U32 = mybir.dt.uint32
U16 = mybir.dt.uint16
U8 = mybir.dt.uint8
FP8X4 = mybir.dt.float8_e4m3fn_x4
FP4X4 = mybir.dt.float4_e2m1fn_x4
ACT = mybir.ActivationFunctionType
ALU = mybir.AluOpType

P = 128
PACK = 4
PASSES = K // (P * PACK)
QUADS = 4
PARKED = 24
LIVE = 100
HALF = J // 2
QUARTER = J // 4
PAIR = N // 2
SRC, DST = 0, 1
WB, WC = 0, 1
EARLY_GROUPS = 4

WIDTHS = (256, 512, 512, 512, 256)
STARTS = [sum(WIDTHS[:c]) for c in range(len(WIDTHS))]
CHUNKS = len(WIDTHS)
SCALAR_CHUNK = 3

KIB = 1024
PAIRS0_AT = 8 * KIB
STAGED_AT = 13 * KIB
ROUNDED_WA0_AT = 38 * KIB
LAST_WO_AT = 51 * KIB
OWN_FIRST_AT = 58 * KIB


def tile_list_rgg_ownreluP_kernel(
    tc, tab_words, tab_scales, wa, wb_words, wb_scales, wc_words, wc_scales, wo, wgo, offs, offs2, out_0, out_1, out_2
):
    nc = tc.nc
    with ExitStack() as ctx:
        keep = ctx.enter_context(tc.tile_pool(name="keep", bufs=1))
        ring = ctx.enter_context(tc.tile_pool(name="ring", bufs=2))
        psum = ctx.enter_context(tc.psum_pool(name="psum", bufs=1))
        placed = ctx.enter_context(tc.tile_pool(name="placed", bufs=1))

        def tile(shape, dtype, name, slot=None):
            return keep.tile(shape, dtype, name=name, tag=slot or name, align_bytes=64)

        def at(shape, dtype, name, offset):
            return placed.tile(shape, dtype, name=name, offset=offset, align_bytes=64)

        lists = [keep.tile([P, J // 16], U16, name="src_list"), keep.tile([P, J // 16], U16, name="dst_list")]
        table = tile([P, T], I32, "table")
        table_sc = tile([P, T], U8, "table_sc")
        picked_sc = [tile([P, PASSES, 2 * HALF], U8, "picked_sc%d" % h) for h in range(2)]
        w4 = tile([P, 2 * PASSES, 2 * N], U8, "w4")
        w4_sc = tile([P, 2 * PASSES, N], U8, "w4_sc")
        ident = tile([P, P], F32, "ident")

        pages = {}
        for q in range(QUADS):
            nc.gpsimd.memset(table_sc[32 * q : 32 * q + PARKED, :].bitcast(I32), 0)
        nc.gpsimd.memset(w4_sc[:].bitcast(I32), 0)

        nc.sync.dma_start(lists[SRC][:], offs)
        nc.sync.dma_start(lists[DST][:], offs2)
        for q in range(QUADS):
            nc.sync.dma_start(
                table_sc[32 * q + PARKED : 32 * (q + 1), :].bitcast(I32), tab_scales[:, 4 * q : 4 * q + 4, :].bitcast(I32)
            )
        nc.sync.dma_start(table[:], tab_words[0].rearrange("p t b -> p (t b)").bitcast(I32))

        def load_pass(weight, a, name, first, last):
            raw = tile([P, PACK, last - first], F32, name)
            nc.sync.dma_start(raw[:], weight[512 * a : 512 * (a + 1), first:last].rearrange("(p j) n -> p j n", j=PACK))
            return raw

        def load_words(w, a):
            nc.sync.dma_start(w4[:, PASSES * w + a, :].bitcast(I32), (wb_words, wc_words)[w][a].bitcast(I32))

        load_words(WC, 0)
        for w, scales in enumerate((wb_scales, wc_scales)):
            nc.sync.dma_start(
                w4_sc[0:P:8, PASSES * w : PASSES * (w + 1), :].bitcast(I32), scales.rearrange("a s n -> s a n").bitcast(I32)
            )
        load_words(WC, 1)
        for a in range(PASSES):
            load_words(WB, a)
        raw_wa0 = load_pass(wa, 0, "raw_wa0", 0, N)

        nc.gpsimd.memset(picked_sc[0][96:P].bitcast(I32), 0)
        make_identity(nc, ident[:])
        warm = tile([P, 1], F32, "warm")
        nc.scalar.activation(warm[:], ident[:, 0:1], ACT.Sigmoid)
        pages[0] = tile([P, T], F32, "page0")
        nc.gpsimd.memset(pages[0][:].bitcast(I32), 0)
        nc.gpsimd.memset(picked_sc[1][96:P].bitcast(I32), 0)

        def offsets(l, first, last):
            return lists[l][:, first // 16 : last // 16]

        def pick_scales(h, rows):
            for l in (SRC, DST):
                nc.vector.tensor_copy(rows[:, HALF * l : HALF * (l + 1)], table_sc[:].indirect(offsets(l, HALF * h, HALF * (h + 1))))
            for a in range(PASSES):
                shift = PARKED + 4 * a
                nc.sync.dma_start(picked_sc[h][0:LIVE, a, :].bitcast(I32), rows[shift : shift + LIVE, :].bitcast(I32))

        def pick_words(h, pairs):
            for l in (SRC, DST):
                nc.vector.tensor_copy(pairs[:, l, :], table[:].bitcast(U32).indirect(offsets(l, HALF * h, HALF * (h + 1))))

        def part_passes(parted, pairs):
            nc.vector.tensor_copy(parted.bitcast(U16), pairs.bitcast(U16).rearrange("p l (s a) -> p l a s", a=PASSES))

        pick_scales(0, tile([P, 2 * HALF], U8, "rows0"))
        for r in range(1, 4):
            nc.sync.dma_start(w4_sc[r:P:32].bitcast(I32), w4_sc[8 * r : P : 32].bitcast(I32))
        raw_wa1 = load_pass(wa, 1, "raw_wa1", 0, N)
        pairs0 = at([P, 2, HALF], U32, "pairs0", PAIRS0_AT)
        pick_words(0, pairs0)
        picked = [tile([P, 2, PASSES, 2 * HALF], U8, "picked0")]
        for l in (SRC, DST):
            part_passes(picked[0][:, l : l + 1], pairs0[:, l : l + 1, :])
        raw_wo0 = load_pass(wo, 0, "raw_wo0", 0, N)
        raw_wo1 = [load_pass(wo, 1, "raw_wo1_%d" % c, PAIR * c, PAIR * (c + 1)) for c in range(2)]
        pick_scales(1, at([P, 2 * HALF], U8, "rows1", PAIRS0_AT + 64))
        pages[1] = at([P, T], F32, "page1", PAIRS0_AT + 64 - 8 * KIB)
        nc.gpsimd.memset(pages[1][:].bitcast(I32), 0)
        pages[3] = pages[0]

        def mx_tiles(name, width):
            return tile([P, PASSES, width], U32, name + "_codes"), tile([P, PASSES, width], U8, name + "_scales")

        def quantize(operand, a, cols, rounded):
            codes, scales = operand
            nc.vector.quantize_mx(out=codes[:, a, cols].bitcast(FP8X4), scales=scales[:, a, cols], in_=rounded)

        wa8 = mx_tiles("wa8", N)

        def round_wa(a, raw, rounded):
            nc.scalar.copy(rounded[:].rearrange("p (c i j) -> p c j i", i=4, j=PACK), raw[:].rearrange("p j (c i) -> p c j i", i=4))
            quantize(wa8, a, slice(0, N), rounded[:])

        round_wa(0, raw_wa0, at([P, N * PACK], BF16, "rounded_wa0", ROUNDED_WA0_AT))
        pairs1 = at([P, 2, HALF], U32, "pairs1", ROUNDED_WA0_AT + 64)
        pick_words(1, pairs1)
        pages[2] = at([P, T], F32, "page2", ROUNDED_WA0_AT + 64 - 8 * KIB)
        nc.gpsimd.memset(pages[2][:].bitcast(I32), 0)
        round_wa(1, raw_wa1, tile([P, N * PACK], BF16, "rounded_wa1"))
        gate = tile([P, J], F32, "gate", "rounded_wa1")
        nc.sync.dma_start(gate[:], wgo)

        def pair_columns(raw, u):
            return raw[:].rearrange("p j (m u e) -> p u m j e", u=2, e=2)[:, u]

        wo8 = [mx_tiles("wo8_pair%d" % u, PAIR) for u in range(2)]

        def round_first_pair(a, cols, raw, rounded):
            nc.scalar.copy(rounded[:].rearrange("p (m e j) -> p m j e", e=2, j=PACK), pair_columns(raw, 0))
            quantize(wo8[0], a, cols, rounded[:])

        def mm(out, l, group, a, rhs, rhs_scale, start, stop):
            h, b = divmod(group, HALF // P)
            nc.tensor.matmul_mx(
                out=out,
                lhsT=picked[h][:, l, a, 2 * P * b : 2 * P * (b + 1)].bitcast(FP4X4),
                lhsT_scale=picked_sc[h][:, a, HALF * l + P * b : HALF * l + P * (b + 1)],
                rhs=rhs,
                rhs_scale=rhs_scale,
                start=start,
                stop=stop,
            )

        def bank(shape, name, b):
            return psum.tile(shape, F32, name=name, tag="bank%d" % b)

        msgs = {q: tile([P, 2, PACK, P], F32, "msg%d" % q) for q in (0, 2, 3)}
        results = tile([P, PACK, J], F32, "results")
        out_rows = out_0.rearrange("(p i) t -> i p t", i=PACK)

        def source_passes(group, ms_bank, za_bank):
            ms, za = bank([P, N], "ms", ms_bank), bank([P, N], "za", za_bank)
            for out, w in ((ms, WC), (za, WB)):
                for a in range(PASSES):
                    v = PASSES * w + a
                    mm(out[:], SRC, group, a, w4[:, v, :].bitcast(FP4X4), w4_sc[:, v, :], a == 0, w == WC and a == PASSES - 1)
            return group, ms, za

        def target_pass(sums, a):
            group, ms, za = sums
            mm(za[:], DST, group, a, wa8[0][:, a, :].bitcast(FP8X4), wa8[1][:, a, :], False, a == PASSES - 1)

        def message(sums, eta=None, plain=None):
            group, ms, za = sums
            if eta is None:
                eta = tile([P, PACK, P], F32, "eta%d" % group)
            nc.scalar.activation(eta[:], za[:].rearrange("p (m i) -> p i m", i=PACK), ACT.Sigmoid)
            by_plane = ms[:].rearrange("p (m i) -> p i m", i=PACK)
            if group < EARLY_GROUPS:
                nc.vector.tensor_tensor(msgs[group // 2][:, group % 2], by_plane, eta[:], ALU.mult)
            else:
                if plain is None:
                    plain = ring.tile([P, PACK, P], F32, name="plain")
                nc.scalar.copy(plain[:], by_plane)
                nc.gpsimd.tensor_tensor(msgs[group // 2][:, group % 2], plain[:], eta[:], ALU.mult)

        def gate_sums(group, ms_bank, za_bank):
            sums = source_passes(group, ms_bank, za_bank)
            for a in range(PASSES):
                target_pass(sums, a)
            return sums

        def late_message(group, ms_bank, za_bank):
            message(gate_sums(group, ms_bank, za_bank))

        def last_message(group, ms_bank, za_bank):
            group, ms, za = gate_sums(group, ms_bank, za_bank)
            eta = tile([P, PACK, P], F32, "eta%d" % group)
            plain = ring.tile([P, PACK, P], F32, name="plain")
            for u in range(2):
                planes = slice(2 * u, 2 * u + 2)
                nc.scalar.copy(plain[:, planes], ms[:].rearrange("p (m i) -> p i m", i=PACK)[:, planes])
                nc.scalar.activation(eta[:, planes], za[:].rearrange("p (m i) -> p i m", i=PACK)[:, planes], ACT.Sigmoid)
                nc.gpsimd.tensor_tensor(msgs[group // 2][:, group % 2, planes], plain[:, planes], eta[:, planes], ALU.mult)

        def project_pair(q, b, parts=None):
            codes, scales = wo8[0]
            ow = bank([P, 2, PAIR], "ow", b)
            for a in range(PASSES):
                for g in range(2):
                    mm(ow[:, g, :], DST, 2 * q + g, a, codes[:, a, :].bitcast(FP8X4), scales[:, a, :], a == 0 and g == 0, a == PASSES - 1 and g == 1)
            by_plane = ow[:].rearrange("p g (m e) -> p g e m", e=2)
            if parts is None:
                own = ring.tile([P, 2, 2, P], F32, name="own", bufs=3)
                nc.scalar.copy(own[:], by_plane)
                return 0, 2 * q, 2, [own[:, :, e] for e in range(2)]
            for e in range(2):
                nc.scalar.copy(parts[e][:], by_plane[:, :, e])
            return 0, 2 * q, 2, parts

        def project_plane(i, h, b, own=None):
            codes, scales = wo8[1]
            ow = bank([P, 4, P], "ow", b)
            if own is None:
                own = ring.tile([P, 4, 1, P], F32, name="own", bufs=3)
            cols = slice(P * (i % 2), P * (i % 2 + 1))
            for a in range(PASSES):
                for g in range(4):
                    mm(ow[:, g, :], DST, 4 * h + g, a, codes[:, a, cols].bitcast(FP8X4), scales[:, a, cols], a == 0 and g == 0, a == PASSES - 1 and g == 3)
            nc.scalar.copy(own[:, 0:4, 0], ow[:])
            return i, 4 * h, 4, [own[:, :, 0]]

        def turn(unit, first, last, b):
            plane0, group0, groups, own = unit
            total = bank([P, PACK // groups, groups * P], "total", b)
            for e in range(first, last):
                for g in range(groups):
                    group = group0 + g
                    for s, summand in enumerate((own[e][:, g], msgs[group // 2][:, group % 2, plane0 + e])):
                        nc.tensor.matmul(
                            total[:, e, P * g : P * (g + 1)], summand, ident[:], start=s == 0, stop=s == 1, is_transpose=True
                        )
            edges = slice(P * group0, P * (group0 + groups))
            nc.scalar.activation(results[:, plane0 + first : plane0 + last, edges], total[:, first:last, :], ACT.Relu)

        def place(i, first, last, weighted=None):
            window = pages[i][:].indirect(offsets(DST, first, last))
            if weighted is None:
                nc.vector.tensor_tensor(window, results[:, i, first:last], gate[:, first:last], ALU.mult)
            else:
                nc.gpsimd.tensor_tensor(weighted[:], results[:, i, first:last], gate[:, first:last], ALU.mult)
                nc.vector.tensor_copy(window, weighted[:])
            if last == J:
                nc.sync.dma_start(out_rows[i], pages[i][:])

        def weigh(i, first, last):
            place(i, first, last, tile([P, last - first], F32, "weighted%d_%d" % (i, first)))

        sums = [gate_sums(g, g, 4 + g) for g in range(2)]
        round_first_pair(0, slice(0, PAIR), raw_wo0, tile([P, PAIR * PACK], BF16, "rounded_wo0"))
        round_first_pair(1, slice(0, P), raw_wo1[0], tile([P, P * PACK], BF16, "rounded_wo1_0"))
        round_first_pair(1, slice(P, 2 * P), raw_wo1[1], at([P, 2 * P * PACK], BF16, "rounded_wo1_1", LAST_WO_AT)[:, 0 : P * PACK])
        picked.append(at([P, 2, PASSES, 2 * HALF], U8, "picked1", LAST_WO_AT + 2 * KIB - 64))
        message(sums[0], tile([P, PACK, P], F32, "eta0", "rounded_wo0"))
        message(sums[1], tile([P, PACK, P], F32, "eta1", "rounded_wo1_0"))
        both = at([P, PASSES, 2, P * PACK], BF16, "rounded_pair1", LAST_WO_AT + 64 - 4 * KIB)
        part_passes(picked[1][:, SRC : SRC + 1], pairs1[:, SRC : SRC + 1, :])
        for c in range(2):
            nc.vector.tensor_copy(both[:, 1, :, PAIR * c : PAIR * (c + 1)].rearrange("p e (m j) -> p m j e", j=PACK), pair_columns(raw_wo1[c], 1))
        part_passes(picked[1][:, DST : DST + 1], pairs1[:, DST : DST + 1, :])
        nc.scalar.copy(both[:, 0].rearrange("p e (m j) -> p m j e", j=PACK), pair_columns(raw_wo0, 1))
        nc.vector.quantize_mx(
            out=wo8[1][0][:].rearrange("p a c -> p (a c)").bitcast(FP8X4),
            scales=wo8[1][1][:].rearrange("p a c -> p (a c)"),
            in_=both[:].rearrange("p a e c -> p (a e c)"),
        )
        msgs[1] = at([P, 2, PACK, P], F32, "msg1", LAST_WO_AT + 128 - 8 * KIB)
        unit = project_pair(0, 6, [tile([P, 2, P], F32, "own_first0"), at([P, 2, P], F32, "own_first1", OWN_FIRST_AT)])
        turn(unit, 0, 1, 1)
        message(gate_sums(2, 2, 4))
        message(gate_sums(3, 3, 5))
        place(0, 0, QUARTER, at([P, QUARTER], F32, "weighted_first", LAST_WO_AT - KIB))
        turn(unit, 1, 2, 0)
        weigh(1, 0, QUARTER)
        turn(project_pair(1, 6), 0, 2, 2)
        for i in range(2):
            weigh(i, QUARTER, HALF)
        message(gate_sums(4, 7, 4), None, at([P, PACK, P], F32, "plain4", OWN_FIRST_AT + 64))
        plane2 = project_plane(2, 0, 3)
        late_message(5, 1, 5)
        turn(plane2, 0, 1, 0)
        weigh(2, 0, HALF)
        late_message(6, 7, 4)
        turn(project_pair(2, 3), 0, 2, 6)
        last_message(7, 1, 5)
        for i in range(2):
            weigh(i, HALF, 3 * QUARTER)
        unit = project_pair(3, 3)
        turn(unit, 0, 1, 2)
        place(0, 3 * QUARTER, J)
        turn(unit, 1, 2, 6)
        place(1, 3 * QUARTER, J)
        plane2 = project_plane(2, 1, 1)
        plane3_first = project_plane(3, 0, 5)
        wide_own = at([P, T * PACK * 2 // (P * 4), 1, P], F32, "wide_own", STAGED_AT)
        plane3_second = project_plane(3, 1, 3, wide_own)
        turn(plane2, 0, 1, 0)
        place(2, HALF, J)
        turn(plane3_first, 0, 1, 7)
        turn(plane3_second, 0, 1, 4)

        staged = [
            placed.tile([P, 2, WIDTHS[c], 2], BF16, name="staged%d" % c, offset=STAGED_AT + PACK * 2 * STARTS[c], align_bytes=64)
            for c in range(CHUNKS)
        ]

        def round_plane(i):
            u, e = divmod(i, 2)
            for c in range(CHUNKS):
                cols = slice(STARTS[c], STARTS[c] + WIDTHS[c])
                if u == 1 and c == 0:
                    nc.vector.tensor_copy(staged[c][:, u, :, e], pages[i][:, cols])
                else:
                    nc.scalar.copy(staged[c][:, u, :, e], pages[i][:, cols])

        round_plane(0)
        place(3, 0, J)
        for i in range(1, PACK):
            round_plane(i)

        y_sc = tile([P, T], U8, "y_sc")
        words_out = out_1[0].rearrange("p t b -> p (t b)").bitcast(I32)
        woven = [tile([P, WIDTHS[c] * PACK], BF16, "woven%d" % c) for c in range(CHUNKS)]
        y_codes = [tile([P, WIDTHS[c]], I32, "y_codes%d" % c) for c in range(CHUNKS)]

        def weave(c):
            dst = woven[c][:].bitcast(U32).rearrange("p (g s u) -> p g u s", s=4, u=2)
            src = staged[c][:].rearrange("p u t e -> p u (t e)").bitcast(U32).rearrange("p u (g s) -> p g u s", s=4)
            if c == SCALAR_CHUNK:
                nc.scalar.copy(dst, src)
            else:
                nc.vector.tensor_copy(dst.bitcast(I32), src.bitcast(I32))

        def quantize_chunk(c):
            cols = slice(STARTS[c], STARTS[c] + WIDTHS[c])
            nc.vector.quantize_mx(out=y_codes[c][:].bitcast(FP8X4), scales=y_sc[:, cols], in_=woven[c][:])
            nc.sync.dma_start(words_out[:, cols], y_codes[c][:])

        weave(0)
        for c in range(CHUNKS):
            if c + 1 < CHUNKS:
                weave(c + 1)
            quantize_chunk(c)
        for q in range(QUADS):
            queue = (nc.scalar, nc.sync)[q % 2]
            queue.dma_start(out_2[0, 4 * q : 4 * q + 4, :].bitcast(I32), y_sc[32 * q : 32 * q + 4, :].bitcast(I32))
